import numpy as np
import ml_dtypes


def mxq(x, axis, fmt="e4m3"):
    dtype, down = {"e4m3": (ml_dtypes.float8_e4m3fn, 7), "e5m2": (ml_dtypes.float8_e5m2, 14)}[fmt]
    v = np.moveaxis(np.asarray(x, np.float32).astype(ml_dtypes.bfloat16).astype(np.float64), axis, -1)
    blocks = v.reshape(v.shape[:-1] + (-1, 32))
    amax = np.abs(blocks).max(-1, keepdims=True)
    byte = np.maximum(np.where(amax > 0, np.frexp(amax)[1] - 1 + 127, 0) - down, 1)
    scale = np.exp2(byte - 127.0)
    codes = (blocks / scale).astype(np.float32).astype(dtype).astype(np.float64)
    return np.moveaxis((codes * scale).reshape(v.shape), -1, axis)


WIDE = False


def mx_kscale(k):
    if not WIDE:
        return np.ones(k)
    levels = np.array([10, -10, 5, -5, 0])
    if k % 512:
        return np.exp2(np.random.permutation(np.resize(levels, k // 32))).repeat(32)
    a = np.empty((k // 512, 16))
    for p in range(k // 512):
        a[p, :8] = np.random.permutation(np.resize(levels, 8))
        for g in range(8):
            far = levels[np.abs(levels - a[p, g]) >= 10]
            a[p, g + 8] = far[np.random.randint(len(far))]
    return np.exp2(a.ravel()).repeat(32)


def f64(x):
    return np.asarray(x).astype(np.float64)


def striped(idx):
    return np.tile(idx.reshape(-1, 16).T, (8, 1)).astype(np.uint16)


def unstriped(offs):
    return offs[:16].T.reshape(-1).astype(np.int64)


E2M1 = np.array([0.0, 0.5, 1.0, 1.5, 2.0, 3.0, 4.0, 6.0, -0.0, -0.5, -1.0, -1.5, -2.0, -3.0, -4.0, -6.0])


def pack_weight(w, fmt):
    k, n = w.shape
    w = f64(np.asarray(w, np.float32).astype(ml_dtypes.bfloat16)).reshape(k // 32, 32, n)
    amax = np.abs(w).max(1)
    if fmt == "e4m3":
        byte = np.frexp(amax)[1] - 1 + 127 - 7
    else:
        mant, ex = np.frexp(amax / 6.0)
        byte = np.where(mant > 0.5, ex, ex - 1) + 127
    byte = np.clip(np.where(amax > 0, byte, 1), 1, 254)
    scaled = (w * np.exp2(127.0 - byte)[:, None, :]).reshape(k, n).astype(np.float32)
    by_word = np.ascontiguousarray(scaled.reshape(k // 512, 128, 4, n).transpose(0, 1, 3, 2))
    if fmt == "e4m3":
        words = by_word.astype(ml_dtypes.float8_e4m3fn).view(np.uint8)
    else:
        c = by_word.astype(ml_dtypes.float4_e2m1fn).view(np.uint8) & 0xF
        words = (c[..., 0::2] | (c[..., 1::2] << 4)).reshape(k // 512, 128, 2 * n)
    return np.ascontiguousarray(words), np.ascontiguousarray(byte.astype(np.uint8).reshape(k // 512, 16, n))


def unpack_weight(words, scales, fmt):
    g, _, n = scales.shape
    words = np.ascontiguousarray(words).reshape(g, 128, n, -1)
    if fmt == "e4m3":
        vals = words.view(ml_dtypes.float8_e4m3fn).astype(np.float64)
    else:
        nib = np.empty((g, 128, n, 4), np.uint8)
        nib[..., 0::2] = words & 0xF
        nib[..., 1::2] = words >> 4
        vals = E2M1[nib]
    vals = vals * np.repeat(np.exp2(scales.astype(np.float64) - 127.0), 8, axis=1)[..., None]
    return vals.transpose(0, 1, 3, 2).reshape(g * 512, n)


def gelu(v):
    return 0.5 * v * (1.0 + np.tanh(np.sqrt(2.0 / np.pi) * (v + 0.044715 * v**3)))


K, H, T, S, T2, S2 = 1536, 512, 2048, 512, 4096, 1536

def setup_inputs():
    n = np.random.standard_normal
    s = mx_kscale(K)[:, None]
    u = mx_kscale(H)[:, None]
    tab_words, tab_scales = pack_weight(n((K, T)) * s, "e4m3")
    tab2_words, tab2_scales = pack_weight(n((H, T2)) / np.sqrt(H) / u, "e4m3")
    wg_words, wg_scales = pack_weight(2.0 * n((K, H)) / np.sqrt(K) / s, "e2m1")
    wq = 3.0 * n((K, H)) / np.sqrt(K) / s * u.T
    return {
        "tab_words": tab_words, "tab_scales": tab_scales,
        "offs": striped(np.random.permutation(T)[:S]),
        "tab2_words": tab2_words, "tab2_scales": tab2_scales,
        "offs2": striped(np.random.permutation(T2)[:S2]),
        "wq": wq.astype(np.float32),
        "wg_words": wg_words, "wg_scales": wg_scales,
    }

def reference(tab_words, tab_scales, offs, tab2_words, tab2_scales, offs2, wq, wg_words, wg_scales):
    cap = 2.0
    v = unpack_weight(tab_words, tab_scales, "e4m3")[:, unstriped(offs)]
    v2 = unpack_weight(tab2_words, tab2_scales, "e4m3")[:, unstriped(offs2)]
    wg = unpack_weight(wg_words, wg_scales, "e2m1")
    a = mxq(f64(wq), 0, "e4m3").T @ v
    b = wg.T @ v
    h = a * (1.0 / (1.0 + np.exp(-b)))
    z = v2.T @ mxq(h, 0, "e4m3")
    return cap * np.tanh(z / cap)

@@ -1,0 +1,209 @@
+from contextlib import ExitStack
+
+import concourse.mybir as mybir
+from concourse.masks import make_identity
+
+K, H, T, S, T2, S2 = 1536, 512, 2048, 512, 4096, 1536
+CAP = 2.0
+FLOPS = 2 * 2 * K * H * S + 2 * H * S2 * S
+
+F32 = mybir.dt.float32
+BF16 = mybir.dt.bfloat16
+I32 = mybir.dt.int32
+U32 = mybir.dt.uint32
+U16 = mybir.dt.uint16
+U8 = mybir.dt.uint8
+FP8X4 = mybir.dt.float8_e4m3fn_x4
+FP4X4 = mybir.dt.float4_e2m1fn_x4
+SIGMOID = mybir.ActivationFunctionType.Sigmoid
+MULT = mybir.AluOpType.mult
+ADD = mybir.AluOpType.add
+
+P = 128
+PACK = 4
+PASSES = K // (P * PACK)
+QCHUNKS = S // P
+KEY_TILES = S2 // P
+KEY_PIECE = 512
+KEY_PIECES = S2 // KEY_PIECE
+KEY_PLANE_ROW = 4
+SCALAR_COLS = (512, 256, 160)
+
+
+def tile_list_paged_softcap_logits_kernel(
+    tc, tab_words, tab_scales, offs, tab2_words, tab2_scales, offs2, wq, wg_words, wg_scales, out
+):
+    nc = tc.nc
+    with ExitStack() as ctx:
+        keep = ctx.enter_context(tc.tile_pool(name="keep", bufs=1))
+        ring = ctx.enter_context(tc.tile_pool(name="ring", bufs=4))
+        psum = ctx.enter_context(tc.psum_pool(name="psum", bufs=8))
+
+        lst = keep.tile([P, S // 16], U16, name="lst")
+        lst2 = keep.tile([P, S2 // 16], U16, name="lst2")
+        tw_first = keep.tile([P, T], I32, name="tw_first", align_bytes=64)
+        tw_rest = keep.tile([P, PASSES - 1, T], I32, name="tw_rest", align_bytes=64)
+        tw = [tw_first[:]] + [tw_rest[:, a, :] for a in range(PASSES - 1)]
+        ts = keep.tile([P, PASSES * T], U8, name="ts", align_bytes=64)
+        t2w = keep.tile([P, T2], I32, name="t2w", align_bytes=64)
+        t2s = keep.tile([P, T2], U8, name="t2s", align_bytes=64)
+        wgw = keep.tile([P, PASSES, 2 * H], U8, name="wgw", align_bytes=64)
+        wgs = keep.tile([P, PASSES * H], U8, name="wgs", align_bytes=64)
+        raw = [keep.tile([P, PACK, H], F32, name="raw%d" % a, align_bytes=64) for a in range(PASSES)]
+        ident = keep.tile([P, P], F32, name="ident", align_bytes=64)
+        warm_in = keep.tile([P, 1], F32, name="warm_in")
+        warm_out = keep.tile([P, 1], F32, name="warm_out")
+
+        nc.vector.memset(warm_in[:], 0.0)
+        nc.scalar.activation(warm_out[:], warm_in[:], SIGMOID)
+        nc.vector.memset(ts[:].bitcast(I32), 0)
+        nc.vector.memset(wgs[:].bitcast(I32), 0)
+        nc.vector.memset(t2s[:].bitcast(I32), 0)
+
+        def load_wq(a):
+            rows = wq[a * P * PACK : (a + 1) * P * PACK, :]
+            nc.sync.dma_start(out=raw[a][:], in_=rows.rearrange("(p j) c -> p j c", j=PACK))
+
+        def load_scale_rows(queue, plane, scales, first_row):
+            passes = scales.shape[0]
+            by_row = scales.rearrange("a (q r) t -> r q a t", r=4)
+            dst = plane[:].bitcast(I32).rearrange("p (a t) -> p a t", a=passes)
+            for r in range(4):
+                queue.dma_start(out=dst[first_row + r : P : 32], in_=by_row[r].bitcast(I32))
+
+        nc.sync.dma_start(lst[:], offs)
+        nc.sync.dma_start(out=tw_first[:], in_=tab_words[0].rearrange("p t i -> p (t i)").bitcast(I32))
+        nc.sync.dma_start(out=wgw[:].bitcast(I32), in_=wg_words.rearrange("a p c -> p a c").bitcast(I32))
+        nc.sync.dma_start(lst2[:], offs2)
+        load_wq(0)
+        nc.sync.dma_start(out=tw_rest[:], in_=tab_words[1:PASSES].rearrange("a p t i -> p a (t i)").bitcast(I32))
+        load_wq(1)
+        load_wq(2)
+        nc.sync.dma_start(out=t2w[:], in_=tab2_words[0].rearrange("p t i -> p (t i)").bitcast(I32))
+        load_scale_rows(nc.gpsimd, ts, tab_scales, 0)
+        load_scale_rows(nc.gpsimd, t2s, tab2_scales, KEY_PLANE_ROW)
+        load_scale_rows(nc.scalar, wgs, wg_scales, 0)
+        make_identity(nc, ident[:])
+
+        vw = [keep.tile([P, S], U32, name="vw%d" % a, tag="words%d" % a, align_bytes=64) for a in range(PASSES)]
+        vs = [keep.tile([P, S], U8, name="vs%d" % a, align_bytes=64) for a in range(PASSES)]
+        ks = [keep.tile([P, KEY_PIECE], U8, name="ks%d" % g, align_bytes=64) for g in range(KEY_PIECES)]
+        wb = [keep.tile([P, H, PACK], BF16, name="wb%d" % a, align_bytes=64) for a in range(PASSES)]
+        wc = [keep.tile([P, H], U32, name="wc%d" % a, align_bytes=64) for a in range(PASSES)]
+        ws = [keep.tile([P, H], U8, name="ws%d" % a, align_bytes=64) for a in range(PASSES)]
+        gate = [keep.tile([P, H], F32, name="gate%d" % c, align_bytes=64) for c in range(QCHUNKS)]
+        hc = keep.tile([P, S], U32, name="hc", align_bytes=64)
+        hs = keep.tile([P, S], U8, name="hs", align_bytes=64)
+
+        def piece(g):
+            cols = KEY_PIECE // 16
+            return lst2[:, g * cols : (g + 1) * cols]
+
+        def gather_words(a):
+            nc.vector.tensor_copy(vw[a][:], tw[a].bitcast(U32).indirect(lst[:]))
+
+        def gather_scales(a):
+            nc.vector.tensor_copy(vs[a][:], ts[:, a * T : (a + 1) * T].indirect(lst[:]))
+
+        def gather_key_scales(g):
+            nc.vector.tensor_copy(ks[g][:], t2s[:].indirect(piece(g)))
+
+        def gather_key_words(g):
+            nc.vector.tensor_copy(kw[:, g * KEY_PIECE : (g + 1) * KEY_PIECE], t2w[:].bitcast(U32).indirect(piece(g)))
+
+        def round_wq(a):
+            split = SCALAR_COLS[a]
+            src = raw[a][:].rearrange("p t (c i) -> p c t i", i=4)
+            dst = wb[a][:].rearrange("p (c i) t -> p c t i", i=4)
+            nc.scalar.copy(dst[:, : split // 4], src[:, : split // 4])
+            if split < H:
+                nc.vector.tensor_copy(dst[:, split // 4 :], src[:, split // 4 :])
+
+        def quantize_wq(a):
+            nc.vector.quantize_mx(
+                out=wc[a][:].bitcast(FP8X4), scales=ws[a][:], in_=wb[a][:].rearrange("p c t -> p (c t)")
+            )
+
+        b_ps = [psum.tile([P, H], F32, tag="bank", name="b_ps%d" % c) for c in range(QCHUNKS)]
+        a_ps = [psum.tile([P, H], F32, tag="bank", name="a_ps%d" % c) for c in range(QCHUNKS)]
+
+        def project(acc, a, rhs, rhs_scale):
+            for c in range(QCHUNKS):
+                cols = slice(c * P, (c + 1) * P)
+                nc.tensor.matmul_mx(
+                    out=acc[c][:],
+                    lhsT=vw[a][:, cols].bitcast(FP8X4),
+                    lhsT_scale=vs[a][:, cols],
+                    rhs=rhs,
+                    rhs_scale=rhs_scale,
+                    start=(a == 0),
+                    stop=(a == PASSES - 1),
+                )
+
+        def gate_pass(a):
+            project(b_ps, a, wgw[:, a, :].bitcast(FP4X4), wgs[:, a * H : (a + 1) * H])
+
+        def query_pass(a):
+            project(a_ps, a, wc[a][:].bitcast(FP8X4), ws[a][:])
+
+        gather_words(0)
+        for a in range(PASSES):
+            gather_scales(a)
+        round_wq(0)
+        gather_words(1)
+        quantize_wq(0)
+        gate_pass(0)
+        query_pass(0)
+        gate_pass(1)
+        gather_words(2)
+        gate_pass(2)
+        for c in range(QCHUNKS):
+            nc.scalar.activation(gate[c][:], b_ps[c][:], SIGMOID)
+        round_wq(1)
+        gather_key_scales(0)
+        quantize_wq(1)
+        query_pass(1)
+        round_wq(2)
+        quantize_wq(2)
+        query_pass(2)
+        kw = keep.tile([P, S2], U32, name="kw", tag="words%d" % (PASSES - 1), align_bytes=64)
+
+        grouped = []
+        for c in range(QCHUNKS):
+            ht = ring.tile([P, H], BF16, name="ht", align_bytes=64)
+            nc.vector.tensor_tensor(ht[:], a_ps[c][:], gate[c][:], MULT)
+            words = ht[:].bitcast(F32)
+            xt = psum.tile([P, 2, P], F32, tag="bank", name="xt%d" % c)
+            for u in range(2):
+                nc.tensor.transpose(xt[:, u, :], words[:, u : H // 2 : 2], ident[:])
+            hg = ring.tile([P, P, PACK], BF16, name="hg", align_bytes=64)
+            nc.scalar.copy(hg[:].bitcast(F32), xt[:].rearrange("p u j -> p j u"))
+            grouped.append(hg)
+        for c in range(QCHUNKS):
+            cols = slice(c * P, (c + 1) * P)
+            nc.vector.quantize_mx(
+                out=hc[:, cols].bitcast(FP8X4), scales=hs[:, cols], in_=grouped[c][:].rearrange("p j t -> p (j t)")
+            )
+
+        tiles_per_piece = KEY_PIECE // P
+        gather_key_words(0)
+        for i in range(KEY_TILES):
+            g, cols = i // tiles_per_piece, slice((i % tiles_per_piece) * P, (i % tiles_per_piece + 1) * P)
+            if i % tiles_per_piece == 0 and g + 1 < KEY_PIECES:
+                gather_key_scales(g + 1)
+                gather_key_words(g + 1)
+            z = psum.tile([P, S], F32, tag="bank", name="z%d" % i)
+            nc.tensor.matmul_mx(
+                out=z[:],
+                lhsT=kw[:, i * P : (i + 1) * P].bitcast(FP8X4),
+                lhsT_scale=ks[g][KEY_PLANE_ROW:P, cols],
+                rhs=hc[:].bitcast(FP8X4),
+                rhs_scale=hs[:],
+                start=True,
+                stop=True,
+            )
+            sig = ring.tile([P, S], F32, name="sig")
+            nc.scalar.activation(sig[:], z[:], SIGMOID, scale=2.0 / CAP)
+            res = keep.tile([P, S], F32, name="res%d" % i)
+            nc.vector.tensor_scalar(res[:], sig[:], 2.0 * CAP, -CAP, MULT, ADD)
+            nc.sync.dma_start(out=out[i * P : (i + 1) * P, :], in_=res[:])

@@ -27,7 +27,7 @@ KEY_TILES = S2 // P
 KEY_PIECE = 512
 KEY_PIECES = S2 // KEY_PIECE
 KEY_PLANE_ROW = 4
-SCALAR_COLS = (512, 256, 160)
+SCALAR_COLS = (512, 512, 160)
 
 
 def tile_list_paged_softcap_logits_kernel(
@@ -41,26 +41,27 @@ def tile_list_paged_softcap_logits_kernel(
 
         lst = keep.tile([P, S // 16], U16, name="lst")
         lst2 = keep.tile([P, S2 // 16], U16, name="lst2")
-        tw_first = keep.tile([P, T], I32, name="tw_first", align_bytes=64)
-        tw_rest = keep.tile([P, PASSES - 1, T], I32, name="tw_rest", align_bytes=64)
-        tw = [tw_first[:]] + [tw_rest[:, a, :] for a in range(PASSES - 1)]
-        ts = keep.tile([P, PASSES * T], U8, name="ts", align_bytes=64)
-        t2w = keep.tile([P, T2], I32, name="t2w", align_bytes=64)
+        ts = keep.tile([P, PASSES * T], U8, name="ts", tag="slot_c", align_bytes=64)
         t2s = keep.tile([P, T2], U8, name="t2s", align_bytes=64)
         wgw = keep.tile([P, PASSES, 2 * H], U8, name="wgw", align_bytes=64)
         wgs = keep.tile([P, PASSES * H], U8, name="wgs", align_bytes=64)
-        raw = [keep.tile([P, PACK, H], F32, name="raw%d" % a, align_bytes=64) for a in range(PASSES)]
+        tw, raw = {}, {}
         ident = keep.tile([P, P], F32, name="ident", align_bytes=64)
-        warm_in = keep.tile([P, 1], F32, name="warm_in")
-        warm_out = keep.tile([P, 1], F32, name="warm_out")
+        warm_in = keep.tile([P, 1], F32, name="warm_in", tag="slot_d", align_bytes=64)
+        warm_out = keep.tile([P, 1], F32, name="warm_out", tag="slot_e", align_bytes=64)
 
         nc.vector.memset(warm_in[:], 0.0)
         nc.scalar.activation(warm_out[:], warm_in[:], SIGMOID)
         nc.vector.memset(ts[:].bitcast(I32), 0)
-        nc.vector.memset(wgs[:].bitcast(I32), 0)
         nc.vector.memset(t2s[:].bitcast(I32), 0)
+        nc.vector.memset(wgs[:].bitcast(I32), 0)
 
-        def load_wq(a):
+        def load_table_words(a, slot):
+            tw[a] = keep.tile([P, T], I32, name="tw%d" % a, tag=slot, align_bytes=64)
+            nc.sync.dma_start(out=tw[a][:], in_=tab_words[a].rearrange("p t i -> p (t i)").bitcast(I32))
+
+        def load_wq(a, slot):
+            raw[a] = keep.tile([P, PACK, H], F32, name="raw%d" % a, tag=slot, align_bytes=64)
             rows = wq[a * P * PACK : (a + 1) * P * PACK, :]
             nc.sync.dma_start(out=raw[a][:], in_=rows.rearrange("(p j) c -> p j c", j=PACK))
 
@@ -72,17 +73,14 @@ def tile_list_paged_softcap_logits_kernel(
                 queue.dma_start(out=dst[first_row + r : P : 32], in_=by_row[r].bitcast(I32))
 
         nc.sync.dma_start(lst[:], offs)
-        nc.sync.dma_start(out=tw_first[:], in_=tab_words[0].rearrange("p t i -> p (t i)").bitcast(I32))
-        nc.sync.dma_start(out=wgw[:].bitcast(I32), in_=wg_words.rearrange("a p c -> p a c").bitcast(I32))
         nc.sync.dma_start(lst2[:], offs2)
-        load_wq(0)
-        nc.sync.dma_start(out=tw_rest[:], in_=tab_words[1:PASSES].rearrange("a p t i -> p a (t i)").bitcast(I32))
-        load_wq(1)
-        load_wq(2)
-        nc.sync.dma_start(out=t2w[:], in_=tab2_words[0].rearrange("p t i -> p (t i)").bitcast(I32))
-        load_scale_rows(nc.gpsimd, ts, tab_scales, 0)
+        load_table_words(0, "slot_a")
+        load_scale_rows(nc.sync, ts, tab_scales, 0)
+        load_wq(0, "slot_d")
+        load_wq(1, "slot_e")
+        nc.gpsimd.dma_start(out=wgw[:].bitcast(I32), in_=wg_words.rearrange("a p c -> p a c").bitcast(I32))
         load_scale_rows(nc.gpsimd, t2s, tab2_scales, KEY_PLANE_ROW)
-        load_scale_rows(nc.scalar, wgs, wg_scales, 0)
+        load_scale_rows(nc.gpsimd, wgs, wg_scales, 0)
         make_identity(nc, ident[:])
 
         vw = [keep.tile([P, S], U32, name="vw%d" % a, tag="words%d" % a, align_bytes=64) for a in range(PASSES)]
@@ -100,7 +98,7 @@ def tile_list_paged_softcap_logits_kernel(
             return lst2[:, g * cols : (g + 1) * cols]
 
         def gather_words(a):
-            nc.vector.tensor_copy(vw[a][:], tw[a].bitcast(U32).indirect(lst[:]))
+            nc.vector.tensor_copy(vw[a][:], tw[a][:].bitcast(U32).indirect(lst[:]))
 
         def gather_scales(a):
             nc.vector.tensor_copy(vs[a][:], ts[:, a * T : (a + 1) * T].indirect(lst[:]))
@@ -147,25 +145,28 @@ def tile_list_paged_softcap_logits_kernel(
             project(a_ps, a, wc[a][:].bitcast(FP8X4), ws[a][:])
 
         gather_words(0)
+        load_table_words(1, "slot_a")
         for a in range(PASSES):
             gather_scales(a)
+        load_table_words(2, "slot_c")
         round_wq(0)
-        gather_words(1)
-        quantize_wq(0)
-        gate_pass(0)
-        query_pass(0)
-        gate_pass(1)
-        gather_words(2)
-        gate_pass(2)
-        for c in range(QCHUNKS):
-            nc.scalar.activation(gate[c][:], b_ps[c][:], SIGMOID)
+        load_wq(2, "slot_d")
         round_wq(1)
-        gather_key_scales(0)
-        quantize_wq(1)
-        query_pass(1)
+        gather_words(1)
+        t2w = keep.tile([P, T2], I32, name="t2w", tag="slot_a", align_bytes=64)
+        nc.sync.dma_start(out=t2w[:], in_=tab2_words[0].rearrange("p t i -> p (t i)").bitcast(I32))
+        gather_words(2)
+        for a in range(PASSES - 1):
+            quantize_wq(a)
+            gate_pass(a)
+            query_pass(a)
+        gate_pass(2)
         round_wq(2)
         quantize_wq(2)
         query_pass(2)
+        for c in range(QCHUNKS):
+            nc.scalar.activation(gate[c][:], b_ps[c][:], SIGMOID)
+        gather_key_scales(0)
         kw = keep.tile([P, S2], U32, name="kw", tag="words%d" % (PASSES - 1), align_bytes=64)
 
         grouped = []

@@ -27,6 +27,7 @@ KEY_TILES = S2 // P
 KEY_PIECE = 512
 KEY_PIECES = S2 // KEY_PIECE
 KEY_PLANE_ROW = 4
+KEY_SLOTS = ("words2", "grouped3", "words2")
 SCALAR_COLS = (512, 512, 160)
 
 
@@ -41,27 +42,25 @@ def tile_list_paged_softcap_logits_kernel(
 
         lst = keep.tile([P, S // 16], U16, name="lst")
         lst2 = keep.tile([P, S2 // 16], U16, name="lst2")
-        ts = keep.tile([P, PASSES * T], U8, name="ts", tag="slot_c", align_bytes=64)
+        ts = keep.tile([P, PASSES * T], U8, name="ts", align_bytes=64)
         t2s = keep.tile([P, T2], U8, name="t2s", align_bytes=64)
-        wgw = keep.tile([P, PASSES, 2 * H], U8, name="wgw", align_bytes=64)
         wgs = keep.tile([P, PASSES * H], U8, name="wgs", align_bytes=64)
-        tw, raw = {}, {}
+        tw, raw, kw = {}, {}, {}
         ident = keep.tile([P, P], F32, name="ident", align_bytes=64)
-        warm_in = keep.tile([P, 1], F32, name="warm_in", tag="slot_d", align_bytes=64)
-        warm_out = keep.tile([P, 1], F32, name="warm_out", tag="slot_e", align_bytes=64)
+        warm_in = keep.tile([P, 1], F32, name="warm_in")
+        warm_out = keep.tile([P, 1], F32, name="warm_out")
 
-        nc.vector.memset(warm_in[:], 0.0)
-        nc.scalar.activation(warm_out[:], warm_in[:], SIGMOID)
         nc.vector.memset(ts[:].bitcast(I32), 0)
+        nc.vector.memset(warm_in[:], 0.0)
         nc.vector.memset(t2s[:].bitcast(I32), 0)
         nc.vector.memset(wgs[:].bitcast(I32), 0)
 
-        def load_table_words(a, slot):
-            tw[a] = keep.tile([P, T], I32, name="tw%d" % a, tag=slot, align_bytes=64)
+        def load_table_words(a):
+            tw[a] = keep.tile([P, T], I32, name="tw%d" % a, align_bytes=64)
             nc.sync.dma_start(out=tw[a][:], in_=tab_words[a].rearrange("p t i -> p (t i)").bitcast(I32))
 
-        def load_wq(a, slot):
-            raw[a] = keep.tile([P, PACK, H], F32, name="raw%d" % a, tag=slot, align_bytes=64)
+        def load_wq(a):
+            raw[a] = keep.tile([P, PACK, H], F32, name="raw%d" % a, tag="raw%d" % a, align_bytes=64)
             rows = wq[a * P * PACK : (a + 1) * P * PACK, :]
             nc.sync.dma_start(out=raw[a][:], in_=rows.rearrange("(p j) c -> p j c", j=PACK))
 
@@ -74,13 +73,20 @@ def tile_list_paged_softcap_logits_kernel(
 
         nc.sync.dma_start(lst[:], offs)
         nc.sync.dma_start(lst2[:], offs2)
-        load_table_words(0, "slot_a")
-        load_scale_rows(nc.sync, ts, tab_scales, 0)
-        load_wq(0, "slot_d")
-        load_wq(1, "slot_e")
-        nc.gpsimd.dma_start(out=wgw[:].bitcast(I32), in_=wg_words.rearrange("a p c -> p a c").bitcast(I32))
-        load_scale_rows(nc.gpsimd, t2s, tab2_scales, KEY_PLANE_ROW)
-        load_scale_rows(nc.gpsimd, wgs, wg_scales, 0)
+        load_table_words(0)
+        load_scale_rows(nc.scalar, ts, tab_scales, 0)
+        nc.scalar.activation(warm_out[:], warm_in[:], SIGMOID)
+        load_wq(0)
+        load_scale_rows(nc.sync, t2s, tab2_scales, KEY_PLANE_ROW)
+        wgw = keep.tile([P, PASSES, 2 * H], U8, name="wgw", align_bytes=64)
+        nc.sync.dma_start(out=wgw[:].bitcast(I32), in_=wg_words.rearrange("a p c -> p a c").bitcast(I32))
+        load_wq(1)
+        load_scale_rows(nc.sync, wgs, wg_scales, 0)
+        load_table_words(1)
+        load_table_words(2)
+        load_wq(2)
+        t2w = keep.tile([P, T2], I32, name="t2w", align_bytes=64)
+        nc.sync.dma_start(out=t2w[:], in_=tab2_words[0].rearrange("p t i -> p (t i)").bitcast(I32))
         make_identity(nc, ident[:])
 
         vw = [keep.tile([P, S], U32, name="vw%d" % a, tag="words%d" % a, align_bytes=64) for a in range(PASSES)]
@@ -89,7 +95,6 @@ def tile_list_paged_softcap_logits_kernel(
         wb = [keep.tile([P, H, PACK], BF16, name="wb%d" % a, align_bytes=64) for a in range(PASSES)]
         wc = [keep.tile([P, H], U32, name="wc%d" % a, align_bytes=64) for a in range(PASSES)]
         ws = [keep.tile([P, H], U8, name="ws%d" % a, align_bytes=64) for a in range(PASSES)]
-        gate = [keep.tile([P, H], F32, name="gate%d" % c, align_bytes=64) for c in range(QCHUNKS)]
         hc = keep.tile([P, S], U32, name="hc", align_bytes=64)
         hs = keep.tile([P, S], U8, name="hs", align_bytes=64)
 
@@ -97,8 +102,13 @@ def tile_list_paged_softcap_logits_kernel(
             cols = KEY_PIECE // 16
             return lst2[:, g * cols : (g + 1) * cols]
 
-        def gather_words(a):
-            nc.vector.tensor_copy(vw[a][:], tw[a][:].bitcast(U32).indirect(lst[:]))
+        def gather_words(a, parts=1):
+            width = S // parts
+            for part in range(parts):
+                offsets = lst[:, part * width // 16 : (part + 1) * width // 16]
+                nc.vector.tensor_copy(
+                    vw[a][:, part * width : (part + 1) * width], tw[a][:].bitcast(U32).indirect(offsets)
+                )
 
         def gather_scales(a):
             nc.vector.tensor_copy(vs[a][:], ts[:, a * T : (a + 1) * T].indirect(lst[:]))
@@ -107,7 +117,8 @@ def tile_list_paged_softcap_logits_kernel(
             nc.vector.tensor_copy(ks[g][:], t2s[:].indirect(piece(g)))
 
         def gather_key_words(g):
-            nc.vector.tensor_copy(kw[:, g * KEY_PIECE : (g + 1) * KEY_PIECE], t2w[:].bitcast(U32).indirect(piece(g)))
+            kw[g] = keep.tile([P, KEY_PIECE], U32, name="kw%d" % g, tag=KEY_SLOTS[g], align_bytes=64)
+            nc.vector.tensor_copy(kw[g][:], t2w[:].bitcast(U32).indirect(piece(g)))
 
         def round_wq(a):
             split = SCALAR_COLS[a]
@@ -125,8 +136,8 @@ def tile_list_paged_softcap_logits_kernel(
         b_ps = [psum.tile([P, H], F32, tag="bank", name="b_ps%d" % c) for c in range(QCHUNKS)]
         a_ps = [psum.tile([P, H], F32, tag="bank", name="a_ps%d" % c) for c in range(QCHUNKS)]
 
-        def project(acc, a, rhs, rhs_scale):
-            for c in range(QCHUNKS):
+        def project(acc, a, rhs, rhs_scale, chunks):
+            for c in chunks:
                 cols = slice(c * P, (c + 1) * P)
                 nc.tensor.matmul_mx(
                     out=acc[c][:],
@@ -138,46 +149,45 @@ def tile_list_paged_softcap_logits_kernel(
                     stop=(a == PASSES - 1),
                 )
 
-        def gate_pass(a):
-            project(b_ps, a, wgw[:, a, :].bitcast(FP4X4), wgs[:, a * H : (a + 1) * H])
+        def gate_pass(a, chunks):
+            project(b_ps, a, wgw[:, a, :].bitcast(FP4X4), wgs[:, a * H : (a + 1) * H], chunks)
 
-        def query_pass(a):
-            project(a_ps, a, wc[a][:].bitcast(FP8X4), ws[a][:])
+        def query_pass(a, chunks):
+            project(a_ps, a, wc[a][:].bitcast(FP8X4), ws[a][:], chunks)
 
+        every_chunk = range(QCHUNKS)
         gather_words(0)
-        load_table_words(1, "slot_a")
         for a in range(PASSES):
             gather_scales(a)
-        load_table_words(2, "slot_c")
+        for g in range(KEY_PIECES):
+            gather_key_scales(g)
         round_wq(0)
-        load_wq(2, "slot_d")
+        quantize_wq(0)
+        gate_pass(0, every_chunk)
+        query_pass(0, every_chunk)
         round_wq(1)
         gather_words(1)
-        t2w = keep.tile([P, T2], I32, name="t2w", tag="slot_a", align_bytes=64)
-        nc.sync.dma_start(out=t2w[:], in_=tab2_words[0].rearrange("p t i -> p (t i)").bitcast(I32))
+        quantize_wq(1)
+        gate_pass(1, every_chunk)
+        query_pass(1, every_chunk)
         gather_words(2)
-        for a in range(PASSES - 1):
-            quantize_wq(a)
-            gate_pass(a)
-            query_pass(a)
-        gate_pass(2)
+        gate_pass(2, every_chunk)
         round_wq(2)
         quantize_wq(2)
-        query_pass(2)
-        for c in range(QCHUNKS):
-            nc.scalar.activation(gate[c][:], b_ps[c][:], SIGMOID)
-        gather_key_scales(0)
-        kw = keep.tile([P, S2], U32, name="kw", tag="words%d" % (PASSES - 1), align_bytes=64)
+        query_pass(2, every_chunk)
+        gate = keep.tile([P, QCHUNKS, H], F32, name="gate", tag="raw%d" % (PASSES - 1), align_bytes=64)
+        for c in every_chunk:
+            nc.scalar.activation(gate[:, c, :], b_ps[c][:], SIGMOID)
 
         grouped = []
         for c in range(QCHUNKS):
             ht = ring.tile([P, H], BF16, name="ht", align_bytes=64)
-            nc.vector.tensor_tensor(ht[:], a_ps[c][:], gate[c][:], MULT)
+            nc.vector.tensor_tensor(ht[:], a_ps[c][:], gate[:, c, :], MULT)
             words = ht[:].bitcast(F32)
             xt = psum.tile([P, 2, P], F32, tag="bank", name="xt%d" % c)
             for u in range(2):
                 nc.tensor.transpose(xt[:, u, :], words[:, u : H // 2 : 2], ident[:])
-            hg = ring.tile([P, P, PACK], BF16, name="hg", align_bytes=64)
+            hg = keep.tile([P, P, PACK], BF16, name="hg%d" % c, tag="grouped%d" % c, align_bytes=64)
             nc.scalar.copy(hg[:].bitcast(F32), xt[:].rearrange("p u j -> p j u"))
             grouped.append(hg)
         for c in range(QCHUNKS):
@@ -191,19 +201,18 @@ def tile_list_paged_softcap_logits_kernel(
         for i in range(KEY_TILES):
             g, cols = i // tiles_per_piece, slice((i % tiles_per_piece) * P, (i % tiles_per_piece + 1) * P)
             if i % tiles_per_piece == 0 and g + 1 < KEY_PIECES:
-                gather_key_scales(g + 1)
                 gather_key_words(g + 1)
             z = psum.tile([P, S], F32, tag="bank", name="z%d" % i)
             nc.tensor.matmul_mx(
                 out=z[:],
-                lhsT=kw[:, i * P : (i + 1) * P].bitcast(FP8X4),
+                lhsT=kw[g][:, cols].bitcast(FP8X4),
                 lhsT_scale=ks[g][KEY_PLANE_ROW:P, cols],
                 rhs=hc[:].bitcast(FP8X4),
                 rhs_scale=hs[:],
                 start=True,
                 stop=True,
             )
-            sig = ring.tile([P, S], F32, name="sig")
+            sig = ring.tile([P, S], F32, name="sig", bufs=6)
             nc.scalar.activation(sig[:], z[:], SIGMOID, scale=2.0 / CAP)
             res = keep.tile([P, S], F32, name="res%d" % i)
             nc.vector.tensor_scalar(res[:], sig[:], 2.0 * CAP, -CAP, MULT, ADD)

@@ -26,9 +26,9 @@ QCHUNKS = S // P
 KEY_TILES = S2 // P
 KEY_PIECE = 512
 KEY_PIECES = S2 // KEY_PIECE
-KEY_PLANE_ROW = 4
-KEY_SLOTS = ("words2", "grouped3", "words2")
-SCALAR_COLS = (512, 512, 160)
+KEY_PLANE_ROW = 12
+KEY_SLOTS = ("words2", "grouped3", "late")
+SCALAR_COLS = (512, 512, 256)
 
 
 def tile_list_paged_softcap_logits_kernel(
@@ -42,7 +42,9 @@ def tile_list_paged_softcap_logits_kernel(
 
         lst = keep.tile([P, S // 16], U16, name="lst")
         lst2 = keep.tile([P, S2 // 16], U16, name="lst2")
-        ts = keep.tile([P, PASSES * T], U8, name="ts", align_bytes=64)
+        ts = keep.tile([P, T], U8, name="ts", align_bytes=64)
+        vs = keep.tile([P, S], U8, name="vs", align_bytes=64)
+        vs_low = keep.tile([P, PASSES - 1, S], U8, name="vs_low", align_bytes=64)
         t2s = keep.tile([P, T2], U8, name="t2s", align_bytes=64)
         wgs = keep.tile([P, PASSES * H], U8, name="wgs", align_bytes=64)
         tw, raw, kw = {}, {}, {}
@@ -54,6 +56,7 @@ def tile_list_paged_softcap_logits_kernel(
         nc.vector.memset(warm_in[:], 0.0)
         nc.vector.memset(t2s[:].bitcast(I32), 0)
         nc.vector.memset(wgs[:].bitcast(I32), 0)
+        nc.vector.memset(vs_low[:].bitcast(I32), 0)
 
         def load_table_words(a):
             tw[a] = keep.tile([P, T], I32, name="tw%d" % a, align_bytes=64)
@@ -72,25 +75,46 @@ def tile_list_paged_softcap_logits_kernel(
                 queue.dma_start(out=dst[first_row + r : P : 32], in_=by_row[r].bitcast(I32))
 
         nc.sync.dma_start(lst[:], offs)
-        nc.sync.dma_start(lst2[:], offs2)
         load_table_words(0)
-        load_scale_rows(nc.scalar, ts, tab_scales, 0)
+        nc.sync.dma_start(lst2[:], offs2)
+        for q in range(4):
+            nc.scalar.dma_start(
+                out=ts[32 * q : 32 * q + 4 * PASSES, :].bitcast(I32), in_=tab_scales[:, 4 * q : 4 * q + 4, :].bitcast(I32)
+            )
         nc.scalar.activation(warm_out[:], warm_in[:], SIGMOID)
-        load_wq(0)
         load_scale_rows(nc.sync, t2s, tab2_scales, KEY_PLANE_ROW)
-        wgw = keep.tile([P, PASSES, 2 * H], U8, name="wgw", align_bytes=64)
-        nc.sync.dma_start(out=wgw[:].bitcast(I32), in_=wg_words.rearrange("a p c -> p a c").bitcast(I32))
+        load_wq(0)
         load_wq(1)
         load_scale_rows(nc.sync, wgs, wg_scales, 0)
+        wgw = keep.tile([P, PASSES, 2 * H], U8, name="wgw", align_bytes=64)
+        nc.sync.dma_start(out=wgw[:].bitcast(I32), in_=wg_words.rearrange("a p c -> p a c").bitcast(I32))
+        vw = [keep.tile([P, S], U32, name="vw%d" % a, tag="words%d" % a, align_bytes=64) for a in range(PASSES)]
+
+        def gather_words(a, parts=1):
+            width = S // parts
+            for part in range(parts):
+                offsets = lst[:, part * width // 16 : (part + 1) * width // 16]
+                nc.vector.tensor_copy(
+                    vw[a][:, part * width : (part + 1) * width], tw[a][:].bitcast(U32).indirect(offsets)
+                )
+
+        def lower_scale_rows(a):
+            for r in range(4):
+                nc.sync.dma_start(
+                    out=vs_low[r:P:32, a - 1, :].bitcast(I32), in_=vs[4 * a + r : P : 32, :].bitcast(I32)
+                )
+
+        gather_words(0)
+        nc.vector.tensor_copy(vs[:], ts[:].indirect(lst[:]))
         load_table_words(1)
-        load_table_words(2)
+        lower_scale_rows(1)
         load_wq(2)
+        lower_scale_rows(2)
+        load_table_words(2)
         t2w = keep.tile([P, T2], I32, name="t2w", align_bytes=64)
         nc.sync.dma_start(out=t2w[:], in_=tab2_words[0].rearrange("p t i -> p (t i)").bitcast(I32))
         make_identity(nc, ident[:])
 
-        vw = [keep.tile([P, S], U32, name="vw%d" % a, tag="words%d" % a, align_bytes=64) for a in range(PASSES)]
-        vs = [keep.tile([P, S], U8, name="vs%d" % a, align_bytes=64) for a in range(PASSES)]
         ks = [keep.tile([P, KEY_PIECE], U8, name="ks%d" % g, align_bytes=64) for g in range(KEY_PIECES)]
         wb = [keep.tile([P, H, PACK], BF16, name="wb%d" % a, align_bytes=64) for a in range(PASSES)]
         wc = [keep.tile([P, H], U32, name="wc%d" % a, align_bytes=64) for a in range(PASSES)]
@@ -101,17 +125,6 @@ def tile_list_paged_softcap_logits_kernel(
         def piece(g):
             cols = KEY_PIECE // 16
             return lst2[:, g * cols : (g + 1) * cols]
-
-        def gather_words(a, parts=1):
-            width = S // parts
-            for part in range(parts):
-                offsets = lst[:, part * width // 16 : (part + 1) * width // 16]
-                nc.vector.tensor_copy(
-                    vw[a][:, part * width : (part + 1) * width], tw[a][:].bitcast(U32).indirect(offsets)
-                )
-
-        def gather_scales(a):
-            nc.vector.tensor_copy(vs[a][:], ts[:, a * T : (a + 1) * T].indirect(lst[:]))
 
         def gather_key_scales(g):
             nc.vector.tensor_copy(ks[g][:], t2s[:].indirect(piece(g)))
@@ -136,13 +149,13 @@ def tile_list_paged_softcap_logits_kernel(
         b_ps = [psum.tile([P, H], F32, tag="bank", name="b_ps%d" % c) for c in range(QCHUNKS)]
         a_ps = [psum.tile([P, H], F32, tag="bank", name="a_ps%d" % c) for c in range(QCHUNKS)]
 
-        def project(acc, a, rhs, rhs_scale, chunks):
+        def project(acc, a, plane, rhs, rhs_scale, chunks):
             for c in chunks:
                 cols = slice(c * P, (c + 1) * P)
                 nc.tensor.matmul_mx(
                     out=acc[c][:],
                     lhsT=vw[a][:, cols].bitcast(FP8X4),
-                    lhsT_scale=vs[a][:, cols],
+                    lhsT_scale=plane[:, cols],
                     rhs=rhs,
                     rhs_scale=rhs_scale,
                     start=(a == 0),
@@ -150,15 +163,12 @@ def tile_list_paged_softcap_logits_kernel(
                 )
 
         def gate_pass(a, chunks):
-            project(b_ps, a, wgw[:, a, :].bitcast(FP4X4), wgs[:, a * H : (a + 1) * H], chunks)
+            project(b_ps, a, vs[:] if a == 0 else vs_low[:, a - 1, :], wgw[:, a, :].bitcast(FP4X4), wgs[:, a * H : (a + 1) * H], chunks)
 
         def query_pass(a, chunks):
-            project(a_ps, a, wc[a][:].bitcast(FP8X4), ws[a][:], chunks)
+            project(a_ps, a, vs[4 * a : P, :], wc[a][:].bitcast(FP8X4), ws[a][:], chunks)
 
         every_chunk = range(QCHUNKS)
-        gather_words(0)
-        for a in range(PASSES):
-            gather_scales(a)
         for g in range(KEY_PIECES):
             gather_key_scales(g)
         round_wq(0)
@@ -170,14 +180,16 @@ def tile_list_paged_softcap_logits_kernel(
         quantize_wq(1)
         gate_pass(1, every_chunk)
         query_pass(1, every_chunk)
-        gather_words(2)
-        gate_pass(2, every_chunk)
         round_wq(2)
         quantize_wq(2)
-        query_pass(2, every_chunk)
-        gate = keep.tile([P, QCHUNKS, H], F32, name="gate", tag="raw%d" % (PASSES - 1), align_bytes=64)
-        for c in every_chunk:
-            nc.scalar.activation(gate[:, c, :], b_ps[c][:], SIGMOID)
+        gather_words(2, parts=2)
+        gate = keep.tile([P, QCHUNKS, H], F32, name="gate", align_bytes=64)
+        for c in range(QCHUNKS + 1):
+            if c < QCHUNKS:
+                gate_pass(2, [c])
+                nc.scalar.activation(gate[:, c, :], b_ps[c][:], SIGMOID)
+            if c > 0:
+                query_pass(2, [c - 1])
 
         grouped = []
         for c in range(QCHUNKS):
@@ -212,8 +224,12 @@ def tile_list_paged_softcap_logits_kernel(
                 start=True,
                 stop=True,
             )
-            sig = ring.tile([P, S], F32, name="sig", bufs=6)
-            nc.scalar.activation(sig[:], z[:], SIGMOID, scale=2.0 / CAP)
+            tag = "late" if i == 1 else "sig%d" % i
+            sig = keep.tile([P, S], F32, name="sig%d" % i, tag=tag, align_bytes=64)
             res = keep.tile([P, S], F32, name="res%d" % i)
-            nc.vector.tensor_scalar(res[:], sig[:], 2.0 * CAP, -CAP, MULT, ADD)
-            nc.sync.dma_start(out=out[i * P : (i + 1) * P, :], in_=res[:])
+            parts = 2 if i == KEY_TILES - 1 else 1
+            for part in range(parts):
+                js = slice(part * S // parts, (part + 1) * S // parts)
+                nc.scalar.activation(sig[:, js], z[:, js], SIGMOID, scale=2.0 / CAP)
+                nc.vector.tensor_scalar(res[:, js], sig[:, js], 2.0 * CAP, -CAP, MULT, ADD)
+                nc.sync.dma_start(out=out[i * P : (i + 1) * P, js], in_=res[:, js])

@@ -1,7 +1,6 @@
 from contextlib import ExitStack
 
 import concourse.mybir as mybir
-from concourse.masks import make_identity
 
 K, H, T, S, T2, S2 = 1536, 512, 2048, 512, 4096, 1536
 CAP = 2.0
@@ -27,8 +26,11 @@ KEY_TILES = S2 // P
 KEY_PIECE = 512
 KEY_PIECES = S2 // KEY_PIECE
 KEY_PLANE_ROW = 12
-KEY_SLOTS = ("words2", "grouped3", "late")
-SCALAR_COLS = (512, 512, 256)
+KEY_SLOTS = ("gate3", "grouped3", "grouped2")
+CODE_SLOTS = ("wc0", "tw0", "tw1")
+PLANE_SLOTS = ("ts", "ws1", "ws2")
+POOL_TILES = 2
+MOVED_ROWS = 112
 
 
 def tile_list_paged_softcap_logits_kernel(
@@ -37,29 +39,27 @@ def tile_list_paged_softcap_logits_kernel(
     nc = tc.nc
     with ExitStack() as ctx:
         keep = ctx.enter_context(tc.tile_pool(name="keep", bufs=1))
-        ring = ctx.enter_context(tc.tile_pool(name="ring", bufs=4))
         psum = ctx.enter_context(tc.psum_pool(name="psum", bufs=8))
 
         lst = keep.tile([P, S // 16], U16, name="lst")
         lst2 = keep.tile([P, S2 // 16], U16, name="lst2")
-        ts = keep.tile([P, T], U8, name="ts", align_bytes=64)
+        ts = keep.tile([P, T], U8, name="ts", tag="ts", align_bytes=64)
         vs = keep.tile([P, S], U8, name="vs", align_bytes=64)
         vs_low = keep.tile([P, PASSES - 1, S], U8, name="vs_low", align_bytes=64)
         t2s = keep.tile([P, T2], U8, name="t2s", align_bytes=64)
         wgs = keep.tile([P, PASSES * H], U8, name="wgs", align_bytes=64)
         tw, raw, kw = {}, {}, {}
-        ident = keep.tile([P, P], F32, name="ident", align_bytes=64)
         warm_in = keep.tile([P, 1], F32, name="warm_in")
         warm_out = keep.tile([P, 1], F32, name="warm_out")
 
         nc.vector.memset(ts[:].bitcast(I32), 0)
         nc.vector.memset(warm_in[:], 0.0)
         nc.vector.memset(t2s[:].bitcast(I32), 0)
-        nc.vector.memset(wgs[:].bitcast(I32), 0)
+        nc.gpsimd.memset(wgs[:].bitcast(I32), 0)
         nc.vector.memset(vs_low[:].bitcast(I32), 0)
 
         def load_table_words(a):
-            tw[a] = keep.tile([P, T], I32, name="tw%d" % a, align_bytes=64)
+            tw[a] = keep.tile([P, T], I32, name="tw%d" % a, tag="tw%d" % a, align_bytes=64)
             nc.sync.dma_start(out=tw[a][:], in_=tab_words[a].rearrange("p t i -> p (t i)").bitcast(I32))
 
         def load_wq(a):
@@ -74,20 +74,6 @@ def tile_list_paged_softcap_logits_kernel(
             for r in range(4):
                 queue.dma_start(out=dst[first_row + r : P : 32], in_=by_row[r].bitcast(I32))
 
-        nc.sync.dma_start(lst[:], offs)
-        load_table_words(0)
-        nc.sync.dma_start(lst2[:], offs2)
-        for q in range(4):
-            nc.scalar.dma_start(
-                out=ts[32 * q : 32 * q + 4 * PASSES, :].bitcast(I32), in_=tab_scales[:, 4 * q : 4 * q + 4, :].bitcast(I32)
-            )
-        nc.scalar.activation(warm_out[:], warm_in[:], SIGMOID)
-        load_scale_rows(nc.sync, t2s, tab2_scales, KEY_PLANE_ROW)
-        load_wq(0)
-        load_wq(1)
-        load_scale_rows(nc.sync, wgs, wg_scales, 0)
-        wgw = keep.tile([P, PASSES, 2 * H], U8, name="wgw", align_bytes=64)
-        nc.sync.dma_start(out=wgw[:].bitcast(I32), in_=wg_words.rearrange("a p c -> p a c").bitcast(I32))
         vw = [keep.tile([P, S], U32, name="vw%d" % a, tag="words%d" % a, align_bytes=64) for a in range(PASSES)]
 
         def gather_words(a, parts=1):
@@ -99,26 +85,44 @@ def tile_list_paged_softcap_logits_kernel(
                 )
 
         def lower_scale_rows(a):
-            for r in range(4):
-                nc.sync.dma_start(
-                    out=vs_low[r:P:32, a - 1, :].bitcast(I32), in_=vs[4 * a + r : P : 32, :].bitcast(I32)
-                )
+            nc.sync.dma_start(
+                out=vs_low[0:MOVED_ROWS, a - 1, :].bitcast(I32), in_=vs[4 * a : 4 * a + MOVED_ROWS, :].bitcast(I32)
+            )
 
-        gather_words(0)
-        nc.vector.tensor_copy(vs[:], ts[:].indirect(lst[:]))
-        load_table_words(1)
-        lower_scale_rows(1)
+        wgw = keep.tile([P, PASSES, 2 * H], U8, name="wgw", align_bytes=64)
+        nc.sync.dma_start(lst[:], offs)
+        nc.sync.dma_start(lst2[:], offs2)
+        nc.sync.dma_start(out=wgw[:].bitcast(I32), in_=wg_words.rearrange("a p c -> p a c").bitcast(I32))
+        load_scale_rows(nc.sync, wgs, wg_scales, 0)
+        nc.scalar.activation(warm_out[:], warm_in[:], SIGMOID)
+        load_wq(0)
+        load_wq(1)
+        for q in range(4):
+            nc.sync.dma_start(
+                out=ts[32 * q : 32 * q + 4 * PASSES, :].bitcast(I32), in_=tab_scales[:, 4 * q : 4 * q + 4, :].bitcast(I32)
+            )
+        load_table_words(0)
+        load_scale_rows(nc.sync, t2s, tab2_scales, KEY_PLANE_ROW)
         load_wq(2)
+        nc.vector.tensor_copy(vs[:], ts[:].indirect(lst[:]))
+        lower_scale_rows(1)
         lower_scale_rows(2)
+        load_table_words(1)
         load_table_words(2)
         t2w = keep.tile([P, T2], I32, name="t2w", align_bytes=64)
         nc.sync.dma_start(out=t2w[:], in_=tab2_words[0].rearrange("p t i -> p (t i)").bitcast(I32))
-        make_identity(nc, ident[:])
+        gw = keep.tile([P, PASSES, H], U16, name="gw", align_bytes=64)
+        gs = keep.tile([P, PASSES, H], U8, name="gs", align_bytes=64)
+        nc.vector.tensor_copy(
+            gw[:].rearrange("p a (j m) -> p a j m", j=PACK), wgw[:].bitcast(U16).rearrange("p a (m j) -> p a j m", j=PACK)
+        )
+        nc.vector.tensor_copy(
+            gs[:].rearrange("p a (j m) -> p a j m", j=PACK), wgs[:].rearrange("p (a m j) -> p a j m", a=PASSES, j=PACK)
+        )
 
-        ks = [keep.tile([P, KEY_PIECE], U8, name="ks%d" % g, align_bytes=64) for g in range(KEY_PIECES)]
-        wb = [keep.tile([P, H, PACK], BF16, name="wb%d" % a, align_bytes=64) for a in range(PASSES)]
-        wc = [keep.tile([P, H], U32, name="wc%d" % a, align_bytes=64) for a in range(PASSES)]
-        ws = [keep.tile([P, H], U8, name="ws%d" % a, align_bytes=64) for a in range(PASSES)]
+        ks = {}
+        wb = [keep.tile([P, H, PACK], BF16, name="wb%d" % a, tag="wb%d" % a, align_bytes=64) for a in range(PASSES)]
+        wc, ws = {}, {}
         hc = keep.tile([P, S], U32, name="hc", align_bytes=64)
         hs = keep.tile([P, S], U8, name="hs", align_bytes=64)
 
@@ -127,6 +131,7 @@ def tile_list_paged_softcap_logits_kernel(
             return lst2[:, g * cols : (g + 1) * cols]
 
         def gather_key_scales(g):
+            ks[g] = keep.tile([P, KEY_PIECE], U8, name="ks%d" % g, align_bytes=64)
             nc.vector.tensor_copy(ks[g][:], t2s[:].indirect(piece(g)))
 
         def gather_key_words(g):
@@ -134,14 +139,13 @@ def tile_list_paged_softcap_logits_kernel(
             nc.vector.tensor_copy(kw[g][:], t2w[:].bitcast(U32).indirect(piece(g)))
 
         def round_wq(a):
-            split = SCALAR_COLS[a]
-            src = raw[a][:].rearrange("p t (c i) -> p c t i", i=4)
-            dst = wb[a][:].rearrange("p (c i) t -> p c t i", i=4)
-            nc.scalar.copy(dst[:, : split // 4], src[:, : split // 4])
-            if split < H:
-                nc.vector.tensor_copy(dst[:, split // 4 :], src[:, split // 4 :])
+            src = raw[a][:].rearrange("p t (m j) -> p m t j", j=PACK)
+            dst = wb[a][:].rearrange("p (j m) t -> p m t j", j=PACK)
+            nc.scalar.copy(dst, src)
 
         def quantize_wq(a):
+            wc[a] = keep.tile([P, H], U32, name="wc%d" % a, tag=CODE_SLOTS[a], align_bytes=64)
+            ws[a] = keep.tile([P, H], U8, name="ws%d" % a, tag=PLANE_SLOTS[a], align_bytes=64)
             nc.vector.quantize_mx(
                 out=wc[a][:].bitcast(FP8X4), scales=ws[a][:], in_=wb[a][:].rearrange("p c t -> p (c t)")
             )
@@ -149,71 +153,83 @@ def tile_list_paged_softcap_logits_kernel(
         b_ps = [psum.tile([P, H], F32, tag="bank", name="b_ps%d" % c) for c in range(QCHUNKS)]
         a_ps = [psum.tile([P, H], F32, tag="bank", name="a_ps%d" % c) for c in range(QCHUNKS)]
 
-        def project(acc, a, plane, rhs, rhs_scale, chunks):
+        def project(acc, a, words, plane, v_plane, chunks):
             for c in chunks:
                 cols = slice(c * P, (c + 1) * P)
-                nc.tensor.matmul_mx(
-                    out=acc[c][:],
-                    lhsT=vw[a][:, cols].bitcast(FP8X4),
-                    lhsT_scale=plane[:, cols],
-                    rhs=rhs,
-                    rhs_scale=rhs_scale,
-                    start=(a == 0),
-                    stop=(a == PASSES - 1),
-                )
+                for j in range(PACK):
+                    nc.tensor.matmul_mx(
+                        out=acc[c][:, j * P : (j + 1) * P],
+                        lhsT=words(j),
+                        lhsT_scale=plane[:, j * P : (j + 1) * P],
+                        rhs=vw[a][:, cols].bitcast(FP8X4),
+                        rhs_scale=v_plane[:, cols],
+                        start=(a == 0 and j == 0),
+                        stop=(a == PASSES - 1 and j == PACK - 1),
+                    )
 
         def gate_pass(a, chunks):
-            project(b_ps, a, vs[:] if a == 0 else vs_low[:, a - 1, :], wgw[:, a, :].bitcast(FP4X4), wgs[:, a * H : (a + 1) * H], chunks)
-
-        def query_pass(a, chunks):
-            project(a_ps, a, vs[4 * a : P, :], wc[a][:].bitcast(FP8X4), ws[a][:], chunks)
-
-        every_chunk = range(QCHUNKS)
-        for g in range(KEY_PIECES):
-            gather_key_scales(g)
-        round_wq(0)
-        quantize_wq(0)
-        gate_pass(0, every_chunk)
-        query_pass(0, every_chunk)
-        round_wq(1)
-        gather_words(1)
-        quantize_wq(1)
-        gate_pass(1, every_chunk)
-        query_pass(1, every_chunk)
-        round_wq(2)
-        quantize_wq(2)
-        gather_words(2, parts=2)
-        gate = keep.tile([P, QCHUNKS, H], F32, name="gate", align_bytes=64)
-        for c in range(QCHUNKS + 1):
-            if c < QCHUNKS:
-                gate_pass(2, [c])
-                nc.scalar.activation(gate[:, c, :], b_ps[c][:], SIGMOID)
-            if c > 0:
-                query_pass(2, [c - 1])
-
-        grouped = []
-        for c in range(QCHUNKS):
-            ht = ring.tile([P, H], BF16, name="ht", align_bytes=64)
-            nc.vector.tensor_tensor(ht[:], a_ps[c][:], gate[:, c, :], MULT)
-            words = ht[:].bitcast(F32)
-            xt = psum.tile([P, 2, P], F32, tag="bank", name="xt%d" % c)
-            for u in range(2):
-                nc.tensor.transpose(xt[:, u, :], words[:, u : H // 2 : 2], ident[:])
-            hg = keep.tile([P, P, PACK], BF16, name="hg%d" % c, tag="grouped%d" % c, align_bytes=64)
-            nc.scalar.copy(hg[:].bitcast(F32), xt[:].rearrange("p u j -> p j u"))
-            grouped.append(hg)
-        for c in range(QCHUNKS):
-            cols = slice(c * P, (c + 1) * P)
-            nc.vector.quantize_mx(
-                out=hc[:, cols].bitcast(FP8X4), scales=hs[:, cols], in_=grouped[c][:].rearrange("p j t -> p (j t)")
+            codes = gw[:, a, :].bitcast(U8)
+            project(
+                b_ps,
+                a,
+                lambda j: codes[:, 2 * j * P : 2 * (j + 1) * P].bitcast(FP4X4),
+                gs[:, a, :],
+                vs[:] if a == 0 else vs_low[:, a - 1, :],
+                chunks,
             )
 
+        def query_pass(a, chunks):
+            project(a_ps, a, lambda j: wc[a][:, j * P : (j + 1) * P].bitcast(FP8X4), ws[a][:], vs[4 * a : P, :], chunks)
+
+        every_chunk = range(QCHUNKS)
+        round_wq(0)
+        quantize_wq(0)
+        round_wq(1)
+        gather_words(0)
+        quantize_wq(1)
+        gate_pass(0, every_chunk)
+        query_pass(0, every_chunk)
+        for g in range(KEY_PIECES):
+            gather_key_scales(g)
+        round_wq(2)
+        gather_words(1, parts=2)
+        quantize_wq(2)
+        for c in every_chunk:
+            gate_pass(1, [c])
+            query_pass(1, [c])
+        gather_words(2, parts=2)
+        gate = [keep.tile([P, H], F32, name="gate%d" % c, tag="gate%d" % c, align_bytes=64) for c in every_chunk]
+        for c in every_chunk:
+            gate_pass(2, [c])
+            nc.scalar.activation(
+                gate[c][:].rearrange("p (s j) -> p s j", j=PACK), b_ps[c][:].rearrange("p (j s) -> p s j", j=PACK), SIGMOID
+            )
+            query_pass(2, [c])
+
+        grouped = []
+
+        def quantize_h(c):
+            cols = slice(c * P, (c + 1) * P)
+            nc.vector.quantize_mx(out=hc[:, cols].bitcast(FP8X4), scales=hs[:, cols], in_=grouped[c][:])
+
+        for c in range(QCHUNKS):
+            hg = keep.tile([P, H], BF16, name="hg%d" % c, tag="grouped%d" % c, align_bytes=64)
+            nc.vector.tensor_tensor(
+                hg[:].rearrange("p (s j) -> p s j", j=PACK),
+                a_ps[c][:].rearrange("p (j s) -> p s j", j=PACK),
+                gate[c][:].rearrange("p (s j) -> p s j", j=PACK),
+                MULT,
+            )
+            grouped.append(hg)
+            if c > 0:
+                quantize_h(c - 1)
+        quantize_h(QCHUNKS - 1)
+
         tiles_per_piece = KEY_PIECE // P
-        gather_key_words(0)
+        for g in range(KEY_PIECES):
+            gather_key_words(g)
         for i in range(KEY_TILES):
             g, cols = i // tiles_per_piece, slice((i % tiles_per_piece) * P, (i % tiles_per_piece + 1) * P)
-            if i % tiles_per_piece == 0 and g + 1 < KEY_PIECES:
-                gather_key_words(g + 1)
             z = psum.tile([P, S], F32, tag="bank", name="z%d" % i)
             nc.tensor.matmul_mx(
                 out=z[:],
@@ -224,12 +240,11 @@ def tile_list_paged_softcap_logits_kernel(
                 start=True,
                 stop=True,
             )
-            tag = "late" if i == 1 else "sig%d" % i
-            sig = keep.tile([P, S], F32, name="sig%d" % i, tag=tag, align_bytes=64)
+            sig = keep.tile([P, S], F32, name="sig%d" % i, align_bytes=64)
             res = keep.tile([P, S], F32, name="res%d" % i)
             parts = 2 if i == KEY_TILES - 1 else 1
             for part in range(parts):
                 js = slice(part * S // parts, (part + 1) * S // parts)
                 nc.scalar.activation(sig[:, js], z[:, js], SIGMOID, scale=2.0 / CAP)
-                nc.vector.tensor_scalar(res[:, js], sig[:, js], 2.0 * CAP, -CAP, MULT, ADD)
+                (nc.gpsimd if i < POOL_TILES else nc.vector).tensor_scalar(res[:, js], sig[:, js], 2.0 * CAP, -CAP, MULT, ADD)
                 nc.sync.dma_start(out=out[i * P : (i + 1) * P, js], in_=res[:, js])

@@ -1,6 +1,7 @@
 from contextlib import ExitStack
 
 import concourse.mybir as mybir
+from concourse.masks import make_identity
 
 K, H, T, S, T2, S2 = 1536, 512, 2048, 512, 4096, 1536
 CAP = 2.0
@@ -26,10 +27,9 @@ KEY_TILES = S2 // P
 KEY_PIECE = 512
 KEY_PIECES = S2 // KEY_PIECE
 KEY_PLANE_ROW = 12
-KEY_SLOTS = ("gate3", "grouped3", "grouped2")
 CODE_SLOTS = ("wc0", "tw0", "tw1")
 PLANE_SLOTS = ("ts", "ws1", "ws2")
-POOL_TILES = 2
+SCALAR_COLS = (512, 512, 512)
 MOVED_ROWS = 112
 
 
@@ -39,6 +39,7 @@ def tile_list_paged_softcap_logits_kernel(
     nc = tc.nc
     with ExitStack() as ctx:
         keep = ctx.enter_context(tc.tile_pool(name="keep", bufs=1))
+        ring = ctx.enter_context(tc.tile_pool(name="ring", bufs=4))
         psum = ctx.enter_context(tc.psum_pool(name="psum", bufs=8))
 
         lst = keep.tile([P, S // 16], U16, name="lst")
@@ -49,13 +50,16 @@ def tile_list_paged_softcap_logits_kernel(
         t2s = keep.tile([P, T2], U8, name="t2s", align_bytes=64)
         wgs = keep.tile([P, PASSES * H], U8, name="wgs", align_bytes=64)
         tw, raw, kw = {}, {}, {}
+        ident = keep.tile([P, P], F32, name="ident", align_bytes=64)
         warm_in = keep.tile([P, 1], F32, name="warm_in")
         warm_out = keep.tile([P, 1], F32, name="warm_out")
 
-        nc.vector.memset(ts[:].bitcast(I32), 0)
+        half = T2 // 8
+        nc.vector.memset(t2s[:].bitcast(I32)[:, :half], 0)
+        nc.gpsimd.memset(t2s[:].bitcast(I32)[:, half:], 0)
         nc.vector.memset(warm_in[:], 0.0)
-        nc.vector.memset(t2s[:].bitcast(I32), 0)
-        nc.gpsimd.memset(wgs[:].bitcast(I32), 0)
+        nc.vector.memset(ts[:].bitcast(I32), 0)
+        nc.vector.memset(wgs[:].bitcast(I32), 0)
         nc.vector.memset(vs_low[:].bitcast(I32), 0)
 
         def load_table_words(a):
@@ -93,7 +97,7 @@ def tile_list_paged_softcap_logits_kernel(
         nc.sync.dma_start(lst[:], offs)
         nc.sync.dma_start(lst2[:], offs2)
         nc.sync.dma_start(out=wgw[:].bitcast(I32), in_=wg_words.rearrange("a p c -> p a c").bitcast(I32))
-        load_scale_rows(nc.sync, wgs, wg_scales, 0)
+        load_scale_rows(nc.sync, t2s, tab2_scales, KEY_PLANE_ROW)
         nc.scalar.activation(warm_out[:], warm_in[:], SIGMOID)
         load_wq(0)
         load_wq(1)
@@ -102,23 +106,14 @@ def tile_list_paged_softcap_logits_kernel(
                 out=ts[32 * q : 32 * q + 4 * PASSES, :].bitcast(I32), in_=tab_scales[:, 4 * q : 4 * q + 4, :].bitcast(I32)
             )
         load_table_words(0)
-        load_scale_rows(nc.sync, t2s, tab2_scales, KEY_PLANE_ROW)
+        load_scale_rows(nc.sync, wgs, wg_scales, 0)
         load_wq(2)
         nc.vector.tensor_copy(vs[:], ts[:].indirect(lst[:]))
         lower_scale_rows(1)
         lower_scale_rows(2)
         load_table_words(1)
         load_table_words(2)
-        t2w = keep.tile([P, T2], I32, name="t2w", align_bytes=64)
-        nc.sync.dma_start(out=t2w[:], in_=tab2_words[0].rearrange("p t i -> p (t i)").bitcast(I32))
-        gw = keep.tile([P, PASSES, H], U16, name="gw", align_bytes=64)
-        gs = keep.tile([P, PASSES, H], U8, name="gs", align_bytes=64)
-        nc.vector.tensor_copy(
-            gw[:].rearrange("p a (j m) -> p a j m", j=PACK), wgw[:].bitcast(U16).rearrange("p a (m j) -> p a j m", j=PACK)
-        )
-        nc.vector.tensor_copy(
-            gs[:].rearrange("p a (j m) -> p a j m", j=PACK), wgs[:].rearrange("p (a m j) -> p a j m", a=PASSES, j=PACK)
-        )
+        make_identity(nc, ident[:])
 
         ks = {}
         wb = [keep.tile([P, H, PACK], BF16, name="wb%d" % a, tag="wb%d" % a, align_bytes=64) for a in range(PASSES)]
@@ -134,14 +129,20 @@ def tile_list_paged_softcap_logits_kernel(
             ks[g] = keep.tile([P, KEY_PIECE], U8, name="ks%d" % g, align_bytes=64)
             nc.vector.tensor_copy(ks[g][:], t2s[:].indirect(piece(g)))
 
-        def gather_key_words(g):
-            kw[g] = keep.tile([P, KEY_PIECE], U32, name="kw%d" % g, tag=KEY_SLOTS[g], align_bytes=64)
-            nc.vector.tensor_copy(kw[g][:], t2w[:].bitcast(U32).indirect(piece(g)))
+        def gather_key_words(first, count, slot):
+            run = keep.tile([P, count * KEY_PIECE], U32, name="kw%d" % first, tag=slot, align_bytes=64)
+            cols = KEY_PIECE // 16
+            nc.vector.tensor_copy(run[:], t2w[:].bitcast(U32).indirect(lst2[:, first * cols : (first + count) * cols]))
+            for n in range(count):
+                kw[first + n] = run[:, n * KEY_PIECE : (n + 1) * KEY_PIECE]
 
         def round_wq(a):
-            src = raw[a][:].rearrange("p t (m j) -> p m t j", j=PACK)
-            dst = wb[a][:].rearrange("p (j m) t -> p m t j", j=PACK)
-            nc.scalar.copy(dst, src)
+            split = SCALAR_COLS[a]
+            src = raw[a][:].rearrange("p t (c i) -> p c t i", i=4)
+            dst = wb[a][:].rearrange("p (c i) t -> p c t i", i=4)
+            nc.scalar.copy(dst[:, : split // 4], src[:, : split // 4])
+            if split < H:
+                nc.vector.tensor_copy(dst[:, split // 4 :], src[:, split // 4 :])
 
         def quantize_wq(a):
             wc[a] = keep.tile([P, H], U32, name="wc%d" % a, tag=CODE_SLOTS[a], align_bytes=64)
@@ -153,35 +154,28 @@ def tile_list_paged_softcap_logits_kernel(
         b_ps = [psum.tile([P, H], F32, tag="bank", name="b_ps%d" % c) for c in range(QCHUNKS)]
         a_ps = [psum.tile([P, H], F32, tag="bank", name="a_ps%d" % c) for c in range(QCHUNKS)]
 
-        def project(acc, a, words, plane, v_plane, chunks):
+        def project(acc, a, plane, rhs, rhs_scale, chunks):
             for c in chunks:
                 cols = slice(c * P, (c + 1) * P)
-                for j in range(PACK):
-                    nc.tensor.matmul_mx(
-                        out=acc[c][:, j * P : (j + 1) * P],
-                        lhsT=words(j),
-                        lhsT_scale=plane[:, j * P : (j + 1) * P],
-                        rhs=vw[a][:, cols].bitcast(FP8X4),
-                        rhs_scale=v_plane[:, cols],
-                        start=(a == 0 and j == 0),
-                        stop=(a == PASSES - 1 and j == PACK - 1),
-                    )
+                nc.tensor.matmul_mx(
+                    out=acc[c][:],
+                    lhsT=vw[a][:, cols].bitcast(FP8X4),
+                    lhsT_scale=plane[:, cols],
+                    rhs=rhs,
+                    rhs_scale=rhs_scale,
+                    start=(a == 0),
+                    stop=(a == PASSES - 1),
+                )
 
         def gate_pass(a, chunks):
-            codes = gw[:, a, :].bitcast(U8)
-            project(
-                b_ps,
-                a,
-                lambda j: codes[:, 2 * j * P : 2 * (j + 1) * P].bitcast(FP4X4),
-                gs[:, a, :],
-                vs[:] if a == 0 else vs_low[:, a - 1, :],
-                chunks,
-            )
+            project(b_ps, a, vs[:] if a == 0 else vs_low[:, a - 1, :], wgw[:, a, :].bitcast(FP4X4), wgs[:, a * H : (a + 1) * H], chunks)
 
         def query_pass(a, chunks):
-            project(a_ps, a, lambda j: wc[a][:, j * P : (j + 1) * P].bitcast(FP8X4), ws[a][:], vs[4 * a : P, :], chunks)
+            project(a_ps, a, vs[4 * a : P, :], wc[a][:].bitcast(FP8X4), ws[a][:], chunks)
 
         every_chunk = range(QCHUNKS)
+        for g in range(KEY_PIECES):
+            gather_key_scales(g)
         round_wq(0)
         quantize_wq(0)
         round_wq(1)
@@ -189,9 +183,9 @@ def tile_list_paged_softcap_logits_kernel(
         quantize_wq(1)
         gate_pass(0, every_chunk)
         query_pass(0, every_chunk)
-        for g in range(KEY_PIECES):
-            gather_key_scales(g)
         round_wq(2)
+        t2w = keep.tile([P, T2], I32, name="t2w", tag="raw2", align_bytes=64)
+        nc.scalar.dma_start(out=t2w[:], in_=tab2_words[0].rearrange("p t i -> p (t i)").bitcast(I32))
         gather_words(1, parts=2)
         quantize_wq(2)
         for c in every_chunk:
@@ -201,33 +195,29 @@ def tile_list_paged_softcap_logits_kernel(
         gate = [keep.tile([P, H], F32, name="gate%d" % c, tag="gate%d" % c, align_bytes=64) for c in every_chunk]
         for c in every_chunk:
             gate_pass(2, [c])
-            nc.scalar.activation(
-                gate[c][:].rearrange("p (s j) -> p s j", j=PACK), b_ps[c][:].rearrange("p (j s) -> p s j", j=PACK), SIGMOID
-            )
+            nc.scalar.activation(gate[c][:], b_ps[c][:], SIGMOID)
             query_pass(2, [c])
 
         grouped = []
-
-        def quantize_h(c):
-            cols = slice(c * P, (c + 1) * P)
-            nc.vector.quantize_mx(out=hc[:, cols].bitcast(FP8X4), scales=hs[:, cols], in_=grouped[c][:])
-
         for c in range(QCHUNKS):
-            hg = keep.tile([P, H], BF16, name="hg%d" % c, tag="grouped%d" % c, align_bytes=64)
-            nc.vector.tensor_tensor(
-                hg[:].rearrange("p (s j) -> p s j", j=PACK),
-                a_ps[c][:].rearrange("p (j s) -> p s j", j=PACK),
-                gate[c][:].rearrange("p (s j) -> p s j", j=PACK),
-                MULT,
-            )
+            ht = ring.tile([P, H], BF16, name="ht", align_bytes=64)
+            nc.vector.tensor_tensor(ht[:], a_ps[c][:], gate[c][:], MULT)
+            words = ht[:].bitcast(F32)
+            xt = psum.tile([P, 2, P], F32, tag="bank", name="xt%d" % c)
+            for u in range(2):
+                nc.tensor.transpose(xt[:, u, :], words[:, u : H // 2 : 2], ident[:])
+            hg = keep.tile([P, P, PACK], BF16, name="hg%d" % c, tag="grouped%d" % c, align_bytes=64)
+            nc.scalar.copy(hg[:].bitcast(F32), xt[:].rearrange("p u j -> p j u"))
             grouped.append(hg)
-            if c > 0:
-                quantize_h(c - 1)
-        quantize_h(QCHUNKS - 1)
+        gather_key_words(0, 1, "gate3")
+        for c in range(QCHUNKS):
+            cols = slice(c * P, (c + 1) * P)
+            nc.vector.quantize_mx(
+                out=hc[:, cols].bitcast(FP8X4), scales=hs[:, cols], in_=grouped[c][:].rearrange("p j t -> p (j t)")
+            )
 
         tiles_per_piece = KEY_PIECE // P
-        for g in range(KEY_PIECES):
-            gather_key_words(g)
+        gather_key_words(1, 2, "grouped3")
         for i in range(KEY_TILES):
             g, cols = i // tiles_per_piece, slice((i % tiles_per_piece) * P, (i % tiles_per_piece + 1) * P)
             z = psum.tile([P, S], F32, tag="bank", name="z%d" % i)
@@ -246,5 +236,5 @@ def tile_list_paged_softcap_logits_kernel(
             for part in range(parts):
                 js = slice(part * S // parts, (part + 1) * S // parts)
                 nc.scalar.activation(sig[:, js], z[:, js], SIGMOID, scale=2.0 / CAP)
-                (nc.gpsimd if i < POOL_TILES else nc.vector).tensor_scalar(res[:, js], sig[:, js], 2.0 * CAP, -CAP, MULT, ADD)
+                nc.vector.tensor_scalar(res[:, js], sig[:, js], 2.0 * CAP, -CAP, MULT, ADD)
                 nc.sync.dma_start(out=out[i * P : (i + 1) * P, js], in_=res[:, js])

@@ -26,11 +26,11 @@ QCHUNKS = S // P
 KEY_TILES = S2 // P
 KEY_PIECE = 512
 KEY_PIECES = S2 // KEY_PIECE
-KEY_PLANE_ROW = 12
+KEY_PLANE_ROW = 8
+TABLE_SPREAD_ROW = 4
+KEY_SPREAD_ROW = 5
 CODE_SLOTS = ("wc0", "tw0", "tw1")
-PLANE_SLOTS = ("ts", "ws1", "ws2")
 SCALAR_COLS = (512, 512, 512)
-MOVED_ROWS = 112
 
 
 def tile_list_paged_softcap_logits_kernel(
@@ -44,9 +44,11 @@ def tile_list_paged_softcap_logits_kernel(
 
         lst = keep.tile([P, S // 16], U16, name="lst")
         lst2 = keep.tile([P, S2 // 16], U16, name="lst2")
-        ts = keep.tile([P, T], U8, name="ts", tag="ts", align_bytes=64)
-        vs = keep.tile([P, S], U8, name="vs", align_bytes=64)
-        vs_low = keep.tile([P, PASSES - 1, S], U8, name="vs_low", align_bytes=64)
+        ts = keep.tile([P, PASSES * T], U8, name="ts", align_bytes=64)
+        vg = keep.tile([P, PASSES * S], U8, name="vg", align_bytes=64)
+        vs = keep.tile([P, PASSES * S], U8, name="vs", align_bytes=64)
+        kg = keep.tile([P, S2], U8, name="kg", align_bytes=64)
+        ks = keep.tile([P, S2], U8, name="ks", align_bytes=64)
         t2s = keep.tile([P, T2], U8, name="t2s", align_bytes=64)
         wgs = keep.tile([P, PASSES * H], U8, name="wgs", align_bytes=64)
         tw, raw, kw = {}, {}, {}
@@ -54,13 +56,14 @@ def tile_list_paged_softcap_logits_kernel(
         warm_in = keep.tile([P, 1], F32, name="warm_in")
         warm_out = keep.tile([P, 1], F32, name="warm_out")
 
-        half = T2 // 8
-        nc.vector.memset(t2s[:].bitcast(I32)[:, :half], 0)
-        nc.gpsimd.memset(t2s[:].bitcast(I32)[:, half:], 0)
+        half = PASSES * T // 8
+        nc.vector.memset(ts[:].bitcast(I32)[:, :half], 0)
+        nc.gpsimd.memset(ts[:].bitcast(I32)[:, half:], 0)
         nc.vector.memset(warm_in[:], 0.0)
-        nc.vector.memset(ts[:].bitcast(I32), 0)
+        nc.vector.memset(t2s[:].bitcast(I32), 0)
         nc.vector.memset(wgs[:].bitcast(I32), 0)
-        nc.vector.memset(vs_low[:].bitcast(I32), 0)
+        nc.vector.memset(vs[:].bitcast(I32), 0)
+        nc.vector.memset(ks[:].bitcast(I32), 0)
 
         def load_table_words(a):
             tw[a] = keep.tile([P, T], I32, name="tw%d" % a, tag="tw%d" % a, align_bytes=64)
@@ -88,46 +91,42 @@ def tile_list_paged_softcap_logits_kernel(
                     vw[a][:, part * width : (part + 1) * width], tw[a][:].bitcast(U32).indirect(offsets)
                 )
 
-        def lower_scale_rows(a):
-            nc.sync.dma_start(
-                out=vs_low[0:MOVED_ROWS, a - 1, :].bitcast(I32), in_=vs[4 * a : 4 * a + MOVED_ROWS, :].bitcast(I32)
-            )
+        def spread_scale_rows(window, scales, first):
+            passes = scales.shape[0]
+            dst = window[:].bitcast(I32).rearrange("p (a t) -> p a t", a=passes)
+            nc.sync.dma_start(out=dst[first:P:8], in_=scales.rearrange("a q t -> q a t").bitcast(I32))
+
+        def place_scale_rows(plane, first_row, picked, first):
+            for r in range(4):
+                nc.sync.dma_start(
+                    out=plane[first_row + r : P : 32, :].bitcast(I32), in_=picked[first + 8 * r : P : 32, :].bitcast(I32)
+                )
 
         wgw = keep.tile([P, PASSES, 2 * H], U8, name="wgw", align_bytes=64)
         nc.sync.dma_start(lst[:], offs)
-        nc.sync.dma_start(lst2[:], offs2)
         nc.sync.dma_start(out=wgw[:].bitcast(I32), in_=wg_words.rearrange("a p c -> p a c").bitcast(I32))
-        load_scale_rows(nc.sync, t2s, tab2_scales, KEY_PLANE_ROW)
+        nc.sync.dma_start(lst2[:], offs2)
+        spread_scale_rows(ts, tab_scales, TABLE_SPREAD_ROW)
         nc.scalar.activation(warm_out[:], warm_in[:], SIGMOID)
         load_wq(0)
+        spread_scale_rows(t2s, tab2_scales, KEY_SPREAD_ROW)
         load_wq(1)
-        for q in range(4):
-            nc.sync.dma_start(
-                out=ts[32 * q : 32 * q + 4 * PASSES, :].bitcast(I32), in_=tab_scales[:, 4 * q : 4 * q + 4, :].bitcast(I32)
-            )
-        load_table_words(0)
         load_scale_rows(nc.sync, wgs, wg_scales, 0)
+        load_table_words(0)
+        for a in range(PASSES):
+            nc.vector.tensor_copy(vg[:, a * S : (a + 1) * S], ts[:, a * T : (a + 1) * T].indirect(lst[:]))
+        place_scale_rows(vs, 0, vg, TABLE_SPREAD_ROW)
         load_wq(2)
-        nc.vector.tensor_copy(vs[:], ts[:].indirect(lst[:]))
-        lower_scale_rows(1)
-        lower_scale_rows(2)
         load_table_words(1)
         load_table_words(2)
+        nc.vector.tensor_copy(kg[:], t2s[:].indirect(lst2[:]))
+        place_scale_rows(ks, KEY_PLANE_ROW, kg, KEY_SPREAD_ROW)
         make_identity(nc, ident[:])
 
-        ks = {}
         wb = [keep.tile([P, H, PACK], BF16, name="wb%d" % a, tag="wb%d" % a, align_bytes=64) for a in range(PASSES)]
         wc, ws = {}, {}
         hc = keep.tile([P, S], U32, name="hc", align_bytes=64)
         hs = keep.tile([P, S], U8, name="hs", align_bytes=64)
-
-        def piece(g):
-            cols = KEY_PIECE // 16
-            return lst2[:, g * cols : (g + 1) * cols]
-
-        def gather_key_scales(g):
-            ks[g] = keep.tile([P, KEY_PIECE], U8, name="ks%d" % g, align_bytes=64)
-            nc.vector.tensor_copy(ks[g][:], t2s[:].indirect(piece(g)))
 
         def gather_key_words(first, count, slot):
             run = keep.tile([P, count * KEY_PIECE], U32, name="kw%d" % first, tag=slot, align_bytes=64)
@@ -146,7 +145,7 @@ def tile_list_paged_softcap_logits_kernel(
 
         def quantize_wq(a):
             wc[a] = keep.tile([P, H], U32, name="wc%d" % a, tag=CODE_SLOTS[a], align_bytes=64)
-            ws[a] = keep.tile([P, H], U8, name="ws%d" % a, tag=PLANE_SLOTS[a], align_bytes=64)
+            ws[a] = keep.tile([P, H], U8, name="ws%d" % a, align_bytes=64)
             nc.vector.quantize_mx(
                 out=wc[a][:].bitcast(FP8X4), scales=ws[a][:], in_=wb[a][:].rearrange("p c t -> p (c t)")
             )
@@ -168,18 +167,16 @@ def tile_list_paged_softcap_logits_kernel(
                 )
 
         def gate_pass(a, chunks):
-            project(b_ps, a, vs[:] if a == 0 else vs_low[:, a - 1, :], wgw[:, a, :].bitcast(FP4X4), wgs[:, a * H : (a + 1) * H], chunks)
+            project(b_ps, a, vs[:, a * S : (a + 1) * S], wgw[:, a, :].bitcast(FP4X4), wgs[:, a * H : (a + 1) * H], chunks)
 
         def query_pass(a, chunks):
-            project(a_ps, a, vs[4 * a : P, :], wc[a][:].bitcast(FP8X4), ws[a][:], chunks)
+            project(a_ps, a, vs[:, a * S : (a + 1) * S], wc[a][:].bitcast(FP8X4), ws[a][:], chunks)
 
         every_chunk = range(QCHUNKS)
-        for g in range(KEY_PIECES):
-            gather_key_scales(g)
         round_wq(0)
         quantize_wq(0)
         round_wq(1)
-        gather_words(0)
+        gather_words(0, parts=2)
         quantize_wq(1)
         gate_pass(0, every_chunk)
         query_pass(0, every_chunk)
@@ -193,10 +190,12 @@ def tile_list_paged_softcap_logits_kernel(
             query_pass(1, [c])
         gather_words(2, parts=2)
         gate = [keep.tile([P, H], F32, name="gate%d" % c, tag="gate%d" % c, align_bytes=64) for c in every_chunk]
-        for c in every_chunk:
-            gate_pass(2, [c])
-            nc.scalar.activation(gate[c][:], b_ps[c][:], SIGMOID)
-            query_pass(2, [c])
+        for c in range(QCHUNKS + 1):
+            if c < QCHUNKS:
+                gate_pass(2, [c])
+                nc.scalar.activation(gate[c][:], b_ps[c][:], SIGMOID)
+            if c > 0:
+                query_pass(2, [c - 1])
 
         grouped = []
         for c in range(QCHUNKS):
@@ -224,7 +223,7 @@ def tile_list_paged_softcap_logits_kernel(
             nc.tensor.matmul_mx(
                 out=z[:],
                 lhsT=kw[g][:, cols].bitcast(FP8X4),
-                lhsT_scale=ks[g][KEY_PLANE_ROW:P, cols],
+                lhsT_scale=ks[KEY_PLANE_ROW:P, i * P : (i + 1) * P],
                 rhs=hc[:].bitcast(FP8X4),
                 rhs_scale=hs[:],
                 start=True,

@@ -16,6 +16,7 @@ U8 = mybir.dt.uint8
 FP8X4 = mybir.dt.float8_e4m3fn_x4
 FP4X4 = mybir.dt.float4_e2m1fn_x4
 SIGMOID = mybir.ActivationFunctionType.Sigmoid
+COPY = mybir.ActivationFunctionType.Copy
 MULT = mybir.AluOpType.mult
 ADD = mybir.AluOpType.add
 
@@ -29,8 +30,9 @@ KEY_PIECES = S2 // KEY_PIECE
 KEY_PLANE_ROW = 8
 TABLE_SPREAD_ROW = 4
 KEY_SPREAD_ROW = 5
-CODE_SLOTS = ("wc0", "tw0", "tw1")
-SCALAR_COLS = (512, 512, 512)
+LATE_TILE = 2
+CODE_SLOTS = ("wc0", "tw0", "wc2")
+SCALAR_COLS = (512, 512, 192)
 
 
 def tile_list_paged_softcap_logits_kernel(
@@ -47,7 +49,7 @@ def tile_list_paged_softcap_logits_kernel(
         ts = keep.tile([P, PASSES * T], U8, name="ts", align_bytes=64)
         vg = keep.tile([P, PASSES * S], U8, name="vg", align_bytes=64)
         vs = keep.tile([P, PASSES * S], U8, name="vs", align_bytes=64)
-        kg = keep.tile([P, S2], U8, name="kg", align_bytes=64)
+        kg = keep.tile([P, S2], U8, name="kg", tag="kg", align_bytes=64)
         ks = keep.tile([P, S2], U8, name="ks", align_bytes=64)
         t2s = keep.tile([P, T2], U8, name="t2s", align_bytes=64)
         wgs = keep.tile([P, PASSES * H], U8, name="wgs", align_bytes=64)
@@ -56,9 +58,9 @@ def tile_list_paged_softcap_logits_kernel(
         warm_in = keep.tile([P, 1], F32, name="warm_in")
         warm_out = keep.tile([P, 1], F32, name="warm_out")
 
-        half = PASSES * T // 8
-        nc.vector.memset(ts[:].bitcast(I32)[:, :half], 0)
-        nc.gpsimd.memset(ts[:].bitcast(I32)[:, half:], 0)
+        split = PASSES * T // 8
+        nc.vector.memset(ts[:].bitcast(I32)[:, :split], 0)
+        nc.gpsimd.memset(ts[:].bitcast(I32)[:, split:], 0)
         nc.vector.memset(warm_in[:], 0.0)
         nc.vector.memset(t2s[:].bitcast(I32), 0)
         nc.vector.memset(wgs[:].bitcast(I32), 0)
@@ -116,9 +118,11 @@ def tile_list_paged_softcap_logits_kernel(
         for a in range(PASSES):
             nc.vector.tensor_copy(vg[:, a * S : (a + 1) * S], ts[:, a * T : (a + 1) * T].indirect(lst[:]))
         place_scale_rows(vs, 0, vg, TABLE_SPREAD_ROW)
-        load_wq(2)
         load_table_words(1)
+        load_wq(2)
         load_table_words(2)
+        t2w = keep.tile([P, T2], I32, name="t2w", align_bytes=64)
+        nc.sync.dma_start(out=t2w[:], in_=tab2_words[0].rearrange("p t i -> p (t i)").bitcast(I32))
         nc.vector.tensor_copy(kg[:], t2s[:].indirect(lst2[:]))
         place_scale_rows(ks, KEY_PLANE_ROW, kg, KEY_SPREAD_ROW)
         make_identity(nc, ident[:])
@@ -126,7 +130,7 @@ def tile_list_paged_softcap_logits_kernel(
         wb = [keep.tile([P, H, PACK], BF16, name="wb%d" % a, tag="wb%d" % a, align_bytes=64) for a in range(PASSES)]
         wc, ws = {}, {}
         hc = keep.tile([P, S], U32, name="hc", align_bytes=64)
-        hs = keep.tile([P, S], U8, name="hs", align_bytes=64)
+        hs = keep.tile([P, S], U8, name="hs", tag="kg", align_bytes=64)
 
         def gather_key_words(first, count, slot):
             run = keep.tile([P, count * KEY_PIECE], U32, name="kw%d" % first, tag=slot, align_bytes=64)
@@ -180,14 +184,12 @@ def tile_list_paged_softcap_logits_kernel(
         quantize_wq(1)
         gate_pass(0, every_chunk)
         query_pass(0, every_chunk)
-        round_wq(2)
-        t2w = keep.tile([P, T2], I32, name="t2w", tag="raw2", align_bytes=64)
-        nc.scalar.dma_start(out=t2w[:], in_=tab2_words[0].rearrange("p t i -> p (t i)").bitcast(I32))
         gather_words(1, parts=2)
-        quantize_wq(2)
         for c in every_chunk:
             gate_pass(1, [c])
             query_pass(1, [c])
+        round_wq(2)
+        quantize_wq(2)
         gather_words(2, parts=2)
         gate = [keep.tile([P, H], F32, name="gate%d" % c, tag="gate%d" % c, align_bytes=64) for c in every_chunk]
         for c in range(QCHUNKS + 1):
@@ -197,43 +199,67 @@ def tile_list_paged_softcap_logits_kernel(
             if c > 0:
                 query_pass(2, [c - 1])
 
-        grouped = []
-        for c in range(QCHUNKS):
-            ht = ring.tile([P, H], BF16, name="ht", align_bytes=64)
-            nc.vector.tensor_tensor(ht[:], a_ps[c][:], gate[c][:], MULT)
-            words = ht[:].bitcast(F32)
-            xt = psum.tile([P, 2, P], F32, tag="bank", name="xt%d" % c)
-            for u in range(2):
-                nc.tensor.transpose(xt[:, u, :], words[:, u : H // 2 : 2], ident[:])
-            hg = keep.tile([P, P, PACK], BF16, name="hg%d" % c, tag="grouped%d" % c, align_bytes=64)
-            nc.scalar.copy(hg[:].bitcast(F32), xt[:].rearrange("p u j -> p j u"))
-            grouped.append(hg)
-        gather_key_words(0, 1, "gate3")
-        for c in range(QCHUNKS):
-            cols = slice(c * P, (c + 1) * P)
-            nc.vector.quantize_mx(
-                out=hc[:, cols].bitcast(FP8X4), scales=hs[:, cols], in_=grouped[c][:].rearrange("p j t -> p (j t)")
+        half = S // 2
+
+        def turn_pair(n):
+            xt = psum.tile([P, 2, 2, P], F32, tag="bank", name="xt%d" % n)
+            for c in range(2):
+                ht = ring.tile([P, H], BF16, name="ht", align_bytes=64)
+                nc.vector.tensor_tensor(ht[:], a_ps[2 * n + c][:], gate[2 * n + c][:], MULT)
+                words = ht[:].bitcast(F32)
+                for u in range(2):
+                    nc.tensor.transpose(xt[:, c, u, :], words[:, u : H // 2 : 2], ident[:])
+            return xt
+
+        def quantize_pair(n, xt):
+            hg = keep.tile([P, half * PACK], BF16, name="hg%d" % n, tag="grouped%d" % n, align_bytes=64)
+            nc.scalar.copy(
+                hg[:].bitcast(F32).rearrange("p (c j u) -> p c j u", c=2, u=2), xt[:].rearrange("p c u j -> p c j u")
             )
+            cols = slice(n * half, (n + 1) * half)
+            nc.vector.quantize_mx(out=hc[:, cols].bitcast(FP8X4), scales=hs[:, cols], in_=hg[:])
+
+        turned = [turn_pair(n) for n in range(2)]
+        gather_key_words(0, 1, "kw0")
+        quantize_pair(0, turned[0])
+        quantize_pair(1, turned[1])
+        gather_key_words(1, 1, "grouped0")
 
         tiles_per_piece = KEY_PIECE // P
-        gather_key_words(1, 2, "grouped3")
         for i in range(KEY_TILES):
             g, cols = i // tiles_per_piece, slice((i % tiles_per_piece) * P, (i % tiles_per_piece + 1) * P)
-            z = psum.tile([P, S], F32, tag="bank", name="z%d" % i)
-            nc.tensor.matmul_mx(
-                out=z[:],
-                lhsT=kw[g][:, cols].bitcast(FP8X4),
-                lhsT_scale=ks[KEY_PLANE_ROW:P, i * P : (i + 1) * P],
-                rhs=hc[:].bitcast(FP8X4),
-                rhs_scale=hs[:],
-                start=True,
-                stop=True,
-            )
-            sig = keep.tile([P, S], F32, name="sig%d" % i, align_bytes=64)
+            if i == LATE_TILE + 1:
+                gather_key_words(2, 1, "sig%d" % LATE_TILE)
+
+            def logits(js):
+                z = psum.tile([P, js.stop - js.start], F32, tag="bank", name="z")
+                nc.tensor.matmul_mx(
+                    out=z[:],
+                    lhsT=kw[g][:, cols].bitcast(FP8X4),
+                    lhsT_scale=ks[KEY_PLANE_ROW:P, i * P : (i + 1) * P],
+                    rhs=hc[:, js].bitcast(FP8X4),
+                    rhs_scale=hs[:, js],
+                    start=True,
+                    stop=True,
+                )
+                return z
+
+            sig = keep.tile([P, S], F32, name="sig%d" % i, tag="sig%d" % i, align_bytes=64)
             res = keep.tile([P, S], F32, name="res%d" % i)
+            if i == 0:
+                for n in range(2):
+                    js = slice(n * half, (n + 1) * half)
+                    nc.scalar.activation(sig[:, js], logits(js)[:], SIGMOID, scale=2.0 / CAP)
+                nc.vector.tensor_scalar(res[:], sig[:], 2.0 * CAP, -CAP, MULT, ADD)
+                nc.sync.dma_start(out=out[0:P, :], in_=res[:])
+                continue
+            z = logits(slice(0, S))
             parts = 2 if i == KEY_TILES - 1 else 1
             for part in range(parts):
                 js = slice(part * S // parts, (part + 1) * S // parts)
                 nc.scalar.activation(sig[:, js], z[:, js], SIGMOID, scale=2.0 / CAP)
-                nc.vector.tensor_scalar(res[:, js], sig[:, js], 2.0 * CAP, -CAP, MULT, ADD)
+                if i == LATE_TILE + 1:
+                    nc.scalar.activation(res[:, js], sig[:, js], COPY, scale=2.0 * CAP, bias=-CAP)
+                else:
+                    nc.vector.tensor_scalar(res[:, js], sig[:, js], 2.0 * CAP, -CAP, MULT, ADD)
                 nc.sync.dma_start(out=out[i * P : (i + 1) * P, js], in_=res[:, js])

@@ -31,8 +31,8 @@ KEY_PLANE_ROW = 8
 TABLE_SPREAD_ROW = 4
 KEY_SPREAD_ROW = 5
 LATE_TILE = 2
-CODE_SLOTS = ("wc0", "tw0", "wc2")
-SCALAR_COLS = (512, 512, 192)
+CODE_SLOTS = ("tw0", "wb0", "wc2")
+SCALAR_COLS = (512, 512, 256)
 
 
 def tile_list_paged_softcap_logits_kernel(
@@ -62,8 +62,8 @@ def tile_list_paged_softcap_logits_kernel(
         nc.vector.memset(ts[:].bitcast(I32)[:, :split], 0)
         nc.gpsimd.memset(ts[:].bitcast(I32)[:, split:], 0)
         nc.vector.memset(warm_in[:], 0.0)
-        nc.vector.memset(t2s[:].bitcast(I32), 0)
         nc.vector.memset(wgs[:].bitcast(I32), 0)
+        nc.vector.memset(t2s[:].bitcast(I32), 0)
         nc.vector.memset(vs[:].bitcast(I32), 0)
         nc.vector.memset(ks[:].bitcast(I32), 0)
 
@@ -107,13 +107,13 @@ def tile_list_paged_softcap_logits_kernel(
         wgw = keep.tile([P, PASSES, 2 * H], U8, name="wgw", align_bytes=64)
         nc.sync.dma_start(lst[:], offs)
         nc.sync.dma_start(out=wgw[:].bitcast(I32), in_=wg_words.rearrange("a p c -> p a c").bitcast(I32))
-        nc.sync.dma_start(lst2[:], offs2)
         spread_scale_rows(ts, tab_scales, TABLE_SPREAD_ROW)
         nc.scalar.activation(warm_out[:], warm_in[:], SIGMOID)
         load_wq(0)
+        load_scale_rows(nc.sync, wgs, wg_scales, 0)
+        nc.sync.dma_start(lst2[:], offs2)
         spread_scale_rows(t2s, tab2_scales, KEY_SPREAD_ROW)
         load_wq(1)
-        load_scale_rows(nc.sync, wgs, wg_scales, 0)
         load_table_words(0)
         for a in range(PASSES):
             nc.vector.tensor_copy(vg[:, a * S : (a + 1) * S], ts[:, a * T : (a + 1) * T].indirect(lst[:]))
@@ -178,9 +178,9 @@ def tile_list_paged_softcap_logits_kernel(
 
         every_chunk = range(QCHUNKS)
         round_wq(0)
-        quantize_wq(0)
         round_wq(1)
         gather_words(0, parts=2)
+        quantize_wq(0)
         quantize_wq(1)
         gate_pass(0, every_chunk)
         query_pass(0, every_chunk)
@@ -254,12 +254,9 @@ def tile_list_paged_softcap_logits_kernel(
                 nc.sync.dma_start(out=out[0:P, :], in_=res[:])
                 continue
             z = logits(slice(0, S))
-            parts = 2 if i == KEY_TILES - 1 else 1
-            for part in range(parts):
-                js = slice(part * S // parts, (part + 1) * S // parts)
-                nc.scalar.activation(sig[:, js], z[:, js], SIGMOID, scale=2.0 / CAP)
-                if i == LATE_TILE + 1:
-                    nc.scalar.activation(res[:, js], sig[:, js], COPY, scale=2.0 * CAP, bias=-CAP)
-                else:
-                    nc.vector.tensor_scalar(res[:, js], sig[:, js], 2.0 * CAP, -CAP, MULT, ADD)
-                nc.sync.dma_start(out=out[i * P : (i + 1) * P, js], in_=res[:, js])
+            nc.scalar.activation(sig[:], z[:], SIGMOID, scale=2.0 / CAP)
+            if i == LATE_TILE + 1:
+                nc.scalar.activation(res[:], sig[:], COPY, scale=2.0 * CAP, bias=-CAP)
+            else:
+                nc.vector.tensor_scalar(res[:], sig[:], 2.0 * CAP, -CAP, MULT, ADD)
+            nc.sync.dma_start(out=out[i * P : (i + 1) * P, :], in_=res[:])

@@ -16,7 +16,6 @@ U8 = mybir.dt.uint8
 FP8X4 = mybir.dt.float8_e4m3fn_x4
 FP4X4 = mybir.dt.float4_e2m1fn_x4
 SIGMOID = mybir.ActivationFunctionType.Sigmoid
-COPY = mybir.ActivationFunctionType.Copy
 MULT = mybir.AluOpType.mult
 ADD = mybir.AluOpType.add
 
@@ -104,9 +103,10 @@ def tile_list_paged_softcap_logits_kernel(
                     out=plane[first_row + r : P : 32, :].bitcast(I32), in_=picked[first + 8 * r : P : 32, :].bitcast(I32)
                 )
 
-        wgw = keep.tile([P, PASSES, 2 * H], U8, name="wgw", align_bytes=64)
+        wgw = keep.tile([P, PASSES - 1, 2 * H], U8, name="wgw", align_bytes=64)
+        wgw_last = keep.tile([P, 2 * H], U8, name="wgw_last", align_bytes=64)
         nc.sync.dma_start(lst[:], offs)
-        nc.sync.dma_start(out=wgw[:].bitcast(I32), in_=wg_words.rearrange("a p c -> p a c").bitcast(I32))
+        nc.sync.dma_start(out=wgw[:].bitcast(I32), in_=wg_words[: PASSES - 1].rearrange("a p c -> p a c").bitcast(I32))
         spread_scale_rows(ts, tab_scales, TABLE_SPREAD_ROW)
         nc.scalar.activation(warm_out[:], warm_in[:], SIGMOID)
         load_wq(0)
@@ -121,6 +121,7 @@ def tile_list_paged_softcap_logits_kernel(
         load_table_words(1)
         load_wq(2)
         load_table_words(2)
+        nc.sync.dma_start(out=wgw_last[:].bitcast(I32), in_=wg_words[PASSES - 1].bitcast(I32))
         t2w = keep.tile([P, T2], I32, name="t2w", align_bytes=64)
         nc.sync.dma_start(out=t2w[:], in_=tab2_words[0].rearrange("p t i -> p (t i)").bitcast(I32))
         nc.vector.tensor_copy(kg[:], t2s[:].indirect(lst2[:]))
@@ -171,7 +172,7 @@ def tile_list_paged_softcap_logits_kernel(
                 )
 
         def gate_pass(a, chunks):
-            project(b_ps, a, vs[:, a * S : (a + 1) * S], wgw[:, a, :].bitcast(FP4X4), wgs[:, a * H : (a + 1) * H], chunks)
+            project(b_ps, a, vs[:, a * S : (a + 1) * S], (wgw_last[:] if a == PASSES - 1 else wgw[:, a, :]).bitcast(FP4X4), wgs[:, a * H : (a + 1) * H], chunks)
 
         def query_pass(a, chunks):
             project(a_ps, a, vs[:, a * S : (a + 1) * S], wc[a][:].bitcast(FP8X4), ws[a][:], chunks)
@@ -256,7 +257,7 @@ def tile_list_paged_softcap_logits_kernel(
             z = logits(slice(0, S))
             nc.scalar.activation(sig[:], z[:], SIGMOID, scale=2.0 / CAP)
             if i == LATE_TILE + 1:
-                nc.scalar.activation(res[:], sig[:], COPY, scale=2.0 * CAP, bias=-CAP)
+                nc.gpsimd.tensor_scalar(res[:], sig[:], 2.0 * CAP, -CAP, MULT, ADD)
             else:
                 nc.vector.tensor_scalar(res[:], sig[:], 2.0 * CAP, -CAP, MULT, ADD)
             nc.sync.dma_start(out=out[i * P : (i + 1) * P, :], in_=res[:])

@@ -21,17 +21,23 @@ ADD = mybir.AluOpType.add
 
 P = 128
 PACK = 4
+QUADRANT = 32
+SCALE_ROWS = 4
+SPREAD = 8
+LIST_ROWS = 16
 PASSES = K // (P * PACK)
-QCHUNKS = S // P
+LAST = PASSES - 1
+CHUNKS = S // P
+HALF = S // 2
 KEY_TILES = S2 // P
 KEY_PIECE = 512
-KEY_PIECES = S2 // KEY_PIECE
-KEY_PLANE_ROW = 8
+TILES_PER_PIECE = KEY_PIECE // P
 TABLE_SPREAD_ROW = 4
 KEY_SPREAD_ROW = 5
-LATE_TILE = 2
-CODE_SLOTS = ("tw0", "wb0", "wc2")
-SCALAR_COLS = (512, 512, 256)
+KEY_PLANE_ROW = 8
+VECTOR_CLEARS = PASSES * T // 6
+SCALAR_COLS = (H, H, H // 2)
+LAST_GATHER_AFTER = 2
 
 
 def tile_list_paged_softcap_logits_kernel(
@@ -40,224 +46,222 @@ def tile_list_paged_softcap_logits_kernel(
     nc = tc.nc
     with ExitStack() as ctx:
         keep = ctx.enter_context(tc.tile_pool(name="keep", bufs=1))
-        ring = ctx.enter_context(tc.tile_pool(name="ring", bufs=4))
+        ring = ctx.enter_context(tc.tile_pool(name="ring", bufs=CHUNKS))
         psum = ctx.enter_context(tc.psum_pool(name="psum", bufs=8))
 
-        lst = keep.tile([P, S // 16], U16, name="lst")
-        lst2 = keep.tile([P, S2 // 16], U16, name="lst2")
-        ts = keep.tile([P, PASSES * T], U8, name="ts", align_bytes=64)
-        vg = keep.tile([P, PASSES * S], U8, name="vg", align_bytes=64)
-        vs = keep.tile([P, PASSES * S], U8, name="vs", align_bytes=64)
-        kg = keep.tile([P, S2], U8, name="kg", tag="kg", align_bytes=64)
-        ks = keep.tile([P, S2], U8, name="ks", align_bytes=64)
-        t2s = keep.tile([P, T2], U8, name="t2s", align_bytes=64)
-        wgs = keep.tile([P, PASSES * H], U8, name="wgs", align_bytes=64)
-        tw, raw, kw = {}, {}, {}
+        token_list = keep.tile([P, S // LIST_ROWS], U16, name="token_list")
+        key_list = keep.tile([P, S2 // LIST_ROWS], U16, name="key_list")
+        v_window = keep.tile([P, PASSES * T], U8, name="v_window", align_bytes=64)
+        v_picked = keep.tile([P, PASSES * S], U8, name="v_picked", align_bytes=64)
+        v_plane = keep.tile([P, PASSES * S], U8, name="v_plane", align_bytes=64)
+        key_picked = keep.tile([P, S2], U8, name="key_picked", tag="key_picked", align_bytes=64)
+        key_plane = keep.tile([P, S2], U8, name="key_plane", align_bytes=64)
+        key_window = keep.tile([P, T2], U8, name="key_window", align_bytes=64)
+        wg_plane = keep.tile([P, PASSES * H], U8, name="wg_plane", align_bytes=64)
+        table_words, wq_raw, key_words = {}, {}, {}
         ident = keep.tile([P, P], F32, name="ident", align_bytes=64)
-        warm_in = keep.tile([P, 1], F32, name="warm_in")
-        warm_out = keep.tile([P, 1], F32, name="warm_out")
+        zero = keep.tile([P, 1], F32, name="zero")
+        centre = keep.tile([P, 1], F32, name="centre")
 
-        split = PASSES * T // 8
-        nc.vector.memset(ts[:].bitcast(I32)[:, :split], 0)
-        nc.gpsimd.memset(ts[:].bitcast(I32)[:, split:], 0)
-        nc.vector.memset(warm_in[:], 0.0)
-        nc.vector.memset(wgs[:].bitcast(I32), 0)
-        nc.vector.memset(t2s[:].bitcast(I32), 0)
-        nc.vector.memset(vs[:].bitcast(I32), 0)
-        nc.vector.memset(ks[:].bitcast(I32), 0)
+        nc.gpsimd.memset(wg_plane[:].bitcast(I32), 0)
+        nc.vector.memset(v_window[:].bitcast(I32)[:, :VECTOR_CLEARS], 0)
+        nc.gpsimd.memset(v_window[:].bitcast(I32)[:, VECTOR_CLEARS:], 0)
+        nc.vector.memset(zero[:], 0.0)
+        nc.vector.memset(key_window[:].bitcast(I32), 0)
+        nc.vector.memset(v_plane[:].bitcast(I32), 0)
+        nc.vector.memset(key_plane[:].bitcast(I32), 0)
 
         def load_table_words(a):
-            tw[a] = keep.tile([P, T], I32, name="tw%d" % a, tag="tw%d" % a, align_bytes=64)
-            nc.sync.dma_start(out=tw[a][:], in_=tab_words[a].rearrange("p t i -> p (t i)").bitcast(I32))
+            table_words[a] = keep.tile([P, T], I32, name="table_words%d" % a, tag="table_words%d" % a, align_bytes=64)
+            nc.sync.dma_start(out=table_words[a][:], in_=tab_words[a].rearrange("p t i -> p (t i)").bitcast(I32))
 
         def load_wq(a):
-            raw[a] = keep.tile([P, PACK, H], F32, name="raw%d" % a, tag="raw%d" % a, align_bytes=64)
+            wq_raw[a] = keep.tile([P, PACK, H], F32, name="wq_raw%d" % a, align_bytes=64)
             rows = wq[a * P * PACK : (a + 1) * P * PACK, :]
-            nc.sync.dma_start(out=raw[a][:], in_=rows.rearrange("(p j) c -> p j c", j=PACK))
+            nc.sync.dma_start(out=wq_raw[a][:], in_=rows.rearrange("(p j) c -> p j c", j=PACK))
 
-        def load_scale_rows(queue, plane, scales, first_row):
-            passes = scales.shape[0]
-            by_row = scales.rearrange("a (q r) t -> r q a t", r=4)
-            dst = plane[:].bitcast(I32).rearrange("p (a t) -> p a t", a=passes)
-            for r in range(4):
-                queue.dma_start(out=dst[first_row + r : P : 32], in_=by_row[r].bitcast(I32))
+        def load_gate_plane():
+            by_row = wg_scales.rearrange("a (q r) t -> r q a t", r=SCALE_ROWS)
+            dst = wg_plane[:].bitcast(I32).rearrange("p (a t) -> p a t", a=PASSES)
+            for r in range(SCALE_ROWS):
+                nc.sync.dma_start(out=dst[r:P:QUADRANT], in_=by_row[r].bitcast(I32))
 
-        vw = [keep.tile([P, S], U32, name="vw%d" % a, tag="words%d" % a, align_bytes=64) for a in range(PASSES)]
+        v_words = [keep.tile([P, S], U32, name="v_words%d" % a, align_bytes=64) for a in range(PASSES)]
 
-        def gather_words(a, parts=1):
-            width = S // parts
-            for part in range(parts):
-                offsets = lst[:, part * width // 16 : (part + 1) * width // 16]
+        def gather_table_words(a):
+            for n in range(2):
+                offsets = token_list[:, n * HALF // LIST_ROWS : (n + 1) * HALF // LIST_ROWS]
                 nc.vector.tensor_copy(
-                    vw[a][:, part * width : (part + 1) * width], tw[a][:].bitcast(U32).indirect(offsets)
+                    v_words[a][:, n * HALF : (n + 1) * HALF], table_words[a][:].bitcast(U32).indirect(offsets)
                 )
 
         def spread_scale_rows(window, scales, first):
             passes = scales.shape[0]
             dst = window[:].bitcast(I32).rearrange("p (a t) -> p a t", a=passes)
-            nc.sync.dma_start(out=dst[first:P:8], in_=scales.rearrange("a q t -> q a t").bitcast(I32))
+            nc.sync.dma_start(out=dst[first:P:SPREAD], in_=scales.rearrange("a q t -> q a t").bitcast(I32))
 
         def place_scale_rows(plane, first_row, picked, first):
-            for r in range(4):
+            for r in range(SCALE_ROWS):
                 nc.sync.dma_start(
-                    out=plane[first_row + r : P : 32, :].bitcast(I32), in_=picked[first + 8 * r : P : 32, :].bitcast(I32)
+                    out=plane[first_row + r : P : QUADRANT, :].bitcast(I32),
+                    in_=picked[first + SPREAD * r : P : QUADRANT, :].bitcast(I32),
                 )
 
-        wgw = keep.tile([P, PASSES - 1, 2 * H], U8, name="wgw", align_bytes=64)
-        wgw_last = keep.tile([P, 2 * H], U8, name="wgw_last", align_bytes=64)
-        nc.sync.dma_start(lst[:], offs)
-        nc.sync.dma_start(out=wgw[:].bitcast(I32), in_=wg_words[: PASSES - 1].rearrange("a p c -> p a c").bitcast(I32))
-        spread_scale_rows(ts, tab_scales, TABLE_SPREAD_ROW)
-        nc.scalar.activation(warm_out[:], warm_in[:], SIGMOID)
+        wg_first = keep.tile([P, LAST, 2 * H], U8, name="wg_first", align_bytes=64)
+        wg_last = keep.tile([P, 2 * H], U8, name="wg_last", align_bytes=64)
+        nc.sync.dma_start(token_list[:], offs)
+        nc.sync.dma_start(out=wg_first[:].bitcast(I32), in_=wg_words[:LAST].rearrange("a p c -> p a c").bitcast(I32))
+        load_gate_plane()
+        spread_scale_rows(v_window, tab_scales, TABLE_SPREAD_ROW)
+        nc.scalar.activation(centre[:], zero[:], SIGMOID)
+        shift = keep.tile([P, 1], F32, name="shift")
+        nc.gpsimd.tensor_scalar(shift[:], centre[:], -2.0 * CAP, 0.0, MULT, ADD)
         load_wq(0)
-        load_scale_rows(nc.sync, wgs, wg_scales, 0)
-        nc.sync.dma_start(lst2[:], offs2)
-        spread_scale_rows(t2s, tab2_scales, KEY_SPREAD_ROW)
+        nc.sync.dma_start(key_list[:], offs2)
+        spread_scale_rows(key_window, tab2_scales, KEY_SPREAD_ROW)
         load_wq(1)
         load_table_words(0)
         for a in range(PASSES):
-            nc.vector.tensor_copy(vg[:, a * S : (a + 1) * S], ts[:, a * T : (a + 1) * T].indirect(lst[:]))
-        place_scale_rows(vs, 0, vg, TABLE_SPREAD_ROW)
+            nc.vector.tensor_copy(
+                v_picked[:, a * S : (a + 1) * S], v_window[:, a * T : (a + 1) * T].indirect(token_list[:])
+            )
+        place_scale_rows(v_plane, 0, v_picked, TABLE_SPREAD_ROW)
         load_table_words(1)
-        load_wq(2)
-        load_table_words(2)
-        nc.sync.dma_start(out=wgw_last[:].bitcast(I32), in_=wg_words[PASSES - 1].bitcast(I32))
-        t2w = keep.tile([P, T2], I32, name="t2w", align_bytes=64)
-        nc.sync.dma_start(out=t2w[:], in_=tab2_words[0].rearrange("p t i -> p (t i)").bitcast(I32))
-        nc.vector.tensor_copy(kg[:], t2s[:].indirect(lst2[:]))
-        place_scale_rows(ks, KEY_PLANE_ROW, kg, KEY_SPREAD_ROW)
+        load_wq(LAST)
+        load_table_words(LAST)
+        nc.sync.dma_start(out=wg_last[:].bitcast(I32), in_=wg_words[LAST].bitcast(I32))
+        key_table = keep.tile([P, T2], I32, name="key_table", align_bytes=64)
+        nc.sync.dma_start(out=key_table[:], in_=tab2_words[0].rearrange("p t i -> p (t i)").bitcast(I32))
+        nc.vector.tensor_copy(key_picked[:], key_window[:].indirect(key_list[:]))
+        place_scale_rows(key_plane, KEY_PLANE_ROW, key_picked, KEY_SPREAD_ROW)
         make_identity(nc, ident[:])
 
-        wb = [keep.tile([P, H, PACK], BF16, name="wb%d" % a, tag="wb%d" % a, align_bytes=64) for a in range(PASSES)]
-        wc, ws = {}, {}
-        hc = keep.tile([P, S], U32, name="hc", align_bytes=64)
-        hs = keep.tile([P, S], U8, name="hs", tag="kg", align_bytes=64)
+        wq_bf16 = [
+            keep.tile([P, H, PACK], BF16, name="wq_bf16_%d" % a, tag="wq_bf16_%d" % a, align_bytes=64)
+            for a in range(PASSES)
+        ]
+        wq_codes, wq_plane = {}, {}
+        h_codes = keep.tile([P, S], U32, name="h_codes", align_bytes=64)
+        h_plane = keep.tile([P, S], U8, name="h_plane", tag="key_picked", align_bytes=64)
 
-        def gather_key_words(first, count, slot):
-            run = keep.tile([P, count * KEY_PIECE], U32, name="kw%d" % first, tag=slot, align_bytes=64)
-            cols = KEY_PIECE // 16
-            nc.vector.tensor_copy(run[:], t2w[:].bitcast(U32).indirect(lst2[:, first * cols : (first + count) * cols]))
-            for n in range(count):
-                kw[first + n] = run[:, n * KEY_PIECE : (n + 1) * KEY_PIECE]
+        def gather_key_words(g, tag):
+            key_words[g] = keep.tile([P, KEY_PIECE], U32, name="key_words%d" % g, tag=tag, align_bytes=64)
+            cols = KEY_PIECE // LIST_ROWS
+            nc.vector.tensor_copy(
+                key_words[g][:], key_table[:].bitcast(U32).indirect(key_list[:, g * cols : (g + 1) * cols])
+            )
 
         def round_wq(a):
-            split = SCALAR_COLS[a]
-            src = raw[a][:].rearrange("p t (c i) -> p c t i", i=4)
-            dst = wb[a][:].rearrange("p (c i) t -> p c t i", i=4)
-            nc.scalar.copy(dst[:, : split // 4], src[:, : split // 4])
-            if split < H:
-                nc.vector.tensor_copy(dst[:, split // 4 :], src[:, split // 4 :])
+            groups = SCALAR_COLS[a] // 4
+            src = wq_raw[a][:].rearrange("p t (c i) -> p c t i", i=4)
+            dst = wq_bf16[a][:].rearrange("p (c i) t -> p c t i", i=4)
+            nc.scalar.copy(dst[:, :groups], src[:, :groups])
+            if SCALAR_COLS[a] < H:
+                nc.vector.tensor_copy(dst[:, groups:], src[:, groups:])
 
-        def quantize_wq(a):
-            wc[a] = keep.tile([P, H], U32, name="wc%d" % a, tag=CODE_SLOTS[a], align_bytes=64)
-            ws[a] = keep.tile([P, H], U8, name="ws%d" % a, align_bytes=64)
+        def quantize_wq(a, tag):
+            wq_codes[a] = keep.tile([P, H], U32, name="wq_codes%d" % a, tag=tag, align_bytes=64)
+            wq_plane[a] = keep.tile([P, H], U8, name="wq_plane%d" % a, align_bytes=64)
             nc.vector.quantize_mx(
-                out=wc[a][:].bitcast(FP8X4), scales=ws[a][:], in_=wb[a][:].rearrange("p c t -> p (c t)")
+                out=wq_codes[a][:].bitcast(FP8X4), scales=wq_plane[a][:], in_=wq_bf16[a][:].rearrange("p c t -> p (c t)")
             )
 
-        b_ps = [psum.tile([P, H], F32, tag="bank", name="b_ps%d" % c) for c in range(QCHUNKS)]
-        a_ps = [psum.tile([P, H], F32, tag="bank", name="a_ps%d" % c) for c in range(QCHUNKS)]
+        b_acc = [psum.tile([P, H], F32, tag="bank", name="b_acc%d" % c) for c in range(CHUNKS)]
+        a_acc = [psum.tile([P, H], F32, tag="bank", name="a_acc%d" % c) for c in range(CHUNKS)]
 
-        def project(acc, a, plane, rhs, rhs_scale, chunks):
-            for c in chunks:
-                cols = slice(c * P, (c + 1) * P)
-                nc.tensor.matmul_mx(
-                    out=acc[c][:],
-                    lhsT=vw[a][:, cols].bitcast(FP8X4),
-                    lhsT_scale=plane[:, cols],
-                    rhs=rhs,
-                    rhs_scale=rhs_scale,
-                    start=(a == 0),
-                    stop=(a == PASSES - 1),
-                )
+        def project(acc, a, c, weight, weight_plane):
+            nc.tensor.matmul_mx(
+                out=acc[c][:],
+                lhsT=v_words[a][:, c * P : (c + 1) * P].bitcast(FP8X4),
+                lhsT_scale=v_plane[:, a * S + c * P : a * S + (c + 1) * P],
+                rhs=weight,
+                rhs_scale=weight_plane,
+                start=(a == 0),
+                stop=(a == LAST),
+            )
 
-        def gate_pass(a, chunks):
-            project(b_ps, a, vs[:, a * S : (a + 1) * S], (wgw_last[:] if a == PASSES - 1 else wgw[:, a, :]).bitcast(FP4X4), wgs[:, a * H : (a + 1) * H], chunks)
+        def gate_pass(a, c):
+            words = wg_last[:] if a == LAST else wg_first[:, a, :]
+            project(b_acc, a, c, words.bitcast(FP4X4), wg_plane[:, a * H : (a + 1) * H])
 
-        def query_pass(a, chunks):
-            project(a_ps, a, vs[:, a * S : (a + 1) * S], wc[a][:].bitcast(FP8X4), ws[a][:], chunks)
+        def query_pass(a, c):
+            project(a_acc, a, c, wq_codes[a][:].bitcast(FP8X4), wq_plane[a][:])
 
-        every_chunk = range(QCHUNKS)
         round_wq(0)
         round_wq(1)
-        gather_words(0, parts=2)
-        quantize_wq(0)
-        quantize_wq(1)
-        gate_pass(0, every_chunk)
-        query_pass(0, every_chunk)
-        gather_words(1, parts=2)
-        for c in every_chunk:
-            gate_pass(1, [c])
-            query_pass(1, [c])
-        round_wq(2)
-        quantize_wq(2)
-        gather_words(2, parts=2)
-        gate = [keep.tile([P, H], F32, name="gate%d" % c, tag="gate%d" % c, align_bytes=64) for c in every_chunk]
-        for c in range(QCHUNKS + 1):
-            if c < QCHUNKS:
-                gate_pass(2, [c])
-                nc.scalar.activation(gate[c][:], b_ps[c][:], SIGMOID)
+        gather_table_words(0)
+        quantize_wq(0, "table_words0")
+        quantize_wq(1, "wq_bf16_0")
+        for c in range(CHUNKS):
+            gate_pass(0, c)
+        for c in range(CHUNKS):
+            query_pass(0, c)
+        gather_table_words(1)
+        for c in range(CHUNKS):
+            gate_pass(1, c)
+            query_pass(1, c)
+        round_wq(LAST)
+        quantize_wq(LAST, "wq_codes_last")
+        gather_table_words(LAST)
+        gate = [keep.tile([P, H], F32, name="gate%d" % c, align_bytes=64) for c in range(CHUNKS)]
+        for c in range(CHUNKS + 1):
+            if c < CHUNKS:
+                gate_pass(LAST, c)
+                nc.scalar.activation(gate[c][:], b_acc[c][:], SIGMOID)
             if c > 0:
-                query_pass(2, [c - 1])
+                query_pass(LAST, c - 1)
 
-        half = S // 2
-
-        def turn_pair(n):
-            xt = psum.tile([P, 2, 2, P], F32, tag="bank", name="xt%d" % n)
+        def turn_half(n):
+            turned = psum.tile([P, 2, 2, P], F32, tag="bank", name="turned%d" % n)
             for c in range(2):
-                ht = ring.tile([P, H], BF16, name="ht", align_bytes=64)
-                nc.vector.tensor_tensor(ht[:], a_ps[2 * n + c][:], gate[2 * n + c][:], MULT)
-                words = ht[:].bitcast(F32)
+                h_rows = ring.tile([P, H], BF16, name="h_rows", align_bytes=64)
+                nc.vector.tensor_tensor(h_rows[:], a_acc[2 * n + c][:], gate[2 * n + c][:], MULT)
+                pairs = h_rows[:].bitcast(F32)
                 for u in range(2):
-                    nc.tensor.transpose(xt[:, c, u, :], words[:, u : H // 2 : 2], ident[:])
-            return xt
+                    nc.tensor.transpose(turned[:, c, u, :], pairs[:, u : H // 2 : 2], ident[:])
+            return turned
 
-        def quantize_pair(n, xt):
-            hg = keep.tile([P, half * PACK], BF16, name="hg%d" % n, tag="grouped%d" % n, align_bytes=64)
+        def quantize_half(n, turned):
+            h_bf16 = keep.tile([P, HALF * PACK], BF16, name="h_bf16_%d" % n, tag="h_bf16_%d" % n, align_bytes=64)
             nc.scalar.copy(
-                hg[:].bitcast(F32).rearrange("p (c j u) -> p c j u", c=2, u=2), xt[:].rearrange("p c u j -> p c j u")
+                h_bf16[:].bitcast(F32).rearrange("p (c j u) -> p c j u", c=2, u=2),
+                turned[:].rearrange("p c u j -> p c j u"),
             )
-            cols = slice(n * half, (n + 1) * half)
-            nc.vector.quantize_mx(out=hc[:, cols].bitcast(FP8X4), scales=hs[:, cols], in_=hg[:])
+            cols = slice(n * HALF, (n + 1) * HALF)
+            nc.vector.quantize_mx(out=h_codes[:, cols].bitcast(FP8X4), scales=h_plane[:, cols], in_=h_bf16[:])
 
-        turned = [turn_pair(n) for n in range(2)]
-        gather_key_words(0, 1, "kw0")
-        quantize_pair(0, turned[0])
-        quantize_pair(1, turned[1])
-        gather_key_words(1, 1, "grouped0")
+        halves = [turn_half(n) for n in range(2)]
+        gather_key_words(0, "key_words0")
+        quantize_half(0, halves[0])
+        quantize_half(1, halves[1])
+        gather_key_words(1, "h_bf16_0")
 
-        tiles_per_piece = KEY_PIECE // P
+        def logits(i, queries):
+            keys = slice((i % TILES_PER_PIECE) * P, (i % TILES_PER_PIECE + 1) * P)
+            z = psum.tile([P, queries.stop - queries.start], F32, tag="bank", name="z")
+            nc.tensor.matmul_mx(
+                out=z[:],
+                lhsT=key_words[i // TILES_PER_PIECE][:, keys].bitcast(FP8X4),
+                lhsT_scale=key_plane[KEY_PLANE_ROW:P, i * P : (i + 1) * P],
+                rhs=h_codes[:, queries].bitcast(FP8X4),
+                rhs_scale=h_plane[:, queries],
+                start=True,
+                stop=True,
+            )
+            return z
+
         for i in range(KEY_TILES):
-            g, cols = i // tiles_per_piece, slice((i % tiles_per_piece) * P, (i % tiles_per_piece + 1) * P)
-            if i == LATE_TILE + 1:
-                gather_key_words(2, 1, "sig%d" % LATE_TILE)
-
-            def logits(js):
-                z = psum.tile([P, js.stop - js.start], F32, tag="bank", name="z")
-                nc.tensor.matmul_mx(
-                    out=z[:],
-                    lhsT=kw[g][:, cols].bitcast(FP8X4),
-                    lhsT_scale=ks[KEY_PLANE_ROW:P, i * P : (i + 1) * P],
-                    rhs=hc[:, js].bitcast(FP8X4),
-                    rhs_scale=hs[:, js],
-                    start=True,
-                    stop=True,
-                )
-                return z
-
+            under_gather = i == LAST_GATHER_AFTER + 1
+            if under_gather:
+                gather_key_words(2, "sig%d" % LAST_GATHER_AFTER)
             sig = keep.tile([P, S], F32, name="sig%d" % i, tag="sig%d" % i, align_bytes=64)
-            res = keep.tile([P, S], F32, name="res%d" % i)
-            if i == 0:
-                for n in range(2):
-                    js = slice(n * half, (n + 1) * half)
-                    nc.scalar.activation(sig[:, js], logits(js)[:], SIGMOID, scale=2.0 / CAP)
-                nc.vector.tensor_scalar(res[:], sig[:], 2.0 * CAP, -CAP, MULT, ADD)
-                nc.sync.dma_start(out=out[0:P, :], in_=res[:])
-                continue
-            z = logits(slice(0, S))
-            nc.scalar.activation(sig[:], z[:], SIGMOID, scale=2.0 / CAP)
-            if i == LATE_TILE + 1:
-                nc.gpsimd.tensor_scalar(res[:], sig[:], 2.0 * CAP, -CAP, MULT, ADD)
+            capped = keep.tile([P, S], F32, name="capped%d" % i)
+            width = HALF if i == 0 else S
+            for first in range(0, S, width):
+                queries = slice(first, first + width)
+                nc.scalar.activation(sig[:, queries], logits(i, queries)[:], SIGMOID, scale=2.0 / CAP)
+            if under_gather:
+                nc.gpsimd.tensor_scalar(capped[:], sig[:], 2.0 * CAP, -CAP, MULT, ADD)
             else:
-                nc.vector.tensor_scalar(res[:], sig[:], 2.0 * CAP, -CAP, MULT, ADD)
-            nc.sync.dma_start(out=out[i * P : (i + 1) * P, :], in_=res[:])
+                nc.vector.tensor_scalar(capped[:], sig[:], 2.0 * CAP, shift[:], MULT, ADD)
+            nc.sync.dma_start(out=out[i * P : (i + 1) * P, :], in_=capped[:])

@@ -29,6 +29,7 @@ PASSES = K // (P * PACK)
 LAST = PASSES - 1
 CHUNKS = S // P
 HALF = S // 2
+SIDE = H // 2
 KEY_TILES = S2 // P
 KEY_PIECE = 512
 TILES_PER_PIECE = KEY_PIECE // P
@@ -36,7 +37,6 @@ TABLE_SPREAD_ROW = 4
 KEY_SPREAD_ROW = 5
 KEY_PLANE_ROW = 8
 VECTOR_CLEARS = PASSES * T // 6
-SCALAR_COLS = (H, H, H // 2)
 LAST_GATHER_AFTER = 2
 
 
@@ -46,7 +46,6 @@ def tile_list_paged_softcap_logits_kernel(
     nc = tc.nc
     with ExitStack() as ctx:
         keep = ctx.enter_context(tc.tile_pool(name="keep", bufs=1))
-        ring = ctx.enter_context(tc.tile_pool(name="ring", bufs=CHUNKS))
         psum = ctx.enter_context(tc.psum_pool(name="psum", bufs=8))
 
         token_list = keep.tile([P, S // LIST_ROWS], U16, name="token_list")
@@ -54,7 +53,6 @@ def tile_list_paged_softcap_logits_kernel(
         v_window = keep.tile([P, PASSES * T], U8, name="v_window", align_bytes=64)
         v_picked = keep.tile([P, PASSES * S], U8, name="v_picked", align_bytes=64)
         v_plane = keep.tile([P, PASSES * S], U8, name="v_plane", align_bytes=64)
-        key_picked = keep.tile([P, S2], U8, name="key_picked", tag="key_picked", align_bytes=64)
         key_plane = keep.tile([P, S2], U8, name="key_plane", align_bytes=64)
         key_window = keep.tile([P, T2], U8, name="key_window", align_bytes=64)
         wg_plane = keep.tile([P, PASSES * H], U8, name="wg_plane", align_bytes=64)
@@ -63,22 +61,30 @@ def tile_list_paged_softcap_logits_kernel(
         zero = keep.tile([P, 1], F32, name="zero")
         centre = keep.tile([P, 1], F32, name="centre")
 
-        nc.gpsimd.memset(wg_plane[:].bitcast(I32), 0)
         nc.vector.memset(v_window[:].bitcast(I32)[:, :VECTOR_CLEARS], 0)
         nc.gpsimd.memset(v_window[:].bitcast(I32)[:, VECTOR_CLEARS:], 0)
         nc.vector.memset(zero[:], 0.0)
         nc.vector.memset(key_window[:].bitcast(I32), 0)
+        nc.gpsimd.memset(wg_plane[:].bitcast(I32), 0)
         nc.vector.memset(v_plane[:].bitcast(I32), 0)
         nc.vector.memset(key_plane[:].bitcast(I32), 0)
 
-        def load_table_words(a):
-            table_words[a] = keep.tile([P, T], I32, name="table_words%d" % a, tag="table_words%d" % a, align_bytes=64)
-            nc.sync.dma_start(out=table_words[a][:], in_=tab_words[a].rearrange("p t i -> p (t i)").bitcast(I32))
+        def load_table_words(a, cols=slice(0, T)):
+            if a not in table_words:
+                name = "table_words%d" % a
+                table_words[a] = keep.tile([P, T], I32, name=name, tag=name, align_bytes=64)
+            words = tab_words[a].rearrange("p t i -> p (t i)").bitcast(I32)
+            nc.sync.dma_start(out=table_words[a][:, cols], in_=words[:, cols])
 
         def load_wq(a):
-            wq_raw[a] = keep.tile([P, PACK, H], F32, name="wq_raw%d" % a, align_bytes=64)
-            rows = wq[a * P * PACK : (a + 1) * P * PACK, :]
-            nc.sync.dma_start(out=wq_raw[a][:], in_=rows.rearrange("(p j) c -> p j c", j=PACK))
+            rows = wq[a * P * PACK : (a + 1) * P * PACK, :].rearrange("(p j) c -> p j c", j=PACK)
+            width = SIDE if a == LAST else H
+            for first in range(0, H, width):
+                name = "wq_raw%d_%d" % (a, first)
+                raw = keep.tile([P, PACK, width], F32, name=name, tag=name, align_bytes=64)
+                nc.sync.dma_start(out=raw[:], in_=rows[:, :, first : first + width])
+                for col in range(first, first + width, SIDE):
+                    wq_raw[a, col // SIDE] = raw[:, :, col - first : col - first + SIDE]
 
         def load_gate_plane():
             by_row = wg_scales.rearrange("a (q r) t -> r q a t", r=SCALE_ROWS)
@@ -89,10 +95,11 @@ def tile_list_paged_softcap_logits_kernel(
         v_words = [keep.tile([P, S], U32, name="v_words%d" % a, align_bytes=64) for a in range(PASSES)]
 
         def gather_table_words(a):
-            for n in range(2):
-                offsets = token_list[:, n * HALF // LIST_ROWS : (n + 1) * HALF // LIST_ROWS]
+            width = HALF if a == LAST else S
+            for first in range(0, S, width):
+                offsets = token_list[:, first // LIST_ROWS : (first + width) // LIST_ROWS]
                 nc.vector.tensor_copy(
-                    v_words[a][:, n * HALF : (n + 1) * HALF], table_words[a][:].bitcast(U32).indirect(offsets)
+                    v_words[a][:, first : first + width], table_words[a][:].bitcast(U32).indirect(offsets)
                 )
 
         def spread_scale_rows(window, scales, first):
@@ -107,39 +114,38 @@ def tile_list_paged_softcap_logits_kernel(
                     in_=picked[first + SPREAD * r : P : QUADRANT, :].bitcast(I32),
                 )
 
-        wg_first = keep.tile([P, LAST, 2 * H], U8, name="wg_first", align_bytes=64)
-        wg_last = keep.tile([P, 2 * H], U8, name="wg_last", align_bytes=64)
+        wg_codes = keep.tile([P, PASSES, 2 * H], U8, name="wg_codes", align_bytes=64)
         nc.sync.dma_start(token_list[:], offs)
-        nc.sync.dma_start(out=wg_first[:].bitcast(I32), in_=wg_words[:LAST].rearrange("a p c -> p a c").bitcast(I32))
-        load_gate_plane()
+        nc.sync.dma_start(key_list[:], offs2)
+        load_table_words(0, slice(0, T // 2))
         spread_scale_rows(v_window, tab_scales, TABLE_SPREAD_ROW)
+        load_table_words(0, slice(T // 2, T))
         nc.scalar.activation(centre[:], zero[:], SIGMOID)
         shift = keep.tile([P, 1], F32, name="shift")
         nc.gpsimd.tensor_scalar(shift[:], centre[:], -2.0 * CAP, 0.0, MULT, ADD)
-        load_wq(0)
-        nc.sync.dma_start(key_list[:], offs2)
         spread_scale_rows(key_window, tab2_scales, KEY_SPREAD_ROW)
-        load_wq(1)
-        load_table_words(0)
+        nc.sync.dma_start(out=wg_codes[:].bitcast(I32), in_=wg_words.rearrange("a p c -> p a c").bitcast(I32))
+        load_wq(0)
+        load_gate_plane()
+        load_table_words(1)
         for a in range(PASSES):
             nc.vector.tensor_copy(
                 v_picked[:, a * S : (a + 1) * S], v_window[:, a * T : (a + 1) * T].indirect(token_list[:])
             )
         place_scale_rows(v_plane, 0, v_picked, TABLE_SPREAD_ROW)
-        load_table_words(1)
-        load_wq(LAST)
+        load_wq(1)
         load_table_words(LAST)
-        nc.sync.dma_start(out=wg_last[:].bitcast(I32), in_=wg_words[LAST].bitcast(I32))
+        load_wq(LAST)
+        gather_table_words(0)
+        key_picked = keep.tile([P, S2], U8, name="key_picked", tag="key_picked", align_bytes=64)
+        nc.vector.tensor_copy(key_picked[:], key_window[:].indirect(key_list[:]))
+        gather_table_words(1)
         key_table = keep.tile([P, T2], I32, name="key_table", align_bytes=64)
         nc.sync.dma_start(out=key_table[:], in_=tab2_words[0].rearrange("p t i -> p (t i)").bitcast(I32))
-        nc.vector.tensor_copy(key_picked[:], key_window[:].indirect(key_list[:]))
         place_scale_rows(key_plane, KEY_PLANE_ROW, key_picked, KEY_SPREAD_ROW)
+        gather_table_words(LAST)
         make_identity(nc, ident[:])
 
-        wq_bf16 = [
-            keep.tile([P, H, PACK], BF16, name="wq_bf16_%d" % a, tag="wq_bf16_%d" % a, align_bytes=64)
-            for a in range(PASSES)
-        ]
         wq_codes, wq_plane = {}, {}
         h_codes = keep.tile([P, S], U32, name="h_codes", align_bytes=64)
         h_plane = keep.tile([P, S], U8, name="h_plane", tag="key_picked", align_bytes=64)
@@ -151,72 +157,75 @@ def tile_list_paged_softcap_logits_kernel(
                 key_words[g][:], key_table[:].bitcast(U32).indirect(key_list[:, g * cols : (g + 1) * cols])
             )
 
-        def round_wq(a):
-            groups = SCALAR_COLS[a] // 4
-            src = wq_raw[a][:].rearrange("p t (c i) -> p c t i", i=4)
-            dst = wq_bf16[a][:].rearrange("p (c i) t -> p c t i", i=4)
-            nc.scalar.copy(dst[:, :groups], src[:, :groups])
-            if SCALAR_COLS[a] < H:
-                nc.vector.tensor_copy(dst[:, groups:], src[:, groups:])
-
-        def quantize_wq(a, tag):
-            wq_codes[a] = keep.tile([P, H], U32, name="wq_codes%d" % a, tag=tag, align_bytes=64)
-            wq_plane[a] = keep.tile([P, H], U8, name="wq_plane%d" % a, align_bytes=64)
+        def quantize_wq(a, n):
+            rounded = keep.tile([P, SIDE, PACK], BF16, name="wq_bf16_%d_%d" % (a, n), align_bytes=64)
+            src = wq_raw[a, n].rearrange("p t (c i) -> p c t i", i=4)
+            dst = rounded[:].rearrange("p (c i) t -> p c t i", i=4)
+            if (a, n) == (LAST, 1):
+                nc.vector.tensor_copy(dst, src)
+            else:
+                nc.scalar.copy(dst, src)
+            name = "wq_codes%d_%d" % (a, n)
+            tag = "table_words%d" % LAST if (a, n) == (1, 1) else name
+            wq_codes[a, n] = keep.tile([P, SIDE], U32, name=name, tag=tag, align_bytes=64)
+            wq_plane[a, n] = keep.tile([P, SIDE], U8, name="wq_plane%d_%d" % (a, n), align_bytes=64)
             nc.vector.quantize_mx(
-                out=wq_codes[a][:].bitcast(FP8X4), scales=wq_plane[a][:], in_=wq_bf16[a][:].rearrange("p c t -> p (c t)")
+                out=wq_codes[a, n][:].bitcast(FP8X4),
+                scales=wq_plane[a, n][:],
+                in_=rounded[:].rearrange("p c t -> p (c t)"),
             )
 
         b_acc = [psum.tile([P, H], F32, tag="bank", name="b_acc%d" % c) for c in range(CHUNKS)]
-        a_acc = [psum.tile([P, H], F32, tag="bank", name="a_acc%d" % c) for c in range(CHUNKS)]
+        a_acc = {
+            (n, pair): psum.tile([P, 2, SIDE], F32, tag="bank", name="a_acc%d_%d" % (n, pair))
+            for n in range(2)
+            for pair in range(2)
+        }
 
-        def project(acc, a, c, weight, weight_plane):
+        def project(acc, a, c, weight, weight_plane, start, stop):
             nc.tensor.matmul_mx(
-                out=acc[c][:],
+                out=acc,
                 lhsT=v_words[a][:, c * P : (c + 1) * P].bitcast(FP8X4),
                 lhsT_scale=v_plane[:, a * S + c * P : a * S + (c + 1) * P],
                 rhs=weight,
                 rhs_scale=weight_plane,
-                start=(a == 0),
-                stop=(a == LAST),
+                start=start,
+                stop=stop,
             )
 
-        def gate_pass(a, c):
-            words = wg_last[:] if a == LAST else wg_first[:, a, :]
-            project(b_acc, a, c, words.bitcast(FP4X4), wg_plane[:, a * H : (a + 1) * H])
+        for a in range(PASSES):
+            for c in range(CHUNKS):
+                words = wg_codes[:, a, :].bitcast(FP4X4)
+                project(b_acc[c][:], a, c, words, wg_plane[:, a * H : (a + 1) * H], a == 0, a == LAST)
+            for n in range(2):
+                quantize_wq(a, n)
+                for c in range(CHUNKS):
+                    project(
+                        a_acc[n, c // 2][:, c % 2, :],
+                        a,
+                        c,
+                        wq_codes[a, n][:].bitcast(FP8X4),
+                        wq_plane[a, n][:],
+                        a == 0 and c % 2 == 0,
+                        a == LAST and c % 2 == 1,
+                    )
 
-        def query_pass(a, c):
-            project(a_acc, a, c, wq_codes[a][:].bitcast(FP8X4), wq_plane[a][:])
-
-        round_wq(0)
-        round_wq(1)
-        gather_table_words(0)
-        quantize_wq(0, "table_words0")
-        quantize_wq(1, "wq_bf16_0")
-        for c in range(CHUNKS):
-            gate_pass(0, c)
-        for c in range(CHUNKS):
-            query_pass(0, c)
-        gather_table_words(1)
-        for c in range(CHUNKS):
-            gate_pass(1, c)
-            query_pass(1, c)
-        round_wq(LAST)
-        quantize_wq(LAST, "wq_codes_last")
-        gather_table_words(LAST)
-        gate = [keep.tile([P, H], F32, name="gate%d" % c, align_bytes=64) for c in range(CHUNKS)]
-        for c in range(CHUNKS + 1):
-            if c < CHUNKS:
-                gate_pass(LAST, c)
-                nc.scalar.activation(gate[c][:], b_acc[c][:], SIGMOID)
-            if c > 0:
-                query_pass(LAST, c - 1)
+        h_rows = [keep.tile([P, 2, H], BF16, name="h_rows%d" % pair, align_bytes=64) for pair in range(2)]
+        gate_tags = ["wq_raw%d_0" % LAST, "gate1"]
+        for n in range(2):
+            cols = slice(n * SIDE, (n + 1) * SIDE)
+            gate = keep.tile([P, CHUNKS, SIDE], F32, name="gate%d" % n, tag=gate_tags[n], align_bytes=64)
+            for c in range(CHUNKS):
+                nc.scalar.activation(gate[:, c, :], b_acc[c][:, cols], SIGMOID)
+            for pair in range(2):
+                nc.vector.tensor_tensor(
+                    h_rows[pair][:, :, cols], a_acc[n, pair][:], gate[:, 2 * pair : 2 * pair + 2, :], MULT
+                )
 
         def turn_half(n):
             turned = psum.tile([P, 2, 2, P], F32, tag="bank", name="turned%d" % n)
             for c in range(2):
-                h_rows = ring.tile([P, H], BF16, name="h_rows", align_bytes=64)
-                nc.vector.tensor_tensor(h_rows[:], a_acc[2 * n + c][:], gate[2 * n + c][:], MULT)
-                pairs = h_rows[:].bitcast(F32)
+                pairs = h_rows[n][:, c, :].bitcast(F32)
                 for u in range(2):
                     nc.tensor.transpose(turned[:, c, u, :], pairs[:, u : H // 2 : 2], ident[:])
             return turned

@@ -23,7 +23,7 @@ P = 128
 PACK = 4
 QUADRANT = 32
 SCALE_ROWS = 4
-SPREAD = 8
+SPREAD = 4
 LIST_ROWS = 16
 PASSES = K // (P * PACK)
 LAST = PASSES - 1
@@ -33,8 +33,8 @@ SIDE = H // 2
 KEY_TILES = S2 // P
 KEY_PIECE = 512
 TILES_PER_PIECE = KEY_PIECE // P
-TABLE_SPREAD_ROW = 4
-KEY_SPREAD_ROW = 5
+TABLE_SPREAD_ROW = 33
+KEY_SPREAD_ROW = 34
 KEY_PLANE_ROW = 8
 VECTOR_CLEARS = PASSES * T // 6
 LAST_GATHER_AFTER = 2
@@ -105,13 +105,13 @@ def tile_list_paged_softcap_logits_kernel(
         def spread_scale_rows(window, scales, first):
             passes = scales.shape[0]
             dst = window[:].bitcast(I32).rearrange("p (a t) -> p a t", a=passes)
-            nc.sync.dma_start(out=dst[first:P:SPREAD], in_=scales.rearrange("a q t -> q a t").bitcast(I32))
+            nc.sync.dma_start(out=dst[first : first + 16 * SPREAD : SPREAD], in_=scales.rearrange("a q t -> q a t").bitcast(I32))
 
         def place_scale_rows(plane, first_row, picked, first):
             for r in range(SCALE_ROWS):
                 nc.sync.dma_start(
                     out=plane[first_row + r : P : QUADRANT, :].bitcast(I32),
-                    in_=picked[first + SPREAD * r : P : QUADRANT, :].bitcast(I32),
+                    in_=picked[first + SPREAD * r : first + 16 * SPREAD : SCALE_ROWS * SPREAD, :].bitcast(I32),
                 )
 
         wg_codes = keep.tile([P, PASSES, 2 * H], U8, name="wg_codes", align_bytes=64)
@@ -137,12 +137,16 @@ def tile_list_paged_softcap_logits_kernel(
         load_table_words(LAST)
         load_wq(LAST)
         gather_table_words(0)
-        key_picked = keep.tile([P, S2], U8, name="key_picked", tag="key_picked", align_bytes=64)
-        nc.vector.tensor_copy(key_picked[:], key_window[:].indirect(key_list[:]))
+        first_cols = KEY_PIECE // LIST_ROWS
+        key_picked = keep.tile([P, KEY_PIECE], U8, name="key_picked", tag="key_picked", align_bytes=64)
+        nc.vector.tensor_copy(key_picked[:], key_window[:].indirect(key_list[:, :first_cols]))
         gather_table_words(1)
+        rest_picked = keep.tile([P, S2 - KEY_PIECE], U8, name="rest_picked", tag="table_words1", align_bytes=64)
+        nc.vector.tensor_copy(rest_picked[:], key_window[:].indirect(key_list[:, first_cols:]))
         key_table = keep.tile([P, T2], I32, name="key_table", align_bytes=64)
         nc.sync.dma_start(out=key_table[:], in_=tab2_words[0].rearrange("p t i -> p (t i)").bitcast(I32))
-        place_scale_rows(key_plane, KEY_PLANE_ROW, key_picked, KEY_SPREAD_ROW)
+        place_scale_rows(key_plane[:, :KEY_PIECE], KEY_PLANE_ROW, key_picked, KEY_SPREAD_ROW)
+        place_scale_rows(key_plane[:, KEY_PIECE:], KEY_PLANE_ROW, rest_picked, KEY_SPREAD_ROW)
         gather_table_words(LAST)
         make_identity(nc, ident[:])
 

@@ -36,7 +36,8 @@ TILES_PER_PIECE = KEY_PIECE // P
 TABLE_SPREAD_ROW = 33
 KEY_SPREAD_ROW = 34
 KEY_PLANE_ROW = 8
-VECTOR_CLEARS = PASSES * T // 6
+VECTOR_CLEARS = 5 * T // 16
+LAST_SPREAD_ROW = 32
 LAST_GATHER_AFTER = 2
 
 
@@ -50,8 +51,8 @@ def tile_list_paged_softcap_logits_kernel(
 
         token_list = keep.tile([P, S // LIST_ROWS], U16, name="token_list")
         key_list = keep.tile([P, S2 // LIST_ROWS], U16, name="key_list")
-        v_window = keep.tile([P, PASSES * T], U8, name="v_window", align_bytes=64)
-        v_picked = keep.tile([P, PASSES * S], U8, name="v_picked", align_bytes=64)
+        v_window = keep.tile([P, LAST * T], U8, name="v_window", align_bytes=64)
+        v_picked = keep.tile([P, LAST * S], U8, name="v_picked", align_bytes=64)
         v_plane = keep.tile([P, PASSES * S], U8, name="v_plane", align_bytes=64)
         key_plane = keep.tile([P, S2], U8, name="key_plane", align_bytes=64)
         key_window = keep.tile([P, T2], U8, name="key_window", align_bytes=64)
@@ -104,7 +105,7 @@ def tile_list_paged_softcap_logits_kernel(
 
         def spread_scale_rows(window, scales, first):
             passes = scales.shape[0]
-            dst = window[:].bitcast(I32).rearrange("p (a t) -> p a t", a=passes)
+            dst = window.bitcast(I32).rearrange("p (a t) -> p a t", a=passes)
             nc.sync.dma_start(out=dst[first : first + 16 * SPREAD : SPREAD], in_=scales.rearrange("a q t -> q a t").bitcast(I32))
 
         def place_scale_rows(plane, first_row, picked, first):
@@ -118,23 +119,25 @@ def tile_list_paged_softcap_logits_kernel(
         nc.sync.dma_start(token_list[:], offs)
         nc.sync.dma_start(key_list[:], offs2)
         load_table_words(0, slice(0, T // 2))
-        spread_scale_rows(v_window, tab_scales, TABLE_SPREAD_ROW)
+        spread_scale_rows(v_window[:], tab_scales[:LAST], TABLE_SPREAD_ROW)
+        spread_scale_rows(v_window[:, :T], tab_scales[LAST:], LAST_SPREAD_ROW)
         load_table_words(0, slice(T // 2, T))
         nc.scalar.activation(centre[:], zero[:], SIGMOID)
         shift = keep.tile([P, 1], F32, name="shift")
         nc.gpsimd.tensor_scalar(shift[:], centre[:], -2.0 * CAP, 0.0, MULT, ADD)
-        spread_scale_rows(key_window, tab2_scales, KEY_SPREAD_ROW)
+        spread_scale_rows(key_window[:], tab2_scales, KEY_SPREAD_ROW)
         nc.sync.dma_start(out=wg_codes[:].bitcast(I32), in_=wg_words.rearrange("a p c -> p a c").bitcast(I32))
         load_wq(0)
         load_gate_plane()
         load_table_words(1)
-        for a in range(PASSES):
+        for n in range(LAST):
             nc.vector.tensor_copy(
-                v_picked[:, a * S : (a + 1) * S], v_window[:, a * T : (a + 1) * T].indirect(token_list[:])
+                v_picked[:, n * S : (n + 1) * S], v_window[:, n * T : (n + 1) * T].indirect(token_list[:])
             )
-        place_scale_rows(v_plane, 0, v_picked, TABLE_SPREAD_ROW)
+        place_scale_rows(v_plane[:, : LAST * S], 0, v_picked[:], TABLE_SPREAD_ROW)
         load_wq(1)
         load_table_words(LAST)
+        place_scale_rows(v_plane[:, LAST * S :], 0, v_picked[:, :S], LAST_SPREAD_ROW)
         load_wq(LAST)
         gather_table_words(0)
         first_cols = KEY_PIECE // LIST_ROWS

@@ -52,7 +52,7 @@ def tile_list_paged_softcap_logits_kernel(
         token_list = keep.tile([P, S // LIST_ROWS], U16, name="token_list")
         key_list = keep.tile([P, S2 // LIST_ROWS], U16, name="key_list")
         v_window = keep.tile([P, LAST * T], U8, name="v_window", align_bytes=64)
-        v_picked = keep.tile([P, LAST * S], U8, name="v_picked", align_bytes=64)
+        v_picked = keep.tile([P, LAST * S], U8, name="v_picked", tag="v_picked", align_bytes=64)
         v_plane = keep.tile([P, PASSES * S], U8, name="v_plane", align_bytes=64)
         key_plane = keep.tile([P, S2], U8, name="key_plane", align_bytes=64)
         key_window = keep.tile([P, T2], U8, name="key_window", align_bytes=64)
@@ -116,9 +116,9 @@ def tile_list_paged_softcap_logits_kernel(
                 )
 
         wg_codes = keep.tile([P, PASSES, 2 * H], U8, name="wg_codes", align_bytes=64)
+        load_table_words(0, slice(0, T // 2))
         nc.sync.dma_start(token_list[:], offs)
         nc.sync.dma_start(key_list[:], offs2)
-        load_table_words(0, slice(0, T // 2))
         spread_scale_rows(v_window[:], tab_scales[:LAST], TABLE_SPREAD_ROW)
         spread_scale_rows(v_window[:, :T], tab_scales[LAST:], LAST_SPREAD_ROW)
         load_table_words(0, slice(T // 2, T))
@@ -166,14 +166,14 @@ def tile_list_paged_softcap_logits_kernel(
 
         def quantize_wq(a, n):
             rounded = keep.tile([P, SIDE, PACK], BF16, name="wq_bf16_%d_%d" % (a, n), align_bytes=64)
-            src = wq_raw[a, n].rearrange("p t (c i) -> p c t i", i=4)
-            dst = rounded[:].rearrange("p (c i) t -> p c t i", i=4)
+            src = wq_raw[a, n].rearrange("p t (j u e) -> p j t u e", u=2, e=2)
+            dst = rounded[:].rearrange("p (u j e) t -> p j t u e", u=2, e=2)
             if (a, n) == (LAST, 1):
                 nc.vector.tensor_copy(dst, src)
             else:
                 nc.scalar.copy(dst, src)
             name = "wq_codes%d_%d" % (a, n)
-            tag = "table_words%d" % LAST if (a, n) == (1, 1) else name
+            tag = "v_picked" if (a, n) == (1, 1) else name
             wq_codes[a, n] = keep.tile([P, SIDE], U32, name=name, tag=tag, align_bytes=64)
             wq_plane[a, n] = keep.tile([P, SIDE], U8, name="wq_plane%d_%d" % (a, n), align_bytes=64)
             nc.vector.quantize_mx(
@@ -218,15 +218,20 @@ def tile_list_paged_softcap_logits_kernel(
                     )
 
         h_rows = [keep.tile([P, 2, H], BF16, name="h_rows%d" % pair, align_bytes=64) for pair in range(2)]
-        gate_tags = ["wq_raw%d_0" % LAST, "gate1"]
+        gate = keep.tile([P, CHUNKS, H], F32, name="gate", tag="wq_raw%d_0" % LAST, align_bytes=64)
+        for c in range(CHUNKS):
+            nc.scalar.activation(
+                gate[:, c, :].rearrange("p (u j e) -> p u j e", u=2, e=2),
+                b_acc[c][:].rearrange("p (j u e) -> p u j e", u=2, e=2),
+                SIGMOID,
+            )
         for n in range(2):
-            cols = slice(n * SIDE, (n + 1) * SIDE)
-            gate = keep.tile([P, CHUNKS, SIDE], F32, name="gate%d" % n, tag=gate_tags[n], align_bytes=64)
-            for c in range(CHUNKS):
-                nc.scalar.activation(gate[:, c, :], b_acc[c][:, cols], SIGMOID)
             for pair in range(2):
                 nc.vector.tensor_tensor(
-                    h_rows[pair][:, :, cols], a_acc[n, pair][:], gate[:, 2 * pair : 2 * pair + 2, :], MULT
+                    h_rows[pair][:].rearrange("p c (u n x) -> p n c u x", u=2, n=2)[:, n],
+                    a_acc[n, pair][:].rearrange("p c (u x) -> p c u x", u=2),
+                    gate[:, 2 * pair : 2 * pair + 2, :].rearrange("p c (u n x) -> p n c u x", u=2, n=2)[:, n],
+                    MULT,
                 )
 
         def turn_half(n):
@@ -234,7 +239,7 @@ def tile_list_paged_softcap_logits_kernel(
             for c in range(2):
                 pairs = h_rows[n][:, c, :].bitcast(F32)
                 for u in range(2):
-                    nc.tensor.transpose(turned[:, c, u, :], pairs[:, u : H // 2 : 2], ident[:])
+                    nc.tensor.transpose(turned[:, c, u, :], pairs[:, u * P : (u + 1) * P], ident[:])
             return turned
 
         def quantize_half(n, turned):
@@ -271,13 +276,13 @@ def tile_list_paged_softcap_logits_kernel(
             if under_gather:
                 gather_key_words(2, "sig%d" % LAST_GATHER_AFTER)
             sig = keep.tile([P, S], F32, name="sig%d" % i, tag="sig%d" % i, align_bytes=64)
-            capped = keep.tile([P, S], F32, name="capped%d" % i)
             width = HALF if i == 0 else S
             for first in range(0, S, width):
                 queries = slice(first, first + width)
+                capped = keep.tile([P, width], F32, name="capped%d_%d" % (i, first))
                 nc.scalar.activation(sig[:, queries], logits(i, queries)[:], SIGMOID, scale=2.0 / CAP)
-            if under_gather:
-                nc.gpsimd.tensor_scalar(capped[:], sig[:], 2.0 * CAP, -CAP, MULT, ADD)
-            else:
-                nc.vector.tensor_scalar(capped[:], sig[:], 2.0 * CAP, shift[:], MULT, ADD)
-            nc.sync.dma_start(out=out[i * P : (i + 1) * P, :], in_=capped[:])
+                if under_gather:
+                    nc.gpsimd.tensor_scalar(capped[:], sig[:], 2.0 * CAP, -CAP, MULT, ADD)
+                else:
+                    nc.vector.tensor_scalar(capped[:], sig[:, queries], 2.0 * CAP, shift[:], MULT, ADD)
+                nc.sync.dma_start(out=out[i * P : (i + 1) * P, queries], in_=capped[:])

@@ -38,7 +38,7 @@ KEY_SPREAD_ROW = 34
 KEY_PLANE_ROW = 8
 VECTOR_CLEARS = 5 * T // 16
 LAST_SPREAD_ROW = 32
-LAST_GATHER_AFTER = 2
+LAST_GATHER_AFTER = 1
 
 
 def tile_list_paged_softcap_logits_kernel(
@@ -51,7 +51,7 @@ def tile_list_paged_softcap_logits_kernel(
 
         token_list = keep.tile([P, S // LIST_ROWS], U16, name="token_list")
         key_list = keep.tile([P, S2 // LIST_ROWS], U16, name="key_list")
-        v_window = keep.tile([P, LAST * T], U8, name="v_window", align_bytes=64)
+        v_window = keep.tile([P, LAST * T], U8, name="v_window", tag="v_window", align_bytes=64)
         v_picked = keep.tile([P, LAST * S], U8, name="v_picked", tag="v_picked", align_bytes=64)
         v_plane = keep.tile([P, PASSES * S], U8, name="v_plane", align_bytes=64)
         key_plane = keep.tile([P, S2], U8, name="key_plane", align_bytes=64)
@@ -70,12 +70,9 @@ def tile_list_paged_softcap_logits_kernel(
         nc.vector.memset(v_plane[:].bitcast(I32), 0)
         nc.vector.memset(key_plane[:].bitcast(I32), 0)
 
-        def load_table_words(a, cols=slice(0, T)):
-            if a not in table_words:
-                name = "table_words%d" % a
-                table_words[a] = keep.tile([P, T], I32, name=name, tag=name, align_bytes=64)
-            words = tab_words[a].rearrange("p t i -> p (t i)").bitcast(I32)
-            nc.sync.dma_start(out=table_words[a][:, cols], in_=words[:, cols])
+        def load_table_words(a):
+            table_words[a] = keep.tile([P, T], I32, name="table_words%d" % a, tag="table_words%d" % a, align_bytes=64)
+            nc.sync.dma_start(out=table_words[a][:], in_=tab_words[a].rearrange("p t i -> p (t i)").bitcast(I32))
 
         def load_wq(a):
             rows = wq[a * P * PACK : (a + 1) * P * PACK, :].rearrange("(p j) c -> p j c", j=PACK)
@@ -87,13 +84,16 @@ def tile_list_paged_softcap_logits_kernel(
                 for col in range(first, first + width, SIDE):
                     wq_raw[a, col // SIDE] = raw[:, :, col - first : col - first + SIDE]
 
-        def load_gate_plane():
+        def load_gate_plane(rows):
             by_row = wg_scales.rearrange("a (q r) t -> r q a t", r=SCALE_ROWS)
             dst = wg_plane[:].bitcast(I32).rearrange("p (a t) -> p a t", a=PASSES)
-            for r in range(SCALE_ROWS):
+            for r in rows:
                 nc.sync.dma_start(out=dst[r:P:QUADRANT], in_=by_row[r].bitcast(I32))
 
-        v_words = [keep.tile([P, S], U32, name="v_words%d" % a, align_bytes=64) for a in range(PASSES)]
+        word_tags = ["v_window", "v_words1", "v_words2"]
+        v_words = [
+            keep.tile([P, S], U32, name="v_words%d" % a, tag=word_tags[a], align_bytes=64) for a in range(PASSES)
+        ]
 
         def gather_table_words(a):
             width = HALF if a == LAST else S
@@ -116,19 +116,19 @@ def tile_list_paged_softcap_logits_kernel(
                 )
 
         wg_codes = keep.tile([P, PASSES, 2 * H], U8, name="wg_codes", align_bytes=64)
-        load_table_words(0, slice(0, T // 2))
+        load_table_words(0)
         nc.sync.dma_start(token_list[:], offs)
-        nc.sync.dma_start(key_list[:], offs2)
         spread_scale_rows(v_window[:], tab_scales[:LAST], TABLE_SPREAD_ROW)
         spread_scale_rows(v_window[:, :T], tab_scales[LAST:], LAST_SPREAD_ROW)
-        load_table_words(0, slice(T // 2, T))
+        load_gate_plane(range(SCALE_ROWS - 1))
+        load_wq(0)
+        load_gate_plane(range(SCALE_ROWS - 1, SCALE_ROWS))
         nc.scalar.activation(centre[:], zero[:], SIGMOID)
         shift = keep.tile([P, 1], F32, name="shift")
         nc.gpsimd.tensor_scalar(shift[:], centre[:], -2.0 * CAP, 0.0, MULT, ADD)
+        nc.sync.dma_start(key_list[:], offs2)
         spread_scale_rows(key_window[:], tab2_scales, KEY_SPREAD_ROW)
         nc.sync.dma_start(out=wg_codes[:].bitcast(I32), in_=wg_words.rearrange("a p c -> p a c").bitcast(I32))
-        load_wq(0)
-        load_gate_plane()
         load_table_words(1)
         for n in range(LAST):
             nc.vector.tensor_copy(
@@ -272,8 +272,8 @@ def tile_list_paged_softcap_logits_kernel(
             return z
 
         for i in range(KEY_TILES):
-            under_gather = i == LAST_GATHER_AFTER + 1
-            if under_gather:
+            under_gather = i - LAST_GATHER_AFTER in (1, 2)
+            if i == LAST_GATHER_AFTER + 1:
                 gather_key_words(2, "sig%d" % LAST_GATHER_AFTER)
             sig = keep.tile([P, S], F32, name="sig%d" % i, tag="sig%d" % i, align_bytes=64)
             width = HALF if i == 0 else S
@@ -285,4 +285,5 @@ def tile_list_paged_softcap_logits_kernel(
                     nc.gpsimd.tensor_scalar(capped[:], sig[:], 2.0 * CAP, -CAP, MULT, ADD)
                 else:
                     nc.vector.tensor_scalar(capped[:], sig[:, queries], 2.0 * CAP, shift[:], MULT, ADD)
-                nc.sync.dma_start(out=out[i * P : (i + 1) * P, queries], in_=capped[:])
+                queue = nc.scalar if i >= 5 and i % 2 == 1 else nc.sync
+                queue.dma_start(out=out[i * P : (i + 1) * P, queries], in_=capped[:])

@@ -38,6 +38,7 @@ KEY_SPREAD_ROW = 34
 KEY_PLANE_ROW = 8
 VECTOR_CLEARS = 5 * T // 16
 LAST_SPREAD_ROW = 32
+VECTOR_COLS = (H // 2, H // 8)
 LAST_GATHER_AFTER = 1
 
 
@@ -75,14 +76,10 @@ def tile_list_paged_softcap_logits_kernel(
             nc.sync.dma_start(out=table_words[a][:], in_=tab_words[a].rearrange("p t i -> p (t i)").bitcast(I32))
 
         def load_wq(a):
-            rows = wq[a * P * PACK : (a + 1) * P * PACK, :].rearrange("(p j) c -> p j c", j=PACK)
-            width = SIDE if a == LAST else H
-            for first in range(0, H, width):
-                name = "wq_raw%d_%d" % (a, first)
-                raw = keep.tile([P, PACK, width], F32, name=name, tag=name, align_bytes=64)
-                nc.sync.dma_start(out=raw[:], in_=rows[:, :, first : first + width])
-                for col in range(first, first + width, SIDE):
-                    wq_raw[a, col // SIDE] = raw[:, :, col - first : col - first + SIDE]
+            name = "wq_raw%d" % a
+            wq_raw[a] = keep.tile([P, PACK, H], F32, name=name, tag=name, align_bytes=64)
+            rows = wq[a * P * PACK : (a + 1) * P * PACK, :]
+            nc.sync.dma_start(out=wq_raw[a][:], in_=rows.rearrange("(p j) c -> p j c", j=PACK))
 
         def load_gate_plane(rows):
             by_row = wg_scales.rearrange("a (q r) t -> r q a t", r=SCALE_ROWS)
@@ -153,7 +150,11 @@ def tile_list_paged_softcap_logits_kernel(
         gather_table_words(LAST)
         make_identity(nc, ident[:])
 
-        wq_codes, wq_plane = {}, {}
+        code_tags = ["wq_codes0", "v_picked", "wq_codes2"]
+        wq_codes = [
+            keep.tile([P, H], U32, name="wq_codes%d" % a, tag=code_tags[a], align_bytes=64) for a in range(PASSES)
+        ]
+        wq_plane = [keep.tile([P, H], U8, name="wq_plane%d" % a, align_bytes=64) for a in range(PASSES)]
         h_codes = keep.tile([P, S], U32, name="h_codes", align_bytes=64)
         h_plane = keep.tile([P, S], U8, name="h_plane", tag="key_picked", align_bytes=64)
 
@@ -164,30 +165,28 @@ def tile_list_paged_softcap_logits_kernel(
                 key_words[g][:], key_table[:].bitcast(U32).indirect(key_list[:, g * cols : (g + 1) * cols])
             )
 
-        def quantize_wq(a, n):
-            rounded = keep.tile([P, SIDE, PACK], BF16, name="wq_bf16_%d_%d" % (a, n), align_bytes=64)
-            src = wq_raw[a, n].rearrange("p t (j u e) -> p j t u e", u=2, e=2)
-            dst = rounded[:].rearrange("p (u j e) t -> p j t u e", u=2, e=2)
-            if (a, n) == (LAST, 1):
-                nc.vector.tensor_copy(dst, src)
-            else:
-                nc.scalar.copy(dst, src)
-            name = "wq_codes%d_%d" % (a, n)
-            tag = "v_picked" if (a, n) == (1, 1) else name
-            wq_codes[a, n] = keep.tile([P, SIDE], U32, name=name, tag=tag, align_bytes=64)
-            wq_plane[a, n] = keep.tile([P, SIDE], U8, name="wq_plane%d_%d" % (a, n), align_bytes=64)
-            nc.vector.quantize_mx(
-                out=wq_codes[a, n][:].bitcast(FP8X4),
-                scales=wq_plane[a, n][:],
-                in_=rounded[:].rearrange("p c t -> p (c t)"),
-            )
+        def quantize_wq(a):
+            rounded = []
+            for n in range(2):
+                side = keep.tile([P, SIDE, PACK], BF16, name="wq_bf16_%d_%d" % (a, n), align_bytes=64)
+                src = wq_raw[a][:, :, n * SIDE : (n + 1) * SIDE].rearrange("p t (j u e) -> p j t u e", u=2, e=2)
+                dst = side[:].rearrange("p (u j e) t -> p j t u e", u=2, e=2)
+                groups = VECTOR_COLS[n] // 4 if a == LAST else 0
+                if groups > 0:
+                    nc.vector.tensor_copy(dst[:, :groups], src[:, :groups])
+                if groups < SIDE // 4:
+                    nc.scalar.copy(dst[:, groups:], src[:, groups:])
+                rounded.append(side)
+            for n in range(2):
+                cols = slice(n * SIDE, (n + 1) * SIDE)
+                nc.vector.quantize_mx(
+                    out=wq_codes[a][:, cols].bitcast(FP8X4),
+                    scales=wq_plane[a][:, cols],
+                    in_=rounded[n][:].rearrange("p c t -> p (c t)"),
+                )
 
         b_acc = [psum.tile([P, H], F32, tag="bank", name="b_acc%d" % c) for c in range(CHUNKS)]
-        a_acc = {
-            (n, pair): psum.tile([P, 2, SIDE], F32, tag="bank", name="a_acc%d_%d" % (n, pair))
-            for n in range(2)
-            for pair in range(2)
-        }
+        a_acc = [psum.tile([P, H], F32, tag="bank", name="a_acc%d" % c) for c in range(CHUNKS)]
 
         def project(acc, a, c, weight, weight_plane, start, stop):
             nc.tensor.matmul_mx(
@@ -204,35 +203,25 @@ def tile_list_paged_softcap_logits_kernel(
             for c in range(CHUNKS):
                 words = wg_codes[:, a, :].bitcast(FP4X4)
                 project(b_acc[c][:], a, c, words, wg_plane[:, a * H : (a + 1) * H], a == 0, a == LAST)
-            for n in range(2):
-                quantize_wq(a, n)
-                for c in range(CHUNKS):
-                    project(
-                        a_acc[n, c // 2][:, c % 2, :],
-                        a,
-                        c,
-                        wq_codes[a, n][:].bitcast(FP8X4),
-                        wq_plane[a, n][:],
-                        a == 0 and c % 2 == 0,
-                        a == LAST and c % 2 == 1,
-                    )
+            quantize_wq(a)
+            for c in range(CHUNKS):
+                project(a_acc[c][:], a, c, wq_codes[a][:].bitcast(FP8X4), wq_plane[a][:], a == 0, a == LAST)
 
         h_rows = [keep.tile([P, 2, H], BF16, name="h_rows%d" % pair, align_bytes=64) for pair in range(2)]
-        gate = keep.tile([P, CHUNKS, H], F32, name="gate", tag="wq_raw%d_0" % LAST, align_bytes=64)
+        gate = keep.tile([P, CHUNKS, H], F32, name="gate", tag="wq_raw%d" % LAST, align_bytes=64)
         for c in range(CHUNKS):
             nc.scalar.activation(
                 gate[:, c, :].rearrange("p (u j e) -> p u j e", u=2, e=2),
                 b_acc[c][:].rearrange("p (j u e) -> p u j e", u=2, e=2),
                 SIGMOID,
             )
-        for n in range(2):
-            for pair in range(2):
-                nc.vector.tensor_tensor(
-                    h_rows[pair][:].rearrange("p c (u n x) -> p n c u x", u=2, n=2)[:, n],
-                    a_acc[n, pair][:].rearrange("p c (u x) -> p c u x", u=2),
-                    gate[:, 2 * pair : 2 * pair + 2, :].rearrange("p c (u n x) -> p n c u x", u=2, n=2)[:, n],
-                    MULT,
-                )
+        for c in range(CHUNKS):
+            nc.vector.tensor_tensor(
+                h_rows[c // 2][:, c % 2, :].rearrange("p (u n x) -> p n u x", u=2, n=2),
+                a_acc[c][:].rearrange("p (n u x) -> p n u x", u=2, n=2),
+                gate[:, c, :].rearrange("p (u n x) -> p n u x", u=2, n=2),
+                MULT,
+            )
 
         def turn_half(n):
             turned = psum.tile([P, 2, 2, P], F32, tag="bank", name="turned%d" % n)

@@ -39,7 +39,7 @@ KEY_PLANE_ROW = 8
 VECTOR_CLEARS = 5 * T // 16
 LAST_SPREAD_ROW = 32
 VECTOR_COLS = (H // 2, H // 8)
-LAST_GATHER_AFTER = 1
+LAST_GATHER_AFTER = 2
 
 
 def tile_list_paged_softcap_logits_kernel(
@@ -207,7 +207,7 @@ def tile_list_paged_softcap_logits_kernel(
             for c in range(CHUNKS):
                 project(a_acc[c][:], a, c, wq_codes[a][:].bitcast(FP8X4), wq_plane[a][:], a == 0, a == LAST)
 
-        h_rows = [keep.tile([P, 2, H], BF16, name="h_rows%d" % pair, align_bytes=64) for pair in range(2)]
+        h_rows = [keep.tile([P, H], BF16, name="h_rows%d" % c, align_bytes=64) for c in range(CHUNKS)]
         gate = keep.tile([P, CHUNKS, H], F32, name="gate", tag="wq_raw%d" % LAST, align_bytes=64)
         for c in range(CHUNKS):
             nc.scalar.activation(
@@ -217,33 +217,34 @@ def tile_list_paged_softcap_logits_kernel(
             )
         for c in range(CHUNKS):
             nc.vector.tensor_tensor(
-                h_rows[c // 2][:, c % 2, :].rearrange("p (u n x) -> p n u x", u=2, n=2),
+                h_rows[c][:].rearrange("p (u n x) -> p n u x", u=2, n=2),
                 a_acc[c][:].rearrange("p (n u x) -> p n u x", u=2, n=2),
                 gate[:, c, :].rearrange("p (u n x) -> p n u x", u=2, n=2),
                 MULT,
             )
 
-        def turn_half(n):
-            turned = psum.tile([P, 2, 2, P], F32, tag="bank", name="turned%d" % n)
-            for c in range(2):
-                pairs = h_rows[n][:, c, :].bitcast(F32)
-                for u in range(2):
-                    nc.tensor.transpose(turned[:, c, u, :], pairs[:, u * P : (u + 1) * P], ident[:])
-            return turned
+        h_bf16 = [
+            keep.tile([P, HALF * PACK], BF16, name="h_bf16_%d" % n, tag="h_bf16_%d" % n, align_bytes=64)
+            for n in range(2)
+        ]
 
-        def quantize_half(n, turned):
-            h_bf16 = keep.tile([P, HALF * PACK], BF16, name="h_bf16_%d" % n, tag="h_bf16_%d" % n, align_bytes=64)
-            nc.scalar.copy(
-                h_bf16[:].bitcast(F32).rearrange("p (c j u) -> p c j u", c=2, u=2),
-                turned[:].rearrange("p c u j -> p c j u"),
-            )
+        def turn_chunk(c):
+            turned = psum.tile([P, 2, P], F32, tag="bank", name="turned%d" % c)
+            pairs = h_rows[c][:].bitcast(F32)
+            for u in range(2):
+                nc.tensor.transpose(turned[:, u, :], pairs[:, u * P : (u + 1) * P], ident[:])
+            words = h_bf16[c // 2][:].bitcast(F32)[:, (c % 2) * 2 * P : (c % 2 + 1) * 2 * P]
+            nc.scalar.copy(words.rearrange("p (j u) -> p j u", u=2), turned[:].rearrange("p u j -> p j u"))
+
+        def quantize_half(n):
             cols = slice(n * HALF, (n + 1) * HALF)
-            nc.vector.quantize_mx(out=h_codes[:, cols].bitcast(FP8X4), scales=h_plane[:, cols], in_=h_bf16[:])
+            nc.vector.quantize_mx(out=h_codes[:, cols].bitcast(FP8X4), scales=h_plane[:, cols], in_=h_bf16[n][:])
 
-        halves = [turn_half(n) for n in range(2)]
+        for c in range(CHUNKS):
+            turn_chunk(c)
         gather_key_words(0, "key_words0")
-        quantize_half(0, halves[0])
-        quantize_half(1, halves[1])
+        quantize_half(0)
+        quantize_half(1)
         gather_key_words(1, "h_bf16_0")
 
         def logits(i, queries):
@@ -261,7 +262,6 @@ def tile_list_paged_softcap_logits_kernel(
             return z
 
         for i in range(KEY_TILES):
-            under_gather = i - LAST_GATHER_AFTER in (1, 2)
             if i == LAST_GATHER_AFTER + 1:
                 gather_key_words(2, "sig%d" % LAST_GATHER_AFTER)
             sig = keep.tile([P, S], F32, name="sig%d" % i, tag="sig%d" % i, align_bytes=64)
@@ -270,8 +270,8 @@ def tile_list_paged_softcap_logits_kernel(
                 queries = slice(first, first + width)
                 capped = keep.tile([P, width], F32, name="capped%d_%d" % (i, first))
                 nc.scalar.activation(sig[:, queries], logits(i, queries)[:], SIGMOID, scale=2.0 / CAP)
-                if under_gather:
-                    nc.gpsimd.tensor_scalar(capped[:], sig[:], 2.0 * CAP, -CAP, MULT, ADD)
+                if (i, first) in ((0, 0), (LAST_GATHER_AFTER + 1, 0)):
+                    nc.gpsimd.tensor_scalar(capped[:], sig[:, queries], 2.0 * CAP, -CAP, MULT, ADD)
                 else:
                     nc.vector.tensor_scalar(capped[:], sig[:, queries], 2.0 * CAP, shift[:], MULT, ADD)
                 queue = nc.scalar if i >= 5 and i % 2 == 1 else nc.sync

@@ -40,6 +40,8 @@ VECTOR_CLEARS = 5 * T // 16
 LAST_SPREAD_ROW = 32
 VECTOR_COLS = (H // 2, H // 8)
 LAST_GATHER_AFTER = 2
+SHIFT_TILE = 8
+WARM_AFTER = (1, 2, 3)
 
 
 def tile_list_paged_softcap_logits_kernel(
@@ -48,7 +50,7 @@ def tile_list_paged_softcap_logits_kernel(
     nc = tc.nc
     with ExitStack() as ctx:
         keep = ctx.enter_context(tc.tile_pool(name="keep", bufs=1))
-        psum = ctx.enter_context(tc.psum_pool(name="psum", bufs=8))
+        psum = ctx.enter_context(tc.psum_pool(name="psum", bufs=1))
 
         token_list = keep.tile([P, S // LIST_ROWS], U16, name="token_list")
         key_list = keep.tile([P, S2 // LIST_ROWS], U16, name="key_list")
@@ -185,8 +187,8 @@ def tile_list_paged_softcap_logits_kernel(
                     in_=rounded[n][:].rearrange("p c t -> p (c t)"),
                 )
 
-        b_acc = [psum.tile([P, H], F32, tag="bank", name="b_acc%d" % c) for c in range(CHUNKS)]
-        a_acc = [psum.tile([P, H], F32, tag="bank", name="a_acc%d" % c) for c in range(CHUNKS)]
+        b_acc = [psum.tile([P, H], F32, tag="bank%d" % c, name="b_acc%d" % c) for c in range(CHUNKS)]
+        a_acc = [psum.tile([P, H], F32, tag="bank%d" % (CHUNKS + c), name="a_acc%d" % c) for c in range(CHUNKS)]
 
         def project(acc, a, c, weight, weight_plane, start, stop):
             nc.tensor.matmul_mx(
@@ -229,7 +231,7 @@ def tile_list_paged_softcap_logits_kernel(
         ]
 
         def turn_chunk(c):
-            turned = psum.tile([P, 2, P], F32, tag="bank", name="turned%d" % c)
+            turned = psum.tile([P, 2, P], F32, tag="bank%d" % c, name="turned%d" % c)
             pairs = h_rows[c][:].bitcast(F32)
             for u in range(2):
                 nc.tensor.transpose(turned[:, u, :], pairs[:, u * P : (u + 1) * P], ident[:])
@@ -242,14 +244,17 @@ def tile_list_paged_softcap_logits_kernel(
 
         for c in range(CHUNKS):
             turn_chunk(c)
+        for c in WARM_AFTER:
+            unread = psum.tile([P, H], F32, tag="bank%d" % (CHUNKS + c), name="unread%d" % c)
+            project(unread[:], LAST, c, wq_codes[LAST][:].bitcast(FP8X4), wq_plane[LAST][:], True, True)
         gather_key_words(0, "key_words0")
         quantize_half(0)
         quantize_half(1)
         gather_key_words(1, "h_bf16_0")
 
-        def logits(i, queries):
+        def logits(i, queries, bank):
             keys = slice((i % TILES_PER_PIECE) * P, (i % TILES_PER_PIECE + 1) * P)
-            z = psum.tile([P, queries.stop - queries.start], F32, tag="bank", name="z")
+            z = psum.tile([P, queries.stop - queries.start], F32, tag="bank%d" % bank, name="z")
             nc.tensor.matmul_mx(
                 out=z[:],
                 lhsT=key_words[i // TILES_PER_PIECE][:, keys].bitcast(FP8X4),
@@ -261,6 +266,7 @@ def tile_list_paged_softcap_logits_kernel(
             )
             return z
 
+        bank = 0
         for i in range(KEY_TILES):
             if i == LAST_GATHER_AFTER + 1:
                 gather_key_words(2, "sig%d" % LAST_GATHER_AFTER)
@@ -269,10 +275,12 @@ def tile_list_paged_softcap_logits_kernel(
             for first in range(0, S, width):
                 queries = slice(first, first + width)
                 capped = keep.tile([P, width], F32, name="capped%d_%d" % (i, first))
-                nc.scalar.activation(sig[:, queries], logits(i, queries)[:], SIGMOID, scale=2.0 / CAP)
+                nc.scalar.activation(sig[:, queries], logits(i, queries, bank)[:], SIGMOID, scale=2.0 / CAP)
+                bank = (bank + 1) % (2 * CHUNKS)
                 if (i, first) in ((0, 0), (LAST_GATHER_AFTER + 1, 0)):
                     nc.gpsimd.tensor_scalar(capped[:], sig[:, queries], 2.0 * CAP, -CAP, MULT, ADD)
                 else:
-                    nc.vector.tensor_scalar(capped[:], sig[:, queries], 2.0 * CAP, shift[:], MULT, ADD)
+                    offset = shift[:] if i == SHIFT_TILE else -CAP
+                    nc.vector.tensor_scalar(capped[:], sig[:, queries], 2.0 * CAP, offset, MULT, ADD)
                 queue = nc.scalar if i >= 5 and i % 2 == 1 else nc.sync
                 queue.dma_start(out=out[i * P : (i + 1) * P, queries], in_=capped[:])

@@ -38,10 +38,9 @@ KEY_SPREAD_ROW = 34
 KEY_PLANE_ROW = 8
 VECTOR_CLEARS = 5 * T // 16
 LAST_SPREAD_ROW = 32
-VECTOR_COLS = (H // 2, H // 8)
+VECTOR_COLS = (H // 2, 3 * H // 16)
 LAST_GATHER_AFTER = 2
 SHIFT_TILE = 8
-WARM_AFTER = (1, 2, 3)
 
 
 def tile_list_paged_softcap_logits_kernel(
@@ -207,9 +206,19 @@ def tile_list_paged_softcap_logits_kernel(
                 project(b_acc[c][:], a, c, words, wg_plane[:, a * H : (a + 1) * H], a == 0, a == LAST)
             quantize_wq(a)
             for c in range(CHUNKS):
-                project(a_acc[c][:], a, c, wq_codes[a][:].bitcast(FP8X4), wq_plane[a][:], a == 0, a == LAST)
+                width = SIDE if (a, c) == (LAST, 0) else H
+                for first in range(0, H, width):
+                    cols = slice(first, first + width)
+                    codes = wq_codes[a][:, cols].bitcast(FP8X4)
+                    closes = a == LAST and cols.stop == H
+                    project(a_acc[c][:, cols], a, c, codes, wq_plane[a][:, cols], a == 0, closes)
 
-        h_rows = [keep.tile([P, H], BF16, name="h_rows%d" % c, align_bytes=64) for c in range(CHUNKS)]
+        h_rows = [
+            [keep.tile([P, H // 2], BF16, name="h_rows%d_%d" % (c, u), align_bytes=64) for u in range(2)]
+            if c == CHUNKS - 1
+            else keep.tile([P, 2, H // 2], BF16, name="h_rows%d" % c, align_bytes=64)
+            for c in range(CHUNKS)
+        ]
         gate = keep.tile([P, CHUNKS, H], F32, name="gate", tag="wq_raw%d" % LAST, align_bytes=64)
         for c in range(CHUNKS):
             nc.scalar.activation(
@@ -217,11 +226,18 @@ def tile_list_paged_softcap_logits_kernel(
                 b_acc[c][:].rearrange("p (j u e) -> p u j e", u=2, e=2),
                 SIGMOID,
             )
-        for c in range(CHUNKS):
+        for c in range(CHUNKS - 1):
             nc.vector.tensor_tensor(
-                h_rows[c][:].rearrange("p (u n x) -> p n u x", u=2, n=2),
+                h_rows[c][:].rearrange("p u (n x) -> p n u x", n=2),
                 a_acc[c][:].rearrange("p (n u x) -> p n u x", u=2, n=2),
                 gate[:, c, :].rearrange("p (u n x) -> p n u x", u=2, n=2),
+                MULT,
+            )
+        for u in range(2):
+            nc.vector.tensor_tensor(
+                h_rows[-1][u][:].rearrange("p (n x) -> p n x", n=2),
+                a_acc[-1][:].rearrange("p (n u x) -> p u n x", u=2, n=2)[:, u],
+                gate[:, CHUNKS - 1, :].rearrange("p (u n x) -> p u n x", u=2, n=2)[:, u],
                 MULT,
             )
 
@@ -232,9 +248,9 @@ def tile_list_paged_softcap_logits_kernel(
 
         def turn_chunk(c):
             turned = psum.tile([P, 2, P], F32, tag="bank%d" % c, name="turned%d" % c)
-            pairs = h_rows[c][:].bitcast(F32)
             for u in range(2):
-                nc.tensor.transpose(turned[:, u, :], pairs[:, u * P : (u + 1) * P], ident[:])
+                half = h_rows[c][u][:] if c == CHUNKS - 1 else h_rows[c][:, u, :]
+                nc.tensor.transpose(turned[:, u, :], half.bitcast(F32), ident[:])
             words = h_bf16[c // 2][:].bitcast(F32)[:, (c % 2) * 2 * P : (c % 2 + 1) * 2 * P]
             nc.scalar.copy(words.rearrange("p (j u) -> p j u", u=2), turned[:].rearrange("p u j -> p j u"))
 
@@ -244,9 +260,6 @@ def tile_list_paged_softcap_logits_kernel(
 
         for c in range(CHUNKS):
             turn_chunk(c)
-        for c in WARM_AFTER:
-            unread = psum.tile([P, H], F32, tag="bank%d" % (CHUNKS + c), name="unread%d" % c)
-            project(unread[:], LAST, c, wq_codes[LAST][:].bitcast(FP8X4), wq_plane[LAST][:], True, True)
         gather_key_words(0, "key_words0")
         quantize_half(0)
         quantize_half(1)
@@ -266,21 +279,27 @@ def tile_list_paged_softcap_logits_kernel(
             )
             return z
 
-        bank = 0
+        def cap_and_store(i, sig, queries):
+            capped = keep.tile([P, queries.stop - queries.start], F32, name="capped%d_%d" % (i, queries.start))
+            if (i, queries.start) in ((0, 0), (LAST_GATHER_AFTER + 1, 0)):
+                nc.gpsimd.tensor_scalar(capped[:], sig[:, queries], 2.0 * CAP, -CAP, MULT, ADD)
+            else:
+                offset = shift[:] if i == SHIFT_TILE else -CAP
+                nc.vector.tensor_scalar(capped[:], sig[:, queries], 2.0 * CAP, offset, MULT, ADD)
+            queue = nc.scalar if i >= 5 and i % 2 == 1 else nc.sync
+            queue.dma_start(out=out[i * P : (i + 1) * P, queries], in_=capped[:])
+
+        bank = CHUNKS
         for i in range(KEY_TILES):
             if i == LAST_GATHER_AFTER + 1:
                 gather_key_words(2, "sig%d" % LAST_GATHER_AFTER)
             sig = keep.tile([P, S], F32, name="sig%d" % i, tag="sig%d" % i, align_bytes=64)
-            width = HALF if i == 0 else S
+            width = HALF if i < 2 else S
             for first in range(0, S, width):
                 queries = slice(first, first + width)
-                capped = keep.tile([P, width], F32, name="capped%d_%d" % (i, first))
                 nc.scalar.activation(sig[:, queries], logits(i, queries, bank)[:], SIGMOID, scale=2.0 / CAP)
                 bank = (bank + 1) % (2 * CHUNKS)
-                if (i, first) in ((0, 0), (LAST_GATHER_AFTER + 1, 0)):
-                    nc.gpsimd.tensor_scalar(capped[:], sig[:, queries], 2.0 * CAP, -CAP, MULT, ADD)
-                else:
-                    offset = shift[:] if i == SHIFT_TILE else -CAP
-                    nc.vector.tensor_scalar(capped[:], sig[:, queries], 2.0 * CAP, offset, MULT, ADD)
-                queue = nc.scalar if i >= 5 and i % 2 == 1 else nc.sync
-                queue.dma_start(out=out[i * P : (i + 1) * P, queries], in_=capped[:])
+                if i == 0:
+                    cap_and_store(i, sig, queries)
+            if i > 0:
+                cap_and_store(i, sig, slice(0, S))

@@ -32,15 +32,12 @@ HALF = S // 2
 SIDE = H // 2
 KEY_TILES = S2 // P
 KEY_PIECE = 512
-TILES_PER_PIECE = KEY_PIECE // P
 TABLE_SPREAD_ROW = 33
 KEY_SPREAD_ROW = 34
 KEY_PLANE_ROW = 8
 VECTOR_CLEARS = 5 * T // 16
 LAST_SPREAD_ROW = 32
 VECTOR_COLS = (H // 2, 3 * H // 16)
-LAST_GATHER_AFTER = 2
-SHIFT_TILE = 8
 
 
 def tile_list_paged_softcap_logits_kernel(
@@ -159,12 +156,12 @@ def tile_list_paged_softcap_logits_kernel(
         h_codes = keep.tile([P, S], U32, name="h_codes", align_bytes=64)
         h_plane = keep.tile([P, S], U8, name="h_plane", tag="key_picked", align_bytes=64)
 
-        def gather_key_words(g, tag):
-            key_words[g] = keep.tile([P, KEY_PIECE], U32, name="key_words%d" % g, tag=tag, align_bytes=64)
-            cols = KEY_PIECE // LIST_ROWS
-            nc.vector.tensor_copy(
-                key_words[g][:], key_table[:].bitcast(U32).indirect(key_list[:, g * cols : (g + 1) * cols])
-            )
+        def gather_key_words(first, count, tag):
+            words = keep.tile([P, count], U32, name="key_words%d" % first, tag=tag, align_bytes=64)
+            offsets = key_list[:, first // LIST_ROWS : (first + count) // LIST_ROWS]
+            nc.vector.tensor_copy(words[:], key_table[:].bitcast(U32).indirect(offsets))
+            for n in range(count // P):
+                key_words[first // P + n] = words[:, n * P : (n + 1) * P]
 
         def quantize_wq(a):
             rounded = []
@@ -260,17 +257,17 @@ def tile_list_paged_softcap_logits_kernel(
 
         for c in range(CHUNKS):
             turn_chunk(c)
-        gather_key_words(0, "key_words0")
+        gather_key_words(0, KEY_PIECE, "key_words0")
         quantize_half(0)
         quantize_half(1)
-        gather_key_words(1, "h_bf16_0")
+        gather_key_words(KEY_PIECE, KEY_PIECE, "h_bf16_0")
+        gather_key_words(2 * KEY_PIECE, KEY_PIECE, "h_bf16_1")
 
         def logits(i, queries, bank):
-            keys = slice((i % TILES_PER_PIECE) * P, (i % TILES_PER_PIECE + 1) * P)
             z = psum.tile([P, queries.stop - queries.start], F32, tag="bank%d" % bank, name="z")
             nc.tensor.matmul_mx(
                 out=z[:],
-                lhsT=key_words[i // TILES_PER_PIECE][:, keys].bitcast(FP8X4),
+                lhsT=key_words[i].bitcast(FP8X4),
                 lhsT_scale=key_plane[KEY_PLANE_ROW:P, i * P : (i + 1) * P],
                 rhs=h_codes[:, queries].bitcast(FP8X4),
                 rhs_scale=h_plane[:, queries],
@@ -281,18 +278,15 @@ def tile_list_paged_softcap_logits_kernel(
 
         def cap_and_store(i, sig, queries):
             capped = keep.tile([P, queries.stop - queries.start], F32, name="capped%d_%d" % (i, queries.start))
-            if (i, queries.start) in ((0, 0), (LAST_GATHER_AFTER + 1, 0)):
+            if i == 0:
                 nc.gpsimd.tensor_scalar(capped[:], sig[:, queries], 2.0 * CAP, -CAP, MULT, ADD)
             else:
-                offset = shift[:] if i == SHIFT_TILE else -CAP
-                nc.vector.tensor_scalar(capped[:], sig[:, queries], 2.0 * CAP, offset, MULT, ADD)
+                nc.vector.tensor_scalar(capped[:], sig[:, queries], 2.0 * CAP, shift[:], MULT, ADD)
             queue = nc.scalar if i >= 5 and i % 2 == 1 else nc.sync
             queue.dma_start(out=out[i * P : (i + 1) * P, queries], in_=capped[:])
 
         bank = CHUNKS
         for i in range(KEY_TILES):
-            if i == LAST_GATHER_AFTER + 1:
-                gather_key_words(2, "sig%d" % LAST_GATHER_AFTER)
             sig = keep.tile([P, S], F32, name="sig%d" % i, tag="sig%d" % i, align_bytes=64)
             width = HALF if i < 2 else S
             for first in range(0, S, width):

@@ -31,13 +31,12 @@ CHUNKS = S // P
 HALF = S // 2
 SIDE = H // 2
 KEY_TILES = S2 // P
-KEY_PIECE = 512
-TABLE_SPREAD_ROW = 33
+KEY_PIECE = 2 * P
+TABLE_SPREAD_ROW = 32
+LAST_SPREAD_ROW = 33
 KEY_SPREAD_ROW = 34
 KEY_PLANE_ROW = 8
-VECTOR_CLEARS = 5 * T // 16
-LAST_SPREAD_ROW = 32
-VECTOR_COLS = (H // 2, 3 * H // 16)
+KEY_TURN = 1024
 
 
 def tile_list_paged_softcap_logits_kernel(
@@ -48,36 +47,45 @@ def tile_list_paged_softcap_logits_kernel(
         keep = ctx.enter_context(tc.tile_pool(name="keep", bufs=1))
         psum = ctx.enter_context(tc.psum_pool(name="psum", bufs=1))
 
+        def sbuf(name, shape, dtype, on=None):
+            return keep.tile(shape, dtype, name=name, tag=on or name, align_bytes=64)
+
         token_list = keep.tile([P, S // LIST_ROWS], U16, name="token_list")
         key_list = keep.tile([P, S2 // LIST_ROWS], U16, name="key_list")
-        v_window = keep.tile([P, LAST * T], U8, name="v_window", tag="v_window", align_bytes=64)
-        v_picked = keep.tile([P, LAST * S], U8, name="v_picked", tag="v_picked", align_bytes=64)
-        v_plane = keep.tile([P, PASSES * S], U8, name="v_plane", align_bytes=64)
-        key_plane = keep.tile([P, S2], U8, name="key_plane", align_bytes=64)
-        key_window = keep.tile([P, T2], U8, name="key_window", align_bytes=64)
-        wg_plane = keep.tile([P, PASSES * H], U8, name="wg_plane", align_bytes=64)
-        table_words, wq_raw, key_words = {}, {}, {}
-        ident = keep.tile([P, P], F32, name="ident", align_bytes=64)
-        zero = keep.tile([P, 1], F32, name="zero")
-        centre = keep.tile([P, 1], F32, name="centre")
+        v_window = sbuf("v_window", [P, T], U8)
+        v_picked = sbuf("v_picked", [P, S], U8)
+        v_plane = sbuf("v_plane", [P, PASSES * S], U8)
+        wg_plane = sbuf("wg_plane", [P, PASSES * H], U8)
+        key_window = sbuf("key_window", [P, T2], U8)
+        planes = sbuf("planes", [P, HALF + S2], U8)
+        wg_codes = [sbuf("wg_early", [P, LAST, 2 * H], U8), sbuf("wg_last", [P, 1, 2 * H], U8)]
+        table_words = [sbuf("table_words%d" % a, [P, T], I32) for a in range(PASSES)]
+        wq_raw = [sbuf("wq_raw%d" % a, [P, PACK, H], F32) for a in range(PASSES)]
+        key_table = sbuf("key_table", [P, T2], I32)
+        ident = sbuf("ident", [P, P], F32)
+        zero = sbuf("zero", [P, 1], F32)
+        centre = sbuf("centre", [P, 1], F32)
+        shift = sbuf("shift", [P, 1], F32)
 
-        nc.vector.memset(v_window[:].bitcast(I32)[:, :VECTOR_CLEARS], 0)
-        nc.gpsimd.memset(v_window[:].bitcast(I32)[:, VECTOR_CLEARS:], 0)
+        nc.vector.memset(v_window[:].bitcast(I32), 0)
         nc.vector.memset(zero[:], 0.0)
         nc.vector.memset(key_window[:].bitcast(I32), 0)
         nc.gpsimd.memset(wg_plane[:].bitcast(I32), 0)
-        nc.vector.memset(v_plane[:].bitcast(I32), 0)
-        nc.vector.memset(key_plane[:].bitcast(I32), 0)
+        nc.gpsimd.memset(v_plane[:].bitcast(I32), 0)
+        nc.gpsimd.memset(planes[:].bitcast(I32), 0)
+        nc.scalar.activation(centre[:], zero[:], SIGMOID)
+        nc.gpsimd.tensor_scalar(shift[:], centre[:], -2.0 * CAP, 0.0, MULT, ADD)
+        make_identity(nc, ident[:])
 
-        def load_table_words(a):
-            table_words[a] = keep.tile([P, T], I32, name="table_words%d" % a, tag="table_words%d" % a, align_bytes=64)
-            nc.sync.dma_start(out=table_words[a][:], in_=tab_words[a].rearrange("p t i -> p (t i)").bitcast(I32))
+        def load_words(tile, words):
+            nc.sync.dma_start(out=tile[:], in_=words.rearrange("p t i -> p (t i)").bitcast(I32))
 
         def load_wq(a):
-            name = "wq_raw%d" % a
-            wq_raw[a] = keep.tile([P, PACK, H], F32, name=name, tag=name, align_bytes=64)
             rows = wq[a * P * PACK : (a + 1) * P * PACK, :]
             nc.sync.dma_start(out=wq_raw[a][:], in_=rows.rearrange("(p j) c -> p j c", j=PACK))
+
+        def load_gate_words(tile, words):
+            nc.sync.dma_start(out=tile[:].bitcast(I32), in_=words.rearrange("a p c -> p a c").bitcast(I32))
 
         def load_gate_plane(rows):
             by_row = wg_scales.rearrange("a (q r) t -> r q a t", r=SCALE_ROWS)
@@ -85,200 +93,175 @@ def tile_list_paged_softcap_logits_kernel(
             for r in rows:
                 nc.sync.dma_start(out=dst[r:P:QUADRANT], in_=by_row[r].bitcast(I32))
 
-        word_tags = ["v_window", "v_words1", "v_words2"]
-        v_words = [
-            keep.tile([P, S], U32, name="v_words%d" % a, tag=word_tags[a], align_bytes=64) for a in range(PASSES)
-        ]
+        def spread_scale_rows(window, scales, first, step):
+            rows = scales.rearrange("a q t -> (a q) t").bitcast(I32)
+            nc.sync.dma_start(out=window[first : first + rows.shape[0] * step : step, :].bitcast(I32), in_=rows)
 
-        def gather_table_words(a):
-            width = HALF if a == LAST else S
-            for first in range(0, S, width):
-                offsets = token_list[:, first // LIST_ROWS : (first + width) // LIST_ROWS]
-                nc.vector.tensor_copy(
-                    v_words[a][:, first : first + width], table_words[a][:].bitcast(U32).indirect(offsets)
-                )
-
-        def spread_scale_rows(window, scales, first):
-            passes = scales.shape[0]
-            dst = window.bitcast(I32).rearrange("p (a t) -> p a t", a=passes)
-            nc.sync.dma_start(out=dst[first : first + 16 * SPREAD : SPREAD], in_=scales.rearrange("a q t -> q a t").bitcast(I32))
-
-        def place_scale_rows(plane, first_row, picked, first):
+        def place_scale_rows(plane, first_row, picked, first, step):
             for r in range(SCALE_ROWS):
                 nc.sync.dma_start(
                     out=plane[first_row + r : P : QUADRANT, :].bitcast(I32),
-                    in_=picked[first + SPREAD * r : first + 16 * SPREAD : SCALE_ROWS * SPREAD, :].bitcast(I32),
+                    in_=picked[first + step * r : first + 16 * step : SCALE_ROWS * step, :].bitcast(I32),
                 )
 
-        wg_codes = keep.tile([P, PASSES, 2 * H], U8, name="wg_codes", align_bytes=64)
-        load_table_words(0)
-        nc.sync.dma_start(token_list[:], offs)
-        spread_scale_rows(v_window[:], tab_scales[:LAST], TABLE_SPREAD_ROW)
-        spread_scale_rows(v_window[:, :T], tab_scales[LAST:], LAST_SPREAD_ROW)
-        load_gate_plane(range(SCALE_ROWS - 1))
-        load_wq(0)
-        load_gate_plane(range(SCALE_ROWS - 1, SCALE_ROWS))
-        nc.scalar.activation(centre[:], zero[:], SIGMOID)
-        shift = keep.tile([P, 1], F32, name="shift")
-        nc.gpsimd.tensor_scalar(shift[:], centre[:], -2.0 * CAP, 0.0, MULT, ADD)
-        nc.sync.dma_start(key_list[:], offs2)
-        spread_scale_rows(key_window[:], tab2_scales, KEY_SPREAD_ROW)
-        nc.sync.dma_start(out=wg_codes[:].bitcast(I32), in_=wg_words.rearrange("a p c -> p a c").bitcast(I32))
-        load_table_words(1)
-        for n in range(LAST):
-            nc.vector.tensor_copy(
-                v_picked[:, n * S : (n + 1) * S], v_window[:, n * T : (n + 1) * T].indirect(token_list[:])
-            )
-        place_scale_rows(v_plane[:, : LAST * S], 0, v_picked[:], TABLE_SPREAD_ROW)
-        load_wq(1)
-        load_table_words(LAST)
-        place_scale_rows(v_plane[:, LAST * S :], 0, v_picked[:, :S], LAST_SPREAD_ROW)
-        load_wq(LAST)
-        gather_table_words(0)
-        first_cols = KEY_PIECE // LIST_ROWS
-        key_picked = keep.tile([P, KEY_PIECE], U8, name="key_picked", tag="key_picked", align_bytes=64)
-        nc.vector.tensor_copy(key_picked[:], key_window[:].indirect(key_list[:, :first_cols]))
-        gather_table_words(1)
-        rest_picked = keep.tile([P, S2 - KEY_PIECE], U8, name="rest_picked", tag="table_words1", align_bytes=64)
-        nc.vector.tensor_copy(rest_picked[:], key_window[:].indirect(key_list[:, first_cols:]))
-        key_table = keep.tile([P, T2], I32, name="key_table", align_bytes=64)
-        nc.sync.dma_start(out=key_table[:], in_=tab2_words[0].rearrange("p t i -> p (t i)").bitcast(I32))
-        place_scale_rows(key_plane[:, :KEY_PIECE], KEY_PLANE_ROW, key_picked, KEY_SPREAD_ROW)
-        place_scale_rows(key_plane[:, KEY_PIECE:], KEY_PLANE_ROW, rest_picked, KEY_SPREAD_ROW)
-        gather_table_words(LAST)
-        make_identity(nc, ident[:])
+        def gather(dst, window, entries, first, count):
+            offsets = entries[:, first // LIST_ROWS : (first + count) // LIST_ROWS]
+            nc.vector.tensor_copy(dst, window.indirect(offsets))
 
-        code_tags = ["wq_codes0", "v_picked", "wq_codes2"]
-        wq_codes = [
-            keep.tile([P, H], U32, name="wq_codes%d" % a, tag=code_tags[a], align_bytes=64) for a in range(PASSES)
-        ]
-        wq_plane = [keep.tile([P, H], U8, name="wq_plane%d" % a, align_bytes=64) for a in range(PASSES)]
-        h_codes = keep.tile([P, S], U32, name="h_codes", align_bytes=64)
-        h_plane = keep.tile([P, S], U8, name="h_plane", tag="key_picked", align_bytes=64)
+        def round_side(a, n, engine_copy):
+            side = sbuf("wq_bf16_%d_%d" % (a, n), [P, SIDE, PACK], BF16)
+            src = wq_raw[a][:, :, n * SIDE : (n + 1) * SIDE].rearrange("p t (j u e) -> p j t u e", u=2, e=2)
+            engine_copy(side[:].rearrange("p (u j e) t -> p j t u e", u=2, e=2), src)
+            return side
 
-        def gather_key_words(first, count, tag):
-            words = keep.tile([P, count], U32, name="key_words%d" % first, tag=tag, align_bytes=64)
-            offsets = key_list[:, first // LIST_ROWS : (first + count) // LIST_ROWS]
-            nc.vector.tensor_copy(words[:], key_table[:].bitcast(U32).indirect(offsets))
-            for n in range(count // P):
-                key_words[first // P + n] = words[:, n * P : (n + 1) * P]
+        wq_codes, wq_plane, v_words = {}, {}, {}
 
-        def quantize_wq(a):
-            rounded = []
-            for n in range(2):
-                side = keep.tile([P, SIDE, PACK], BF16, name="wq_bf16_%d_%d" % (a, n), align_bytes=64)
-                src = wq_raw[a][:, :, n * SIDE : (n + 1) * SIDE].rearrange("p t (j u e) -> p j t u e", u=2, e=2)
-                dst = side[:].rearrange("p (u j e) t -> p j t u e", u=2, e=2)
-                groups = VECTOR_COLS[n] // 4 if a == LAST else 0
-                if groups > 0:
-                    nc.vector.tensor_copy(dst[:, :groups], src[:, :groups])
-                if groups < SIDE // 4:
-                    nc.scalar.copy(dst[:, groups:], src[:, groups:])
-                rounded.append(side)
-            for n in range(2):
+        def quantize_sides(a, sides, on):
+            wq_codes[a] = sbuf("wq_codes%d" % a, [P, H], U32, on)
+            wq_plane[a] = sbuf("wq_plane%d" % a, [P, H], U8)
+            for n, side in sides:
                 cols = slice(n * SIDE, (n + 1) * SIDE)
                 nc.vector.quantize_mx(
                     out=wq_codes[a][:, cols].bitcast(FP8X4),
                     scales=wq_plane[a][:, cols],
-                    in_=rounded[n][:].rearrange("p c t -> p (c t)"),
+                    in_=side[:].rearrange("p c t -> p (c t)"),
                 )
 
         b_acc = [psum.tile([P, H], F32, tag="bank%d" % c, name="b_acc%d" % c) for c in range(CHUNKS)]
         a_acc = [psum.tile([P, H], F32, tag="bank%d" % (CHUNKS + c), name="a_acc%d" % c) for c in range(CHUNKS)]
 
-        def project(acc, a, c, weight, weight_plane, start, stop):
+        def project(acc, a, c, weight, weight_plane):
             nc.tensor.matmul_mx(
-                out=acc,
+                out=acc[:],
                 lhsT=v_words[a][:, c * P : (c + 1) * P].bitcast(FP8X4),
                 lhsT_scale=v_plane[:, a * S + c * P : a * S + (c + 1) * P],
                 rhs=weight,
                 rhs_scale=weight_plane,
-                start=start,
-                stop=stop,
+                start=a == 0,
+                stop=a == LAST,
             )
 
-        for a in range(PASSES):
-            for c in range(CHUNKS):
-                words = wg_codes[:, a, :].bitcast(FP4X4)
-                project(b_acc[c][:], a, c, words, wg_plane[:, a * H : (a + 1) * H], a == 0, a == LAST)
-            quantize_wq(a)
-            for c in range(CHUNKS):
-                width = SIDE if (a, c) == (LAST, 0) else H
-                for first in range(0, H, width):
-                    cols = slice(first, first + width)
-                    codes = wq_codes[a][:, cols].bitcast(FP8X4)
-                    closes = a == LAST and cols.stop == H
-                    project(a_acc[c][:, cols], a, c, codes, wq_plane[a][:, cols], a == 0, closes)
+        def project_gate(a, c):
+            project(b_acc[c], a, c, wg_codes[a // LAST][:, a % LAST, :].bitcast(FP4X4), wg_plane[:, a * H : (a + 1) * H])
 
-        h_rows = [
-            [keep.tile([P, H // 2], BF16, name="h_rows%d_%d" % (c, u), align_bytes=64) for u in range(2)]
-            if c == CHUNKS - 1
-            else keep.tile([P, 2, H // 2], BF16, name="h_rows%d" % c, align_bytes=64)
-            for c in range(CHUNKS)
-        ]
-        gate = keep.tile([P, CHUNKS, H], F32, name="gate", tag="wq_raw%d" % LAST, align_bytes=64)
+        def project_query(a, c):
+            project(a_acc[c], a, c, wq_codes[a][:].bitcast(FP8X4), wq_plane[a][:])
+
+        load_words(table_words[0], tab_words[0])
+        nc.sync.dma_start(token_list[:], offs)
+        spread_scale_rows(v_window, tab_scales[:LAST], TABLE_SPREAD_ROW, 2)
+        spread_scale_rows(v_window, tab_scales[LAST:], LAST_SPREAD_ROW, SPREAD)
+        nc.sync.dma_start(key_list[:], offs2)
+        spread_scale_rows(key_window, tab2_scales, KEY_SPREAD_ROW, SPREAD)
+        load_wq(0)
+        load_gate_words(wg_codes[0], wg_words[:LAST])
+        load_gate_plane(range(SCALE_ROWS))
+        load_wq(1)
+        v_words[0] = sbuf("v_words0", [P, S], U32)
+        gather(v_words[0][:], table_words[0][:].bitcast(U32), token_list, 0, S)
+        gather(v_picked[:], v_window[:], token_list, 0, S)
+        place_scale_rows(v_plane[:, :S], 0, v_picked, TABLE_SPREAD_ROW, 2)
+        load_words(table_words[1], tab_words[1])
+        place_scale_rows(v_plane[:, S : 2 * S], 0, v_picked, TABLE_SPREAD_ROW + 32, 2)
+        load_wq(LAST)
+        load_words(table_words[LAST], tab_words[LAST])
+        load_gate_words(wg_codes[1], wg_words[LAST:])
+        place_scale_rows(v_plane[:, LAST * S :], 0, v_picked, LAST_SPREAD_ROW, SPREAD)
+        load_words(key_table, tab2_words[0])
+
+        quantize_sides(0, [(n, round_side(0, n, nc.scalar.copy)) for n in range(2)], None)
         for c in range(CHUNKS):
+            project_gate(0, c)
+        for c in range(CHUNKS):
+            project_query(0, c)
+
+        key_picked = sbuf("key_picked", [P, S2], U8)
+        gather(key_picked[:, S2 - KEY_TURN :], key_window[:], key_list, 0, KEY_TURN)
+        gather(key_picked[:, : S2 - KEY_TURN], key_window[:], key_list, KEY_TURN, S2 - KEY_TURN)
+        place_scale_rows(planes[:, HALF:], KEY_PLANE_ROW, key_picked, KEY_SPREAD_ROW, SPREAD)
+
+        v_words[1] = sbuf("v_words1", [P, S], U32)
+        gather(v_words[1][:], table_words[1][:].bitcast(U32), token_list, 0, S)
+        quantize_sides(1, [(n, round_side(1, n, nc.scalar.copy)) for n in range(2)], None)
+        for c in range(CHUNKS):
+            project_gate(1, c)
+        for c in range(CHUNKS):
+            project_query(1, c)
+
+        left = round_side(LAST, 0, nc.scalar.copy)
+        right = round_side(LAST, 1, nc.vector.tensor_copy)
+        quantize_sides(LAST, [(1, right), (0, left)], None)
+        v_words[LAST] = sbuf("v_words2", [P, S], U32)
+        gates, h_rows = [], []
+        for c in range(CHUNKS):
+            gather(v_words[LAST][:, c * P : (c + 1) * P], table_words[LAST][:].bitcast(U32), token_list, c * P, P)
+            project_gate(LAST, c)
+            if c > 0:
+                project_query(LAST, c - 1)
+        project_query(LAST, CHUNKS - 1)
+        for c in range(CHUNKS):
+            gates.append(sbuf("gate%d" % c, [P, H], F32))
             nc.scalar.activation(
-                gate[:, c, :].rearrange("p (u j e) -> p u j e", u=2, e=2),
+                gates[c][:].rearrange("p (u j e) -> p u j e", u=2, e=2),
                 b_acc[c][:].rearrange("p (j u e) -> p u j e", u=2, e=2),
                 SIGMOID,
             )
-        for c in range(CHUNKS - 1):
+        for c in range(CHUNKS):
+            h_rows.append(sbuf("h_rows%d" % c, [P, 2, H // 2], BF16))
             nc.vector.tensor_tensor(
                 h_rows[c][:].rearrange("p u (n x) -> p n u x", n=2),
                 a_acc[c][:].rearrange("p (n u x) -> p n u x", u=2, n=2),
-                gate[:, c, :].rearrange("p (u n x) -> p n u x", u=2, n=2),
-                MULT,
-            )
-        for u in range(2):
-            nc.vector.tensor_tensor(
-                h_rows[-1][u][:].rearrange("p (n x) -> p n x", n=2),
-                a_acc[-1][:].rearrange("p (n u x) -> p u n x", u=2, n=2)[:, u],
-                gate[:, CHUNKS - 1, :].rearrange("p (u n x) -> p u n x", u=2, n=2)[:, u],
+                gates[c][:].rearrange("p (u n x) -> p n u x", u=2, n=2),
                 MULT,
             )
 
-        h_bf16 = [
-            keep.tile([P, HALF * PACK], BF16, name="h_bf16_%d" % n, tag="h_bf16_%d" % n, align_bytes=64)
-            for n in range(2)
-        ]
-
-        def turn_chunk(c):
+        h_bf16 = [sbuf("h_bf16_%d" % n, [P, HALF * PACK], BF16) for n in range(2)]
+        for c in range(CHUNKS):
             turned = psum.tile([P, 2, P], F32, tag="bank%d" % c, name="turned%d" % c)
             for u in range(2):
-                half = h_rows[c][u][:] if c == CHUNKS - 1 else h_rows[c][:, u, :]
-                nc.tensor.transpose(turned[:, u, :], half.bitcast(F32), ident[:])
+                nc.tensor.transpose(turned[:, u, :], h_rows[c][:, u, :].bitcast(F32), ident[:])
             words = h_bf16[c // 2][:].bitcast(F32)[:, (c % 2) * 2 * P : (c % 2 + 1) * 2 * P]
             nc.scalar.copy(words.rearrange("p (j u) -> p j u", u=2), turned[:].rearrange("p u j -> p j u"))
 
+        h_codes = sbuf("h_codes", [P, S], U32)
+
         def quantize_half(n):
             cols = slice(n * HALF, (n + 1) * HALF)
-            nc.vector.quantize_mx(out=h_codes[:, cols].bitcast(FP8X4), scales=h_plane[:, cols], in_=h_bf16[n][:])
+            nc.vector.quantize_mx(out=h_codes[:, cols].bitcast(FP8X4), scales=planes[:, cols], in_=h_bf16[n][:])
 
-        for c in range(CHUNKS):
-            turn_chunk(c)
-        gather_key_words(0, KEY_PIECE, "key_words0")
+        key_words = {}
+
+        def gather_keys(words, first, count):
+            gather(words, key_table[:].bitcast(U32), key_list, first, count)
+            for n in range(count // P):
+                key_words[first // P + n] = words[:, n * P : (n + 1) * P]
+
         quantize_half(0)
+        first_keys = sbuf("first_keys", [P, KEY_PIECE], U32)
+        gather_keys(first_keys[:], 0, KEY_PIECE)
         quantize_half(1)
-        gather_key_words(KEY_PIECE, KEY_PIECE, "h_bf16_0")
-        gather_key_words(2 * KEY_PIECE, KEY_PIECE, "h_bf16_1")
+        other_keys = sbuf("other_keys", [P, S2 - KEY_PIECE], U32, "h_bf16_1")
+        gather_keys(other_keys[:, :KEY_PIECE], KEY_PIECE, KEY_PIECE)
+        for first in range(2 * KEY_PIECE, S2, 2 * KEY_PIECE):
+            gather_keys(other_keys[:, first - KEY_PIECE : first + KEY_PIECE], first, 2 * KEY_PIECE)
 
         def logits(i, queries, bank):
             z = psum.tile([P, queries.stop - queries.start], F32, tag="bank%d" % bank, name="z")
+            column = HALF + (i * P + S2 - KEY_TURN) % S2
             nc.tensor.matmul_mx(
                 out=z[:],
                 lhsT=key_words[i].bitcast(FP8X4),
-                lhsT_scale=key_plane[KEY_PLANE_ROW:P, i * P : (i + 1) * P],
+                lhsT_scale=planes[KEY_PLANE_ROW:P, column : column + P],
                 rhs=h_codes[:, queries].bitcast(FP8X4),
-                rhs_scale=h_plane[:, queries],
+                rhs_scale=planes[:, queries],
                 start=True,
                 stop=True,
             )
             return z
 
         def cap_and_store(i, sig, queries):
-            capped = keep.tile([P, queries.stop - queries.start], F32, name="capped%d_%d" % (i, queries.start))
-            if i == 0:
+            capped = sbuf("capped%d_%d" % (i, queries.start), [P, queries.stop - queries.start], F32)
+            if i < 3:
                 nc.gpsimd.tensor_scalar(capped[:], sig[:, queries], 2.0 * CAP, -CAP, MULT, ADD)
             else:
                 nc.vector.tensor_scalar(capped[:], sig[:, queries], 2.0 * CAP, shift[:], MULT, ADD)
@@ -287,7 +270,7 @@ def tile_list_paged_softcap_logits_kernel(
 
         bank = CHUNKS
         for i in range(KEY_TILES):
-            sig = keep.tile([P, S], F32, name="sig%d" % i, tag="sig%d" % i, align_bytes=64)
+            sig = sbuf("sig%d" % i, [P, S], F32)
             width = HALF if i < 2 else S
             for first in range(0, S, width):
                 queries = slice(first, first + width)

@@ -23,7 +23,7 @@ P = 128
 PACK = 4
 QUADRANT = 32
 SCALE_ROWS = 4
-SPREAD = 4
+SPREAD = 8
 LIST_ROWS = 16
 PASSES = K // (P * PACK)
 LAST = PASSES - 1
@@ -32,9 +32,7 @@ HALF = S // 2
 SIDE = H // 2
 KEY_TILES = S2 // P
 KEY_PIECE = 2 * P
-TABLE_SPREAD_ROW = 32
-LAST_SPREAD_ROW = 33
-KEY_SPREAD_ROW = 34
+SPREAD_ROW = 4
 KEY_PLANE_ROW = 8
 KEY_TURN = 1024
 
@@ -93,15 +91,14 @@ def tile_list_paged_softcap_logits_kernel(
             for r in rows:
                 nc.sync.dma_start(out=dst[r:P:QUADRANT], in_=by_row[r].bitcast(I32))
 
-        def spread_scale_rows(window, scales, first, step):
-            rows = scales.rearrange("a q t -> (a q) t").bitcast(I32)
-            nc.sync.dma_start(out=window[first : first + rows.shape[0] * step : step, :].bitcast(I32), in_=rows)
+        def spread_scale_rows(window, rows, first):
+            nc.sync.dma_start(out=window[first:P:SPREAD, :].bitcast(I32), in_=rows.bitcast(I32))
 
-        def place_scale_rows(plane, first_row, picked, first, step):
+        def place_scale_rows(plane, first_row, picked, first):
             for r in range(SCALE_ROWS):
                 nc.sync.dma_start(
                     out=plane[first_row + r : P : QUADRANT, :].bitcast(I32),
-                    in_=picked[first + step * r : first + 16 * step : SCALE_ROWS * step, :].bitcast(I32),
+                    in_=picked[first + SPREAD * r : P : QUADRANT, :].bitcast(I32),
                 )
 
         def gather(dst, window, entries, first, count):
@@ -149,10 +146,10 @@ def tile_list_paged_softcap_logits_kernel(
 
         load_words(table_words[0], tab_words[0])
         nc.sync.dma_start(token_list[:], offs)
-        spread_scale_rows(v_window, tab_scales[:LAST], TABLE_SPREAD_ROW, 2)
-        spread_scale_rows(v_window, tab_scales[LAST:], LAST_SPREAD_ROW, SPREAD)
+        for a in range(PASSES):
+            spread_scale_rows(v_window, tab_scales[a], SPREAD_ROW + a)
         nc.sync.dma_start(key_list[:], offs2)
-        spread_scale_rows(key_window, tab2_scales, KEY_SPREAD_ROW, SPREAD)
+        spread_scale_rows(key_window, tab2_scales[0], SPREAD_ROW)
         load_wq(0)
         load_gate_words(wg_codes[0], wg_words[:LAST])
         load_gate_plane(range(SCALE_ROWS))
@@ -160,13 +157,13 @@ def tile_list_paged_softcap_logits_kernel(
         v_words[0] = sbuf("v_words0", [P, S], U32)
         gather(v_words[0][:], table_words[0][:].bitcast(U32), token_list, 0, S)
         gather(v_picked[:], v_window[:], token_list, 0, S)
-        place_scale_rows(v_plane[:, :S], 0, v_picked, TABLE_SPREAD_ROW, 2)
+        place_scale_rows(v_plane[:, :S], 0, v_picked, SPREAD_ROW)
         load_words(table_words[1], tab_words[1])
-        place_scale_rows(v_plane[:, S : 2 * S], 0, v_picked, TABLE_SPREAD_ROW + 32, 2)
+        place_scale_rows(v_plane[:, S : 2 * S], 0, v_picked, SPREAD_ROW + 1)
         load_wq(LAST)
         load_words(table_words[LAST], tab_words[LAST])
         load_gate_words(wg_codes[1], wg_words[LAST:])
-        place_scale_rows(v_plane[:, LAST * S :], 0, v_picked, LAST_SPREAD_ROW, SPREAD)
+        place_scale_rows(v_plane[:, LAST * S :], 0, v_picked, SPREAD_ROW + LAST)
         load_words(key_table, tab2_words[0])
 
         quantize_sides(0, [(n, round_side(0, n, nc.scalar.copy)) for n in range(2)], None)
@@ -178,7 +175,7 @@ def tile_list_paged_softcap_logits_kernel(
         key_picked = sbuf("key_picked", [P, S2], U8)
         gather(key_picked[:, S2 - KEY_TURN :], key_window[:], key_list, 0, KEY_TURN)
         gather(key_picked[:, : S2 - KEY_TURN], key_window[:], key_list, KEY_TURN, S2 - KEY_TURN)
-        place_scale_rows(planes[:, HALF:], KEY_PLANE_ROW, key_picked, KEY_SPREAD_ROW, SPREAD)
+        place_scale_rows(planes[:, HALF:], KEY_PLANE_ROW, key_picked, SPREAD_ROW)
 
         v_words[1] = sbuf("v_words1", [P, S], U32)
         gather(v_words[1][:], table_words[1][:].bitcast(U32), token_list, 0, S)
@@ -240,10 +237,9 @@ def tile_list_paged_softcap_logits_kernel(
         first_keys = sbuf("first_keys", [P, KEY_PIECE], U32)
         gather_keys(first_keys[:], 0, KEY_PIECE)
         quantize_half(1)
-        other_keys = sbuf("other_keys", [P, S2 - KEY_PIECE], U32, "h_bf16_1")
+        other_keys = sbuf("other_keys", [P, 3 * KEY_PIECE], U32, "h_bf16_1")
         gather_keys(other_keys[:, :KEY_PIECE], KEY_PIECE, KEY_PIECE)
-        for first in range(2 * KEY_PIECE, S2, 2 * KEY_PIECE):
-            gather_keys(other_keys[:, first - KEY_PIECE : first + KEY_PIECE], first, 2 * KEY_PIECE)
+        gather_keys(other_keys[:, KEY_PIECE:], 2 * KEY_PIECE, 2 * KEY_PIECE)
 
         def logits(i, queries, bank):
             z = psum.tile([P, queries.stop - queries.start], F32, tag="bank%d" % bank, name="z")
@@ -261,7 +257,7 @@ def tile_list_paged_softcap_logits_kernel(
 
         def cap_and_store(i, sig, queries):
             capped = sbuf("capped%d_%d" % (i, queries.start), [P, queries.stop - queries.start], F32)
-            if i < 3:
+            if i in (0, 3, 5):
                 nc.gpsimd.tensor_scalar(capped[:], sig[:, queries], 2.0 * CAP, -CAP, MULT, ADD)
             else:
                 nc.vector.tensor_scalar(capped[:], sig[:, queries], 2.0 * CAP, shift[:], MULT, ADD)
@@ -280,3 +276,6 @@ def tile_list_paged_softcap_logits_kernel(
                     cap_and_store(i, sig, queries)
             if i > 0:
                 cap_and_store(i, sig, slice(0, S))
+            if i in (2, 4):
+                late_keys = sbuf("late_keys%d" % i, [P, KEY_PIECE], U32, "sig%d" % i)
+                gather_keys(late_keys[:], (i // 2 + 3) * KEY_PIECE, KEY_PIECE)

@@ -23,7 +23,7 @@ P = 128
 PACK = 4
 QUADRANT = 32
 SCALE_ROWS = 4
-SPREAD = 8
+SPREAD = 4
 LIST_ROWS = 16
 PASSES = K // (P * PACK)
 LAST = PASSES - 1
@@ -32,7 +32,9 @@ HALF = S // 2
 SIDE = H // 2
 KEY_TILES = S2 // P
 KEY_PIECE = 2 * P
-SPREAD_ROW = 4
+TABLE_SPREAD_ROW = 32
+LAST_SPREAD_ROW = 33
+KEY_SPREAD_ROW = 34
 KEY_PLANE_ROW = 8
 KEY_TURN = 1024
 
@@ -60,20 +62,18 @@ def tile_list_paged_softcap_logits_kernel(
         table_words = [sbuf("table_words%d" % a, [P, T], I32) for a in range(PASSES)]
         wq_raw = [sbuf("wq_raw%d" % a, [P, PACK, H], F32) for a in range(PASSES)]
         key_table = sbuf("key_table", [P, T2], I32)
-        ident = sbuf("ident", [P, P], F32)
         zero = sbuf("zero", [P, 1], F32)
         centre = sbuf("centre", [P, 1], F32)
         shift = sbuf("shift", [P, 1], F32)
 
         nc.vector.memset(v_window[:].bitcast(I32), 0)
         nc.vector.memset(zero[:], 0.0)
+        nc.vector.memset(wg_plane[:].bitcast(I32), 0)
         nc.vector.memset(key_window[:].bitcast(I32), 0)
-        nc.gpsimd.memset(wg_plane[:].bitcast(I32), 0)
-        nc.gpsimd.memset(v_plane[:].bitcast(I32), 0)
-        nc.gpsimd.memset(planes[:].bitcast(I32), 0)
+        nc.vector.memset(v_plane[:].bitcast(I32), 0)
+        nc.vector.memset(planes[:].bitcast(I32), 0)
         nc.scalar.activation(centre[:], zero[:], SIGMOID)
         nc.gpsimd.tensor_scalar(shift[:], centre[:], -2.0 * CAP, 0.0, MULT, ADD)
-        make_identity(nc, ident[:])
 
         def load_words(tile, words):
             nc.sync.dma_start(out=tile[:], in_=words.rearrange("p t i -> p (t i)").bitcast(I32))
@@ -91,14 +91,15 @@ def tile_list_paged_softcap_logits_kernel(
             for r in rows:
                 nc.sync.dma_start(out=dst[r:P:QUADRANT], in_=by_row[r].bitcast(I32))
 
-        def spread_scale_rows(window, rows, first):
-            nc.sync.dma_start(out=window[first:P:SPREAD, :].bitcast(I32), in_=rows.bitcast(I32))
+        def spread_scale_rows(window, scales, first, step):
+            rows = scales.rearrange("a q t -> (a q) t").bitcast(I32)
+            nc.sync.dma_start(out=window[first : first + rows.shape[0] * step : step, :].bitcast(I32), in_=rows)
 
-        def place_scale_rows(plane, first_row, picked, first):
-            for r in range(SCALE_ROWS):
+        def place_scale_rows(plane, first_row, picked, first, step, rows=range(SCALE_ROWS)):
+            for r in rows:
                 nc.sync.dma_start(
                     out=plane[first_row + r : P : QUADRANT, :].bitcast(I32),
-                    in_=picked[first + SPREAD * r : P : QUADRANT, :].bitcast(I32),
+                    in_=picked[first + step * r : first + 16 * step : SCALE_ROWS * step, :].bitcast(I32),
                 )
 
         def gather(dst, window, entries, first, count):
@@ -146,36 +147,40 @@ def tile_list_paged_softcap_logits_kernel(
 
         load_words(table_words[0], tab_words[0])
         nc.sync.dma_start(token_list[:], offs)
-        for a in range(PASSES):
-            spread_scale_rows(v_window, tab_scales[a], SPREAD_ROW + a)
-        nc.sync.dma_start(key_list[:], offs2)
-        spread_scale_rows(key_window, tab2_scales[0], SPREAD_ROW)
+        spread_scale_rows(v_window, tab_scales[:LAST], TABLE_SPREAD_ROW, 2)
+        spread_scale_rows(v_window, tab_scales[LAST:], LAST_SPREAD_ROW, SPREAD)
         load_wq(0)
-        load_gate_words(wg_codes[0], wg_words[:LAST])
-        load_gate_plane(range(SCALE_ROWS))
+        nc.sync.dma_start(key_list[:], offs2)
+        spread_scale_rows(key_window, tab2_scales, KEY_SPREAD_ROW, SPREAD)
+        load_gate_plane(range(3))
         load_wq(1)
+        load_gate_plane(range(3, SCALE_ROWS))
+        load_gate_words(wg_codes[0], wg_words[:LAST])
         v_words[0] = sbuf("v_words0", [P, S], U32)
         gather(v_words[0][:], table_words[0][:].bitcast(U32), token_list, 0, S)
         gather(v_picked[:], v_window[:], token_list, 0, S)
-        place_scale_rows(v_plane[:, :S], 0, v_picked, SPREAD_ROW)
+        place_scale_rows(v_plane[:, :S], 0, v_picked, TABLE_SPREAD_ROW, 2)
         load_words(table_words[1], tab_words[1])
-        place_scale_rows(v_plane[:, S : 2 * S], 0, v_picked, SPREAD_ROW + 1)
+        place_scale_rows(v_plane[:, S : 2 * S], 0, v_picked, TABLE_SPREAD_ROW + 32, 2, range(2))
         load_wq(LAST)
+        place_scale_rows(v_plane[:, S : 2 * S], 0, v_picked, TABLE_SPREAD_ROW + 32, 2, range(2, SCALE_ROWS))
         load_words(table_words[LAST], tab_words[LAST])
         load_gate_words(wg_codes[1], wg_words[LAST:])
-        place_scale_rows(v_plane[:, LAST * S :], 0, v_picked, SPREAD_ROW + LAST)
+        place_scale_rows(v_plane[:, LAST * S :], 0, v_picked, LAST_SPREAD_ROW, SPREAD)
         load_words(key_table, tab2_words[0])
-
-        quantize_sides(0, [(n, round_side(0, n, nc.scalar.copy)) for n in range(2)], None)
-        for c in range(CHUNKS):
-            project_gate(0, c)
-        for c in range(CHUNKS):
-            project_query(0, c)
+        ident = sbuf("ident", [P, P], F32, "v_window")
+        make_identity(nc, ident[:])
 
         key_picked = sbuf("key_picked", [P, S2], U8)
         gather(key_picked[:, S2 - KEY_TURN :], key_window[:], key_list, 0, KEY_TURN)
         gather(key_picked[:, : S2 - KEY_TURN], key_window[:], key_list, KEY_TURN, S2 - KEY_TURN)
-        place_scale_rows(planes[:, HALF:], KEY_PLANE_ROW, key_picked, SPREAD_ROW)
+        place_scale_rows(planes[:, HALF:], KEY_PLANE_ROW, key_picked, KEY_SPREAD_ROW, SPREAD)
+
+        quantize_sides(0, [(n, round_side(0, n, nc.scalar.copy)) for n in range(2)], "key_window")
+        for c in range(CHUNKS):
+            project_gate(0, c)
+        for c in range(CHUNKS):
+            project_query(0, c)
 
         v_words[1] = sbuf("v_words1", [P, S], U32)
         gather(v_words[1][:], table_words[1][:].bitcast(U32), token_list, 0, S)

@@ -260,27 +260,45 @@ def tile_list_paged_softcap_logits_kernel(
             )
             return z
 
-        def cap_and_store(i, sig, queries):
-            capped = sbuf("capped%d_%d" % (i, queries.start), [P, queries.stop - queries.start], F32)
-            if i in (0, 3, 5):
-                nc.gpsimd.tensor_scalar(capped[:], sig[:, queries], 2.0 * CAP, -CAP, MULT, ADD)
-            else:
-                nc.vector.tensor_scalar(capped[:], sig[:, queries], 2.0 * CAP, shift[:], MULT, ADD)
-            queue = nc.scalar if i >= 5 and i % 2 == 1 else nc.sync
-            queue.dma_start(out=out[i * P : (i + 1) * P, queries], in_=capped[:])
+        def squash(i, queries, bank):
+            sig = sbuf("sig%d_%d" % (i, queries.start), [P, queries.stop - queries.start], F32)
+            nc.scalar.activation(sig[:], logits(i, queries, bank)[:], SIGMOID, scale=2.0 / CAP)
+            return sig
 
-        bank = CHUNKS
-        for i in range(KEY_TILES):
-            sig = sbuf("sig%d" % i, [P, S], F32)
-            width = HALF if i < 2 else S
-            for first in range(0, S, width):
-                queries = slice(first, first + width)
-                nc.scalar.activation(sig[:, queries], logits(i, queries, bank)[:], SIGMOID, scale=2.0 / CAP)
-                bank = (bank + 1) % (2 * CHUNKS)
-                if i == 0:
-                    cap_and_store(i, sig, queries)
-            if i > 0:
-                cap_and_store(i, sig, slice(0, S))
-            if i in (2, 4):
-                late_keys = sbuf("late_keys%d" % i, [P, KEY_PIECE], U32, "sig%d" % i)
+        def cap_on_vector(capped, sig):
+            nc.vector.tensor_scalar(capped, sig[:], 2.0 * CAP, shift[:], MULT, ADD)
+
+        def cap_on_gpsimd(capped, sig):
+            nc.gpsimd.tensor_scalar(capped, sig[:], 2.0 * CAP, -CAP, MULT, ADD)
+
+        halves = [slice(0, HALF), slice(HALF, S)]
+        used = []
+
+        def next_bank():
+            used.append(None)
+            return (CHUNKS + len(used) - 1) % (2 * CHUNKS)
+
+        for queries in halves:
+            capped = sbuf("capped0_%d" % queries.start, [P, HALF], F32)
+            cap_on_gpsimd(capped[:], squash(0, queries, next_bank()))
+            nc.sync.dma_start(out=out[:P, queries], in_=capped[:])
+        for i in range(1, KEY_TILES - 1):
+            capped = sbuf("capped%d" % i, [P, S], F32)
+            if i in (3, 5):
+                cap_on_vector(capped[:, halves[0]], squash(i, halves[0], next_bank()))
+                late_keys = sbuf("late_keys%d" % i, [P, KEY_PIECE], U32, "sig%d_0" % i)
                 gather_keys(late_keys[:], (i // 2 + 3) * KEY_PIECE, KEY_PIECE)
+                cap_on_gpsimd(capped[:, halves[1]], squash(i, halves[1], next_bank()))
+            elif i == 1:
+                sig = sbuf("sig1", [P, S], F32)
+                for queries in halves:
+                    nc.scalar.activation(sig[:, queries], logits(i, queries, next_bank())[:], SIGMOID, scale=2.0 / CAP)
+                cap_on_vector(capped[:], sig)
+            else:
+                cap_on_vector(capped[:], squash(i, slice(0, S), next_bank()))
+            queue = nc.scalar if i >= 7 and i % 2 == 1 else nc.sync
+            queue.dma_start(out=out[i * P : (i + 1) * P, :], in_=capped[:])
+        for queries, queue in zip(halves, (nc.sync, nc.scalar)):
+            capped = sbuf("capped_last%d" % queries.start, [P, HALF], F32)
+            cap_on_vector(capped[:], squash(KEY_TILES - 1, queries, next_bank()))
+            queue.dma_start(out=out[S2 - P :, queries], in_=capped[:])

@@ -37,6 +37,7 @@ LAST_SPREAD_ROW = 33
 KEY_SPREAD_ROW = 34
 KEY_PLANE_ROW = 8
 KEY_TURN = 1024
+VECTOR_COLS = 160
 
 
 def tile_list_paged_softcap_logits_kernel(
@@ -106,10 +107,14 @@ def tile_list_paged_softcap_logits_kernel(
             offsets = entries[:, first // LIST_ROWS : (first + count) // LIST_ROWS]
             nc.vector.tensor_copy(dst, window.indirect(offsets))
 
-        def round_side(a, n, engine_copy):
+        def round_side(a, n, vector_cols):
             side = sbuf("wq_bf16_%d_%d" % (a, n), [P, SIDE, PACK], BF16)
             src = wq_raw[a][:, :, n * SIDE : (n + 1) * SIDE].rearrange("p t (j u e) -> p j t u e", u=2, e=2)
-            engine_copy(side[:].rearrange("p (u j e) t -> p j t u e", u=2, e=2), src)
+            dst = side[:].rearrange("p (u j e) t -> p j t u e", u=2, e=2)
+            groups = vector_cols // PACK
+            if groups > 0:
+                nc.vector.tensor_copy(dst[:, :groups], src[:, :groups])
+            nc.scalar.copy(dst[:, groups:], src[:, groups:])
             return side
 
         wq_codes, wq_plane, v_words = {}, {}, {}
@@ -176,7 +181,7 @@ def tile_list_paged_softcap_logits_kernel(
         gather(key_picked[:, : S2 - KEY_TURN], key_window[:], key_list, KEY_TURN, S2 - KEY_TURN)
         place_scale_rows(planes[:, HALF:], KEY_PLANE_ROW, key_picked, KEY_SPREAD_ROW, SPREAD)
 
-        quantize_sides(0, [(n, round_side(0, n, nc.scalar.copy)) for n in range(2)], "key_window")
+        quantize_sides(0, [(n, round_side(0, n, 0)) for n in range(2)], None)
         for c in range(CHUNKS):
             project_gate(0, c)
         for c in range(CHUNKS):
@@ -184,15 +189,13 @@ def tile_list_paged_softcap_logits_kernel(
 
         v_words[1] = sbuf("v_words1", [P, S], U32)
         gather(v_words[1][:], table_words[1][:].bitcast(U32), token_list, 0, S)
-        quantize_sides(1, [(n, round_side(1, n, nc.scalar.copy)) for n in range(2)], None)
+        quantize_sides(1, [(n, round_side(1, n, 0)) for n in range(2)], "table_words1")
         for c in range(CHUNKS):
             project_gate(1, c)
         for c in range(CHUNKS):
             project_query(1, c)
 
-        left = round_side(LAST, 0, nc.scalar.copy)
-        right = round_side(LAST, 1, nc.vector.tensor_copy)
-        quantize_sides(LAST, [(1, right), (0, left)], None)
+        quantize_sides(LAST, [(n, round_side(LAST, n, n * VECTOR_COLS)) for n in range(2)], None)
         v_words[LAST] = sbuf("v_words2", [P, S], U32)
         gates, h_rows = [], []
         for c in range(CHUNKS):

@@ -58,7 +58,7 @@ def tile_list_paged_softcap_logits_kernel(
         v_plane = sbuf("v_plane", [P, PASSES * S], U8)
         wg_plane = sbuf("wg_plane", [P, PASSES * H], U8)
         key_window = sbuf("key_window", [P, T2], U8)
-        planes = sbuf("planes", [P, HALF + S2], U8)
+        planes = sbuf("planes", [P, P + S2], U8)
         wg_codes = [sbuf("wg_early", [P, LAST, 2 * H], U8), sbuf("wg_last", [P, 1, 2 * H], U8)]
         table_words = [sbuf("table_words%d" % a, [P, T], I32) for a in range(PASSES)]
         wq_raw = [sbuf("wq_raw%d" % a, [P, PACK, H], F32) for a in range(PASSES)]
@@ -179,7 +179,7 @@ def tile_list_paged_softcap_logits_kernel(
         key_picked = sbuf("key_picked", [P, S2], U8)
         gather(key_picked[:, S2 - KEY_TURN :], key_window[:], key_list, 0, KEY_TURN)
         gather(key_picked[:, : S2 - KEY_TURN], key_window[:], key_list, KEY_TURN, S2 - KEY_TURN)
-        place_scale_rows(planes[:, HALF:], KEY_PLANE_ROW, key_picked, KEY_SPREAD_ROW, SPREAD)
+        place_scale_rows(planes[:, P:], KEY_PLANE_ROW, key_picked, KEY_SPREAD_ROW, SPREAD)
 
         quantize_sides(0, [(n, round_side(0, n, 0)) for n in range(2)], None)
         for c in range(CHUNKS):
@@ -204,34 +204,41 @@ def tile_list_paged_softcap_logits_kernel(
             if c > 0:
                 project_query(LAST, c - 1)
         project_query(LAST, CHUNKS - 1)
+        def parts(c):
+            return [slice(0, 1), slice(1, 2)] if c == CHUNKS - 1 else [slice(0, 2)]
+
         for c in range(CHUNKS):
             gates.append(sbuf("gate%d" % c, [P, H], F32))
-            nc.scalar.activation(
-                gates[c][:].rearrange("p (u j e) -> p u j e", u=2, e=2),
-                b_acc[c][:].rearrange("p (j u e) -> p u j e", u=2, e=2),
-                SIGMOID,
-            )
+            for u in parts(c):
+                nc.scalar.activation(
+                    gates[c][:].rearrange("p (u j e) -> p u j e", u=2, e=2)[:, u],
+                    b_acc[c][:].rearrange("p (j u e) -> p u j e", u=2, e=2)[:, u],
+                    SIGMOID,
+                )
         for c in range(CHUNKS):
             h_rows.append(sbuf("h_rows%d" % c, [P, 2, H // 2], BF16))
-            nc.vector.tensor_tensor(
-                h_rows[c][:].rearrange("p u (n x) -> p n u x", n=2),
-                a_acc[c][:].rearrange("p (n u x) -> p n u x", u=2, n=2),
-                gates[c][:].rearrange("p (u n x) -> p n u x", u=2, n=2),
-                MULT,
-            )
+            for u in parts(c):
+                nc.vector.tensor_tensor(
+                    h_rows[c][:].rearrange("p u (n x) -> p n u x", n=2)[:, :, u],
+                    a_acc[c][:].rearrange("p (n u x) -> p n u x", u=2, n=2)[:, :, u],
+                    gates[c][:].rearrange("p (u n x) -> p n u x", u=2, n=2)[:, :, u],
+                    MULT,
+                )
 
-        h_bf16 = [sbuf("h_bf16_%d" % n, [P, HALF * PACK], BF16) for n in range(2)]
+        pieces = [slice(0, P), slice(P, HALF), slice(HALF, S)]
+        h_bf16 = [sbuf("h_bf16_%d" % n, [P, (q.stop - q.start) * PACK], BF16) for n, q in enumerate(pieces)]
         for c in range(CHUNKS):
             turned = psum.tile([P, 2, P], F32, tag="bank%d" % c, name="turned%d" % c)
             for u in range(2):
                 nc.tensor.transpose(turned[:, u, :], h_rows[c][:, u, :].bitcast(F32), ident[:])
-            words = h_bf16[c // 2][:].bitcast(F32)[:, (c % 2) * 2 * P : (c % 2 + 1) * 2 * P]
+            first = max(c - 2, 0) * 2 * P
+            words = h_bf16[min(c, 2)][:].bitcast(F32)[:, first : first + 2 * P]
             nc.scalar.copy(words.rearrange("p (j u) -> p j u", u=2), turned[:].rearrange("p u j -> p j u"))
 
         h_codes = sbuf("h_codes", [P, S], U32)
 
-        def quantize_half(n):
-            cols = slice(n * HALF, (n + 1) * HALF)
+        def quantize_piece(n):
+            cols = pieces[n]
             nc.vector.quantize_mx(out=h_codes[:, cols].bitcast(FP8X4), scales=planes[:, cols], in_=h_bf16[n][:])
 
         key_words = {}
@@ -241,17 +248,18 @@ def tile_list_paged_softcap_logits_kernel(
             for n in range(count // P):
                 key_words[first // P + n] = words[:, n * P : (n + 1) * P]
 
-        quantize_half(0)
+        quantize_piece(0)
         first_keys = sbuf("first_keys", [P, KEY_PIECE], U32)
         gather_keys(first_keys[:], 0, KEY_PIECE)
-        quantize_half(1)
-        other_keys = sbuf("other_keys", [P, 3 * KEY_PIECE], U32, "h_bf16_1")
+        quantize_piece(1)
+        quantize_piece(2)
+        other_keys = sbuf("other_keys", [P, 2 * KEY_PIECE], U32, "h_bf16_2")
         gather_keys(other_keys[:, :KEY_PIECE], KEY_PIECE, KEY_PIECE)
-        gather_keys(other_keys[:, KEY_PIECE:], 2 * KEY_PIECE, 2 * KEY_PIECE)
+        gather_keys(other_keys[:, KEY_PIECE:], 2 * KEY_PIECE, KEY_PIECE)
 
         def logits(i, queries, bank):
             z = psum.tile([P, queries.stop - queries.start], F32, tag="bank%d" % bank, name="z")
-            column = HALF + (i * P + S2 - KEY_TURN) % S2
+            column = P + (i * P + S2 - KEY_TURN) % S2
             nc.tensor.matmul_mx(
                 out=z[:],
                 lhsT=key_words[i].bitcast(FP8X4),
@@ -281,22 +289,21 @@ def tile_list_paged_softcap_logits_kernel(
             used.append(None)
             return (CHUNKS + len(used) - 1) % (2 * CHUNKS)
 
-        for queries in halves:
+        for queries, cuts in zip(halves, (pieces[:2], pieces[2:])):
+            sig = sbuf("sig0_%d" % queries.start, [P, HALF], F32)
+            for cut in cuts:
+                part = sig[:, cut.start - queries.start : cut.stop - queries.start]
+                nc.scalar.activation(part, logits(0, cut, next_bank())[:], SIGMOID, scale=2.0 / CAP)
             capped = sbuf("capped0_%d" % queries.start, [P, HALF], F32)
-            cap_on_gpsimd(capped[:], squash(0, queries, next_bank()))
+            cap_on_gpsimd(capped[:], sig)
             nc.sync.dma_start(out=out[:P, queries], in_=capped[:])
         for i in range(1, KEY_TILES - 1):
             capped = sbuf("capped%d" % i, [P, S], F32)
-            if i in (3, 5):
+            if i in (1, 3, 5):
                 cap_on_vector(capped[:, halves[0]], squash(i, halves[0], next_bank()))
                 late_keys = sbuf("late_keys%d" % i, [P, KEY_PIECE], U32, "sig%d_0" % i)
                 gather_keys(late_keys[:], (i // 2 + 3) * KEY_PIECE, KEY_PIECE)
                 cap_on_gpsimd(capped[:, halves[1]], squash(i, halves[1], next_bank()))
-            elif i == 1:
-                sig = sbuf("sig1", [P, S], F32)
-                for queries in halves:
-                    nc.scalar.activation(sig[:, queries], logits(i, queries, next_bank())[:], SIGMOID, scale=2.0 / CAP)
-                cap_on_vector(capped[:], sig)
             else:
                 cap_on_vector(capped[:], squash(i, slice(0, S), next_bank()))
             queue = nc.scalar if i >= 7 and i % 2 == 1 else nc.sync

@@ -235,6 +235,18 @@ def tile_list_paged_softcap_logits_kernel(
             words = h_bf16[min(c, 2)][:].bitcast(F32)[:, first : first + 2 * P]
             nc.scalar.copy(words.rearrange("p (j u) -> p j u", u=2), turned[:].rearrange("p u j -> p j u"))
 
+        unread = psum.tile([P, H], F32, tag="bank%d" % (2 * CHUNKS - 1), name="unread")
+        for c in range(2):
+            nc.tensor.matmul_mx(
+                out=unread[:],
+                lhsT=v_words[LAST][:, c * P : (c + 1) * P].bitcast(FP8X4),
+                lhsT_scale=v_plane[:, LAST * S + c * P : LAST * S + (c + 1) * P],
+                rhs=wq_codes[LAST][:].bitcast(FP8X4),
+                rhs_scale=wq_plane[LAST][:],
+                start=True,
+                stop=True,
+            )
+
         h_codes = sbuf("h_codes", [P, S], U32)
 
         def quantize_piece(n):

@@ -38,6 +38,7 @@ KEY_SPREAD_ROW = 34
 KEY_PLANE_ROW = 8
 KEY_TURN = 1024
 VECTOR_COLS = 160
+GATHER_BEHIND = (1, 3, 5)
 
 
 def tile_list_paged_softcap_logits_kernel(
@@ -75,6 +76,11 @@ def tile_list_paged_softcap_logits_kernel(
         nc.vector.memset(planes[:].bitcast(I32), 0)
         nc.scalar.activation(centre[:], zero[:], SIGMOID)
         nc.gpsimd.tensor_scalar(shift[:], centre[:], -2.0 * CAP, 0.0, MULT, ADD)
+
+        shifts = {}
+        for i in GATHER_BEHIND:
+            shifts[i] = sbuf("shift%d" % i, [P, 1], F32)
+            nc.gpsimd.memset(shifts[i][:], -CAP)
 
         def load_words(tile, words):
             nc.sync.dma_start(out=tile[:], in_=words.rearrange("p t i -> p (t i)").bitcast(I32))
@@ -265,9 +271,12 @@ def tile_list_paged_softcap_logits_kernel(
         gather_keys(first_keys[:], 0, KEY_PIECE)
         quantize_piece(1)
         quantize_piece(2)
-        other_keys = sbuf("other_keys", [P, 2 * KEY_PIECE], U32, "h_bf16_2")
-        gather_keys(other_keys[:, :KEY_PIECE], KEY_PIECE, KEY_PIECE)
-        gather_keys(other_keys[:, KEY_PIECE:], 2 * KEY_PIECE, KEY_PIECE)
+
+        def more_keys(n, on):
+            gather_keys(sbuf("keys%d" % n, [P, KEY_PIECE], U32, on)[:], n * KEY_PIECE, KEY_PIECE)
+
+        more_keys(1, "h_bf16_1")
+        more_keys(2, "h_bf16_2")
 
         def logits(i, queries, bank):
             z = psum.tile([P, queries.stop - queries.start], F32, tag="bank%d" % bank, name="z")
@@ -288,13 +297,14 @@ def tile_list_paged_softcap_logits_kernel(
             nc.scalar.activation(sig[:], logits(i, queries, bank)[:], SIGMOID, scale=2.0 / CAP)
             return sig
 
-        def cap_on_vector(capped, sig):
-            nc.vector.tensor_scalar(capped, sig[:], 2.0 * CAP, shift[:], MULT, ADD)
+        def cap_on_vector(capped, sig, cols=slice(None), constant=shift):
+            nc.vector.tensor_scalar(capped, sig[:, cols], 2.0 * CAP, constant[:], MULT, ADD)
 
         def cap_on_gpsimd(capped, sig):
             nc.gpsimd.tensor_scalar(capped, sig[:], 2.0 * CAP, -CAP, MULT, ADD)
 
         halves = [slice(0, HALF), slice(HALF, S)]
+
         used = []
 
         def next_bank():
@@ -311,11 +321,14 @@ def tile_list_paged_softcap_logits_kernel(
             nc.sync.dma_start(out=out[:P, queries], in_=capped[:])
         for i in range(1, KEY_TILES - 1):
             capped = sbuf("capped%d" % i, [P, S], F32)
-            if i in (1, 3, 5):
-                cap_on_vector(capped[:, halves[0]], squash(i, halves[0], next_bank()))
-                late_keys = sbuf("late_keys%d" % i, [P, KEY_PIECE], U32, "sig%d_0" % i)
-                gather_keys(late_keys[:], (i // 2 + 3) * KEY_PIECE, KEY_PIECE)
-                cap_on_gpsimd(capped[:, halves[1]], squash(i, halves[1], next_bank()))
+            if i - 1 in GATHER_BEHIND:
+                cap_on_gpsimd(capped[:, halves[0]], squash(i, halves[0], next_bank()))
+                cap_on_vector(capped[:, halves[1]], squash(i, halves[1], next_bank()))
+            elif i in GATHER_BEHIND:
+                sig = squash(i, slice(0, S), next_bank())
+                cap_on_vector(capped[:, halves[0]], sig, halves[0], shifts[i])
+                cap_on_vector(capped[:, halves[1]], sig, halves[1])
+                more_keys(i // 2 + 3, "shift%d" % i)
             else:
                 cap_on_vector(capped[:], squash(i, slice(0, S), next_bank()))
             queue = nc.scalar if i >= 7 and i % 2 == 1 else nc.sync

from contextlib import ExitStack

import concourse.mybir as mybir
from concourse.masks import make_identity

K, H, T, S, T2, S2 = 1536, 512, 2048, 512, 4096, 1536
CAP = 2.0
FLOPS = 2 * 2 * K * H * S + 2 * H * S2 * S

F32 = mybir.dt.float32
BF16 = mybir.dt.bfloat16
I32 = mybir.dt.int32
U32 = mybir.dt.uint32
U16 = mybir.dt.uint16
U8 = mybir.dt.uint8
FP8X4 = mybir.dt.float8_e4m3fn_x4
FP4X4 = mybir.dt.float4_e2m1fn_x4
SIGMOID = mybir.ActivationFunctionType.Sigmoid
MULT = mybir.AluOpType.mult
ADD = mybir.AluOpType.add

P = 128
PACK = 4
QUADRANT = 32
SCALE_ROWS = 4
SPREAD = 4
LIST_ROWS = 16
PASSES = K // (P * PACK)
LAST = PASSES - 1
CHUNKS = S // P
HALF = S // 2
SIDE = H // 2
KEY_TILES = S2 // P
KEY_PIECE = 2 * P
TABLE_SPREAD_ROW = 32
LAST_SPREAD_ROW = 33
KEY_SPREAD_ROW = 34
KEY_PLANE_ROW = 8
KEY_TURN = 1024
VECTOR_COLS = 160
GATHER_BEHIND = (1, 3, 5)


def tile_list_paged_softcap_logits_kernel(
    tc, tab_words, tab_scales, offs, tab2_words, tab2_scales, offs2, wq, wg_words, wg_scales, out
):
    nc = tc.nc
    with ExitStack() as ctx:
        keep = ctx.enter_context(tc.tile_pool(name="keep", bufs=1))
        psum = ctx.enter_context(tc.psum_pool(name="psum", bufs=1))

        def sbuf(name, shape, dtype, on=None):
            return keep.tile(shape, dtype, name=name, tag=on or name, align_bytes=64)

        token_list = keep.tile([P, S // LIST_ROWS], U16, name="token_list")
        key_list = keep.tile([P, S2 // LIST_ROWS], U16, name="key_list")
        v_window = sbuf("v_window", [P, T], U8)
        v_picked = sbuf("v_picked", [P, S], U8)
        v_plane = sbuf("v_plane", [P, PASSES * S], U8)
        wg_plane = sbuf("wg_plane", [P, PASSES * H], U8)
        key_window = sbuf("key_window", [P, T2], U8)
        planes = sbuf("planes", [P, P + S2], U8)
        wg_codes = [sbuf("wg_early", [P, LAST, 2 * H], U8), sbuf("wg_last", [P, 1, 2 * H], U8)]
        table_words = [sbuf("table_words%d" % a, [P, T], I32) for a in range(PASSES)]
        wq_raw = [sbuf("wq_raw%d" % a, [P, PACK, H], F32) for a in range(PASSES)]
        key_table = sbuf("key_table", [P, T2], I32)
        zero = sbuf("zero", [P, 1], F32)
        centre = sbuf("centre", [P, 1], F32)
        shift = sbuf("shift", [P, 1], F32)

        nc.vector.memset(v_window[:].bitcast(I32), 0)
        nc.vector.memset(zero[:], 0.0)
        nc.vector.memset(wg_plane[:].bitcast(I32), 0)
        nc.vector.memset(key_window[:].bitcast(I32), 0)
        nc.vector.memset(v_plane[:].bitcast(I32), 0)
        nc.vector.memset(planes[:].bitcast(I32), 0)
        nc.scalar.activation(centre[:], zero[:], SIGMOID)
        nc.gpsimd.tensor_scalar(shift[:], centre[:], -2.0 * CAP, 0.0, MULT, ADD)

        shifts = {}
        for i in GATHER_BEHIND:
            shifts[i] = sbuf("shift%d" % i, [P, 1], F32)
            nc.gpsimd.memset(shifts[i][:], -CAP)

        def load_words(tile, words):
            nc.sync.dma_start(out=tile[:], in_=words.rearrange("p t i -> p (t i)").bitcast(I32))

        def load_wq(a):
            rows = wq[a * P * PACK : (a + 1) * P * PACK, :]
            nc.sync.dma_start(out=wq_raw[a][:], in_=rows.rearrange("(p j) c -> p j c", j=PACK))

        def load_gate_words(tile, words):
            nc.sync.dma_start(out=tile[:].bitcast(I32), in_=words.rearrange("a p c -> p a c").bitcast(I32))

        def load_gate_plane(rows):
            by_row = wg_scales.rearrange("a (q r) t -> r q a t", r=SCALE_ROWS)
            dst = wg_plane[:].bitcast(I32).rearrange("p (a t) -> p a t", a=PASSES)
            for r in rows:
                nc.sync.dma_start(out=dst[r:P:QUADRANT], in_=by_row[r].bitcast(I32))

        def spread_scale_rows(window, scales, first, step):
            rows = scales.rearrange("a q t -> (a q) t").bitcast(I32)
            nc.sync.dma_start(out=window[first : first + rows.shape[0] * step : step, :].bitcast(I32), in_=rows)

        def place_scale_rows(plane, first_row, picked, first, step, rows=range(SCALE_ROWS)):
            for r in rows:
                nc.sync.dma_start(
                    out=plane[first_row + r : P : QUADRANT, :].bitcast(I32),
                    in_=picked[first + step * r : first + 16 * step : SCALE_ROWS * step, :].bitcast(I32),
                )

        def gather(dst, window, entries, first, count):
            offsets = entries[:, first // LIST_ROWS : (first + count) // LIST_ROWS]
            nc.vector.tensor_copy(dst, window.indirect(offsets))

        def round_side(a, n, vector_cols):
            side = sbuf("wq_bf16_%d_%d" % (a, n), [P, SIDE, PACK], BF16)
            src = wq_raw[a][:, :, n * SIDE : (n + 1) * SIDE].rearrange("p t (j u e) -> p j t u e", u=2, e=2)
            dst = side[:].rearrange("p (u j e) t -> p j t u e", u=2, e=2)
            groups = vector_cols // PACK
            if groups > 0:
                nc.vector.tensor_copy(dst[:, :groups], src[:, :groups])
            nc.scalar.copy(dst[:, groups:], src[:, groups:])
            return side

        wq_codes, wq_plane, v_words = {}, {}, {}

        def quantize_sides(a, sides, on):
            wq_codes[a] = sbuf("wq_codes%d" % a, [P, H], U32, on)
            wq_plane[a] = sbuf("wq_plane%d" % a, [P, H], U8)
            for n, side in sides:
                cols = slice(n * SIDE, (n + 1) * SIDE)
                nc.vector.quantize_mx(
                    out=wq_codes[a][:, cols].bitcast(FP8X4),
                    scales=wq_plane[a][:, cols],
                    in_=side[:].rearrange("p c t -> p (c t)"),
                )

        b_acc = [psum.tile([P, H], F32, tag="bank%d" % c, name="b_acc%d" % c) for c in range(CHUNKS)]
        a_acc = [psum.tile([P, H], F32, tag="bank%d" % (CHUNKS + c), name="a_acc%d" % c) for c in range(CHUNKS)]

        def project(acc, a, c, weight, weight_plane):
            nc.tensor.matmul_mx(
                out=acc[:],
                lhsT=v_words[a][:, c * P : (c + 1) * P].bitcast(FP8X4),
                lhsT_scale=v_plane[:, a * S + c * P : a * S + (c + 1) * P],
                rhs=weight,
                rhs_scale=weight_plane,
                start=a == 0,
                stop=a == LAST,
            )

        def project_gate(a, c):
            project(b_acc[c], a, c, wg_codes[a // LAST][:, a % LAST, :].bitcast(FP4X4), wg_plane[:, a * H : (a + 1) * H])

        def project_query(a, c):
            project(a_acc[c], a, c, wq_codes[a][:].bitcast(FP8X4), wq_plane[a][:])

        load_words(table_words[0], tab_words[0])
        nc.sync.dma_start(token_list[:], offs)
        spread_scale_rows(v_window, tab_scales[:LAST], TABLE_SPREAD_ROW, 2)
        spread_scale_rows(v_window, tab_scales[LAST:], LAST_SPREAD_ROW, SPREAD)
        load_wq(0)
        nc.sync.dma_start(key_list[:], offs2)
        spread_scale_rows(key_window, tab2_scales, KEY_SPREAD_ROW, SPREAD)
        load_gate_plane(range(3))
        load_wq(1)
        load_gate_plane(range(3, SCALE_ROWS))
        load_gate_words(wg_codes[0], wg_words[:LAST])
        v_words[0] = sbuf("v_words0", [P, S], U32)
        gather(v_words[0][:], table_words[0][:].bitcast(U32), token_list, 0, S)
        gather(v_picked[:], v_window[:], token_list, 0, S)
        place_scale_rows(v_plane[:, :S], 0, v_picked, TABLE_SPREAD_ROW, 2)
        load_words(table_words[1], tab_words[1])
        place_scale_rows(v_plane[:, S : 2 * S], 0, v_picked, TABLE_SPREAD_ROW + 32, 2, range(2))
        load_wq(LAST)
        place_scale_rows(v_plane[:, S : 2 * S], 0, v_picked, TABLE_SPREAD_ROW + 32, 2, range(2, SCALE_ROWS))
        load_words(table_words[LAST], tab_words[LAST])
        load_gate_words(wg_codes[1], wg_words[LAST:])
        place_scale_rows(v_plane[:, LAST * S :], 0, v_picked, LAST_SPREAD_ROW, SPREAD)
        load_words(key_table, tab2_words[0])
        ident = sbuf("ident", [P, P], F32, "v_window")
        make_identity(nc, ident[:])

        key_picked = sbuf("key_picked", [P, S2], U8)
        gather(key_picked[:, S2 - KEY_TURN :], key_window[:], key_list, 0, KEY_TURN)
        gather(key_picked[:, : S2 - KEY_TURN], key_window[:], key_list, KEY_TURN, S2 - KEY_TURN)
        place_scale_rows(planes[:, P:], KEY_PLANE_ROW, key_picked, KEY_SPREAD_ROW, SPREAD)

        quantize_sides(0, [(n, round_side(0, n, 0)) for n in range(2)], None)
        for c in range(CHUNKS):
            project_gate(0, c)
        for c in range(CHUNKS):
            project_query(0, c)

        v_words[1] = sbuf("v_words1", [P, S], U32)
        gather(v_words[1][:], table_words[1][:].bitcast(U32), token_list, 0, S)
        quantize_sides(1, [(n, round_side(1, n, 0)) for n in range(2)], "table_words1")
        for c in range(CHUNKS):
            project_gate(1, c)
        for c in range(CHUNKS):
            project_query(1, c)

        quantize_sides(LAST, [(n, round_side(LAST, n, n * VECTOR_COLS)) for n in range(2)], None)
        v_words[LAST] = sbuf("v_words2", [P, S], U32)
        gates, h_rows = [], []
        for c in range(CHUNKS):
            gather(v_words[LAST][:, c * P : (c + 1) * P], table_words[LAST][:].bitcast(U32), token_list, c * P, P)
            project_gate(LAST, c)
            if c > 0:
                project_query(LAST, c - 1)
        project_query(LAST, CHUNKS - 1)
        def parts(c):
            return [slice(0, 1), slice(1, 2)] if c == CHUNKS - 1 else [slice(0, 2)]

        for c in range(CHUNKS):
            gates.append(sbuf("gate%d" % c, [P, H], F32))
            for u in parts(c):
                nc.scalar.activation(
                    gates[c][:].rearrange("p (u j e) -> p u j e", u=2, e=2)[:, u],
                    b_acc[c][:].rearrange("p (j u e) -> p u j e", u=2, e=2)[:, u],
                    SIGMOID,
                )
        for c in range(CHUNKS):
            h_rows.append(sbuf("h_rows%d" % c, [P, 2, H // 2], BF16))
            for u in parts(c):
                nc.vector.tensor_tensor(
                    h_rows[c][:].rearrange("p u (n x) -> p n u x", n=2)[:, :, u],
                    a_acc[c][:].rearrange("p (n u x) -> p n u x", u=2, n=2)[:, :, u],
                    gates[c][:].rearrange("p (u n x) -> p n u x", u=2, n=2)[:, :, u],
                    MULT,
                )

        pieces = [slice(0, P), slice(P, HALF), slice(HALF, S)]
        h_bf16 = [sbuf("h_bf16_%d" % n, [P, (q.stop - q.start) * PACK], BF16) for n, q in enumerate(pieces)]
        for c in range(CHUNKS):
            turned = psum.tile([P, 2, P], F32, tag="bank%d" % c, name="turned%d" % c)
            for u in range(2):
                nc.tensor.transpose(turned[:, u, :], h_rows[c][:, u, :].bitcast(F32), ident[:])
            first = max(c - 2, 0) * 2 * P
            words = h_bf16[min(c, 2)][:].bitcast(F32)[:, first : first + 2 * P]
            nc.scalar.copy(words.rearrange("p (j u) -> p j u", u=2), turned[:].rearrange("p u j -> p j u"))

        unread = psum.tile([P, H], F32, tag="bank%d" % (2 * CHUNKS - 1), name="unread")
        for c in range(2):
            nc.tensor.matmul_mx(
                out=unread[:],
                lhsT=v_words[LAST][:, c * P : (c + 1) * P].bitcast(FP8X4),
                lhsT_scale=v_plane[:, LAST * S + c * P : LAST * S + (c + 1) * P],
                rhs=wq_codes[LAST][:].bitcast(FP8X4),
                rhs_scale=wq_plane[LAST][:],
                start=True,
                stop=True,
            )

        h_codes = sbuf("h_codes", [P, S], U32)

        def quantize_piece(n):
            cols = pieces[n]
            nc.vector.quantize_mx(out=h_codes[:, cols].bitcast(FP8X4), scales=planes[:, cols], in_=h_bf16[n][:])

        key_words = {}

        def gather_keys(words, first, count):
            gather(words, key_table[:].bitcast(U32), key_list, first, count)
            for n in range(count // P):
                key_words[first // P + n] = words[:, n * P : (n + 1) * P]

        quantize_piece(0)
        first_keys = sbuf("first_keys", [P, KEY_PIECE], U32)
        gather_keys(first_keys[:], 0, KEY_PIECE)
        quantize_piece(1)
        quantize_piece(2)

        def more_keys(n, on):
            gather_keys(sbuf("keys%d" % n, [P, KEY_PIECE], U32, on)[:], n * KEY_PIECE, KEY_PIECE)

        more_keys(1, "h_bf16_1")
        more_keys(2, "h_bf16_2")

        def logits(i, queries, bank):
            z = psum.tile([P, queries.stop - queries.start], F32, tag="bank%d" % bank, name="z")
            column = P + (i * P + S2 - KEY_TURN) % S2
            nc.tensor.matmul_mx(
                out=z[:],
                lhsT=key_words[i].bitcast(FP8X4),
                lhsT_scale=planes[KEY_PLANE_ROW:P, column : column + P],
                rhs=h_codes[:, queries].bitcast(FP8X4),
                rhs_scale=planes[:, queries],
                start=True,
                stop=True,
            )
            return z

        def squash(i, queries, bank):
            sig = sbuf("sig%d_%d" % (i, queries.start), [P, queries.stop - queries.start], F32)
            nc.scalar.activation(sig[:], logits(i, queries, bank)[:], SIGMOID, scale=2.0 / CAP)
            return sig

        def cap_on_vector(capped, sig, cols=slice(None), constant=shift):
            nc.vector.tensor_scalar(capped, sig[:, cols], 2.0 * CAP, constant[:], MULT, ADD)

        def cap_on_gpsimd(capped, sig):
            nc.gpsimd.tensor_scalar(capped, sig[:], 2.0 * CAP, -CAP, MULT, ADD)

        halves = [slice(0, HALF), slice(HALF, S)]

        used = []

        def next_bank():
            used.append(None)
            return (CHUNKS + len(used) - 1) % (2 * CHUNKS)

        for queries, cuts in zip(halves, (pieces[:2], pieces[2:])):
            sig = sbuf("sig0_%d" % queries.start, [P, HALF], F32)
            for cut in cuts:
                part = sig[:, cut.start - queries.start : cut.stop - queries.start]
                nc.scalar.activation(part, logits(0, cut, next_bank())[:], SIGMOID, scale=2.0 / CAP)
            capped = sbuf("capped0_%d" % queries.start, [P, HALF], F32)
            cap_on_gpsimd(capped[:], sig)
            nc.sync.dma_start(out=out[:P, queries], in_=capped[:])
        for i in range(1, KEY_TILES - 1):
            capped = sbuf("capped%d" % i, [P, S], F32)
            if i - 1 in GATHER_BEHIND:
                cap_on_gpsimd(capped[:, halves[0]], squash(i, halves[0], next_bank()))
                cap_on_vector(capped[:, halves[1]], squash(i, halves[1], next_bank()))
            elif i in GATHER_BEHIND:
                sig = squash(i, slice(0, S), next_bank())
                cap_on_vector(capped[:, halves[0]], sig, halves[0], shifts[i])
                cap_on_vector(capped[:, halves[1]], sig, halves[1])
                more_keys(i // 2 + 3, "shift%d" % i)
            else:
                cap_on_vector(capped[:], squash(i, slice(0, S), next_bank()))
            queue = nc.scalar if i >= 7 and i % 2 == 1 else nc.sync
            queue.dma_start(out=out[i * P : (i + 1) * P, :], in_=capped[:])
        for queries, queue in zip(halves, (nc.sync, nc.scalar)):
            capped = sbuf("capped_last%d" % queries.start, [P, HALF], F32)
            cap_on_vector(capped[:], squash(KEY_TILES - 1, queries, next_bank()))
            queue.dma_start(out=out[S2 - P :, queries], in_=capped[:])
